import numpy as np
import ml_dtypes


def mxq(x, axis, fmt="e4m3"):
    dtype, down = {"e4m3": (ml_dtypes.float8_e4m3fn, 7), "e5m2": (ml_dtypes.float8_e5m2, 14)}[fmt]
    v = np.moveaxis(np.asarray(x, np.float32).astype(ml_dtypes.bfloat16).astype(np.float64), axis, -1)
    blocks = v.reshape(v.shape[:-1] + (-1, 32))
    amax = np.abs(blocks).max(-1, keepdims=True)
    byte = np.maximum(np.where(amax > 0, np.frexp(amax)[1] - 1 + 127, 0) - down, 1)
    scale = np.exp2(byte - 127.0)
    codes = (blocks / scale).astype(np.float32).astype(dtype).astype(np.float64)
    return np.moveaxis((codes * scale).reshape(v.shape), -1, axis)


WIDE = False


def mx_kscale(k):
    if not WIDE:
        return np.ones(k)
    levels = np.array([10, -10, 5, -5, 0])
    if k % 512:
        return np.exp2(np.random.permutation(np.resize(levels, k // 32))).repeat(32)
    a = np.empty((k // 512, 16))
    for p in range(k // 512):
        a[p, :8] = np.random.permutation(np.resize(levels, 8))
        for g in range(8):
            far = levels[np.abs(levels - a[p, g]) >= 10]
            a[p, g + 8] = far[np.random.randint(len(far))]
    return np.exp2(a.ravel()).repeat(32)


def f64(x):
    return np.asarray(x).astype(np.float64)


def striped(idx):
    return np.tile(idx.reshape(-1, 16).T, (8, 1)).astype(np.uint16)


def unstriped(offs):
    return offs[:16].T.reshape(-1).astype(np.int64)


E2M1 = np.array([0.0, 0.5, 1.0, 1.5, 2.0, 3.0, 4.0, 6.0, -0.0, -0.5, -1.0, -1.5, -2.0, -3.0, -4.0, -6.0])


def pack_fp4(w):
    k, n = w.shape
    w = f64(np.asarray(w, np.float32).astype(ml_dtypes.bfloat16)).reshape(k // 32, 32, n)
    amax = np.abs(w).max(1)
    mant, ex = np.frexp(amax / 6.0)
    byte = np.clip(np.where(amax > 0, np.where(mant > 0.5, ex, ex - 1) + 127, 1), 1, 254)
    scaled = (w * np.exp2(127.0 - byte)[:, None, :]).reshape(k, n).astype(np.float32)
    c = np.ascontiguousarray(scaled.reshape(k // 512, 128, 4, n).transpose(0, 1, 3, 2)).astype(ml_dtypes.float4_e2m1fn).view(np.uint8) & 0xF
    words = (c[..., 0::2] | (c[..., 1::2] << 4)).reshape(k // 512, 128, 2 * n)
    return np.ascontiguousarray(words), np.ascontiguousarray(byte.astype(np.uint8).reshape(k // 512, 16, n))


def unpack_fp4(words, scales):
    g, _, n = scales.shape
    words = np.ascontiguousarray(words).reshape(g, 128, n, 2)
    nib = np.empty((g, 128, n, 4), np.uint8)
    nib[..., 0::2] = words & 0xF
    nib[..., 1::2] = words >> 4
    vals = E2M1[nib] * np.repeat(np.exp2(scales.astype(np.float64) - 127.0), 8, axis=1)[..., None]
    return vals.transpose(0, 1, 3, 2).reshape(g * 512, n)


K, T, S, N, U = 512, 2048, 1024, 128, 2048


def setup_inputs():
    n = np.random.standard_normal
    s = mx_kscale(K)[:, None]
    packed_w1 = pack_fp4(n((K, N)) / np.sqrt(K) / s)
    return {
        "xT": (n((K, T)) * s).astype(np.float32),
        "mem": n((N, U)).astype(np.float32),
        "w1_words": packed_w1[0],
        "w1_scales": packed_w1[1],
        "offs": striped(np.random.permutation(T)[:S]),
        "slot": striped(np.random.permutation(U)[:S]),
    }


def reference(xT, mem, w1_words, w1_scales, offs, slot):
    xq = mxq(f64(xT)[:, unstriped(offs)], 0, "e4m3")
    y = unpack_fp4(w1_words, w1_scales).T @ xq
    out = f64(mem).copy()
    out[:, unstriped(slot)] = f64(mem)[:, unstriped(slot)] + y
    return out

@@ -1,0 +1,94 @@
+from contextlib import ExitStack
+
+import concourse.mybir as mybir
+
+K, T, S, N, U = 512, 2048, 1024, 128, 2048
+FLOPS = 2 * K * N * S
+
+F32 = mybir.dt.float32
+BF16 = mybir.dt.bfloat16
+I32 = mybir.dt.int32
+U32 = mybir.dt.uint32
+U16 = mybir.dt.uint16
+U8 = mybir.dt.uint8
+FP8X4 = mybir.dt.float8_e4m3fn_x4
+FP4X4 = mybir.dt.float4_e2m1fn_x4
+ADD = mybir.AluOpType.add
+
+P = 128
+PACK = 4
+LANES = 16
+PIECE = 256
+LAST_CUTS = [0, 128, 256, 512, 768, 1024]
+PUT_CUTS = [0, 256, 1024]
+
+
+def tile_picked_idxput_add_e_kernel(tc, xT, mem, w1_words, w1_scales, offs, slot, out):
+    nc = tc.nc
+    with ExitStack() as ctx:
+        sb = ctx.enter_context(tc.tile_pool(name="sb", bufs=1))
+        ps = ctx.enter_context(tc.psum_pool(name="ps", bufs=1))
+
+        offs_sb = sb.tile([P, S // LANES], U16, name="offs_sb")
+        slot_sb = sb.tile([P, S // LANES], U16, name="slot_sb")
+        planes = [sb.tile([P, T], F32, name=f"plane{j}") for j in range(PACK)]
+        store = sb.tile([P, U], F32, name="store")
+        w_codes = sb.tile([P, 2 * N], U8, name="w_codes", align_bytes=64)
+        w_scales = sb.tile([P, N], U8, name="w_scales", align_bytes=64)
+
+        x_rows = xT.rearrange("(p j) t -> p j t", j=PACK)
+        nc.gpsimd.memset(w_scales[:], 0)
+        nc.sync.dma_start(planes[0][:], x_rows[:, 0, :])
+        nc.sync.dma_start(offs_sb[:], offs)
+        nc.sync.dma_start(planes[1][:], x_rows[:, 1, :])
+        nc.sync.dma_start(slot_sb[:], slot)
+        nc.sync.dma_start(planes[2][:], x_rows[:, 2, :])
+        nc.sync.dma_start(planes[3][:], x_rows[:, 3, :])
+        nc.sync.dma_start(store[:], mem)
+        nc.sync.dma_start(w_codes[:].bitcast(I32), w1_words[0].bitcast(I32))
+        for q in range(4):
+            nc.sync.dma_start(w_scales[32 * q : 32 * q + 4, :].bitcast(I32), w1_scales[0, 4 * q : 4 * q + 4, :].bitcast(I32))
+
+        picked = [
+            sb.tile([P, PACK, b - a], BF16, name=f"picked{i}", tag=f"picked{i}", align_bytes=64)
+            for i, (a, b) in enumerate(zip(PUT_CUTS[:-1], PUT_CUTS[1:]))
+        ]
+
+        def picked_cols(a, b):
+            i = 0 if b <= PUT_CUTS[1] else 1
+            return picked[i][:, :, a - PUT_CUTS[i] : b - PUT_CUTS[i]]
+
+        for j in range(PACK):
+            cuts = LAST_CUTS if j == PACK - 1 else PUT_CUTS
+            for a, b in zip(cuts[:-1], cuts[1:]):
+                nc.vector.tensor_copy(picked_cols(a, b)[:, j, :], planes[j][:].indirect(offs_sb[:, a // LANES : b // LANES]))
+        woven = [sb.tile([P, PIECE, PACK], BF16, name=f"woven{c}", align_bytes=64) for c in range(S // PIECE)]
+        for a, b in zip(LAST_CUTS[:-1], LAST_CUTS[1:]):
+            c = a // PIECE
+            nc.scalar.copy(woven[c][:, a - c * PIECE : b - c * PIECE, :], picked_cols(a, b).rearrange("p j n -> p n j"))
+
+        y = sb.tile([P, S], F32, name="y")
+        banks = []
+        for c in range(S // PIECE):
+            codes = sb.tile([P, PIECE], U32, name=f"codes{c}", align_bytes=64)
+            scales = sb.tile([P, PIECE], U8, name=f"scales{c}", align_bytes=64)
+            nc.vector.quantize_mx(out=codes[:].bitcast(FP8X4), scales=scales[:], in_=woven[c][:].rearrange("p n j -> p (n j)"))
+            bank = ps.tile([N, PIECE], F32, name=f"bank{c}")
+            nc.tensor.matmul_mx(
+                out=bank[:],
+                lhsT=w_codes[:].bitcast(FP4X4),
+                lhsT_scale=w_scales[:],
+                rhs=codes[:].bitcast(FP8X4),
+                rhs_scale=scales[:],
+                start=True,
+                stop=True,
+            )
+            banks.append(bank)
+            if c == 0:
+                old = sb.tile([P, S], F32, name="old", tag="picked0", align_bytes=64)
+                nc.vector.tensor_copy(old[:], store[:].indirect(slot_sb[:]))
+        for c in range(S // PIECE):
+            nc.scalar.copy(y[:, c * PIECE : (c + 1) * PIECE], banks[c][:])
+        for a, b in zip(PUT_CUTS[:-1], PUT_CUTS[1:]):
+            nc.vector.tensor_tensor(store[:].indirect(slot_sb[:, a // LANES : b // LANES]), old[:, a:b], y[:, a:b], ADD)
+        nc.sync.dma_start(out, store[:])

@@ -14,13 +14,16 @@ U8 = mybir.dt.uint8
 FP8X4 = mybir.dt.float8_e4m3fn_x4
 FP4X4 = mybir.dt.float4_e2m1fn_x4
 ADD = mybir.AluOpType.add
+COPY = mybir.ActivationFunctionType.Copy
 
 P = 128
 PACK = 4
 LANES = 16
 PIECE = 256
-LAST_CUTS = [0, 128, 256, 512, 768, 1024]
-PUT_CUTS = [0, 256, 1024]
+PIECES = S // PIECE
+LOADS_OF_PLANE = [1, 1, 1, 1]
+SHARED = ()
+SPLIT = 1024
 
 
 def tile_picked_idxput_add_e_kernel(tc, xT, mem, w1_words, w1_scales, offs, slot, out):
@@ -32,50 +35,46 @@ def tile_picked_idxput_add_e_kernel(tc, xT, mem, w1_words, w1_scales, offs, slot
         offs_sb = sb.tile([P, S // LANES], U16, name="offs_sb")
         slot_sb = sb.tile([P, S // LANES], U16, name="slot_sb")
         planes = [sb.tile([P, T], F32, name=f"plane{j}") for j in range(PACK)]
+        rounded = {j: sb.tile([P, T], BF16, name=f"rounded{j}") for j in SHARED}
         store = sb.tile([P, U], F32, name="store")
         w_codes = sb.tile([P, 2 * N], U8, name="w_codes", align_bytes=64)
         w_scales = sb.tile([P, N], U8, name="w_scales", align_bytes=64)
-
-        x_rows = xT.rearrange("(p j) t -> p j t", j=PACK)
-        nc.gpsimd.memset(w_scales[:], 0)
-        nc.sync.dma_start(planes[0][:], x_rows[:, 0, :])
-        nc.sync.dma_start(offs_sb[:], offs)
-        nc.sync.dma_start(planes[1][:], x_rows[:, 1, :])
-        nc.sync.dma_start(slot_sb[:], slot)
-        nc.sync.dma_start(planes[2][:], x_rows[:, 2, :])
-        nc.sync.dma_start(planes[3][:], x_rows[:, 3, :])
-        nc.sync.dma_start(store[:], mem)
-        nc.sync.dma_start(w_codes[:].bitcast(I32), w1_words[0].bitcast(I32))
-        for q in range(4):
-            nc.sync.dma_start(w_scales[32 * q : 32 * q + 4, :].bitcast(I32), w1_scales[0, 4 * q : 4 * q + 4, :].bitcast(I32))
-
-        picked = [
-            sb.tile([P, PACK, b - a], BF16, name=f"picked{i}", tag=f"picked{i}", align_bytes=64)
-            for i, (a, b) in enumerate(zip(PUT_CUTS[:-1], PUT_CUTS[1:]))
-        ]
-
-        def picked_cols(a, b):
-            i = 0 if b <= PUT_CUTS[1] else 1
-            return picked[i][:, :, a - PUT_CUTS[i] : b - PUT_CUTS[i]]
-
-        for j in range(PACK):
-            cuts = LAST_CUTS if j == PACK - 1 else PUT_CUTS
-            for a, b in zip(cuts[:-1], cuts[1:]):
-                nc.vector.tensor_copy(picked_cols(a, b)[:, j, :], planes[j][:].indirect(offs_sb[:, a // LANES : b // LANES]))
-        woven = [sb.tile([P, PIECE, PACK], BF16, name=f"woven{c}", align_bytes=64) for c in range(S // PIECE)]
-        for a, b in zip(LAST_CUTS[:-1], LAST_CUTS[1:]):
-            c = a // PIECE
-            nc.scalar.copy(woven[c][:, a - c * PIECE : b - c * PIECE, :], picked_cols(a, b).rearrange("p j n -> p n j"))
-
+        first = sb.tile([P, PACK, PIECE], BF16, name="first", tag="first", align_bytes=64)
+        rest = sb.tile([P, PACK, S - PIECE], BF16, name="rest", align_bytes=64)
+        woven = {c: sb.tile([P, PIECE, PACK], BF16, name=f"woven{c}", align_bytes=64) for c in (0, 1, 3)}
         y = sb.tile([P, S], F32, name="y")
-        banks = []
-        for c in range(S // PIECE):
-            codes = sb.tile([P, PIECE], U32, name=f"codes{c}", align_bytes=64)
+        banks = [ps.tile([N, PIECE], F32, name=f"bank{c}") for c in range(PIECES)]
+        x_rows = xT.rearrange("(p j) t -> p j t", j=PACK)
+
+        def entries(lst, a, b):
+            return lst[:, a // LANES : b // LANES]
+
+        def picked(a, b):
+            return first[:, :, a:b] if b <= PIECE else rest[:, :, a - PIECE : b - PIECE]
+
+        def load_plane(j):
+            width = T // LOADS_OF_PLANE[j]
+            for a in range(0, T, width):
+                nc.sync.dma_start(planes[j][:, a : a + width], x_rows[:, j, a : a + width])
+                if j in SHARED:
+                    nc.scalar.copy(rounded[j][:, a : a + width], planes[j][:, a : a + width])
+
+        def pick_on_vector(j, a, b):
+            nc.vector.tensor_copy(picked(a, b)[:, j, :], planes[j][:].indirect(entries(offs_sb, a, b)))
+
+        def pick_on_scalar(j, a, b):
+            nc.scalar.activation(picked(a, b)[:, j, :], rounded[j][:].indirect(entries(offs_sb, a, b)), COPY)
+
+        def weave(a, b):
+            c = a // PIECE
+            nc.scalar.copy(woven[c][:, a - c * PIECE : b - c * PIECE, :], picked(a, b).rearrange("p j n -> p n j"))
+
+        def project(c):
+            codes = sb.tile([P, PIECE], U32, name=f"codes{c}", tag=f"codes{c}", align_bytes=64)
             scales = sb.tile([P, PIECE], U8, name=f"scales{c}", align_bytes=64)
             nc.vector.quantize_mx(out=codes[:].bitcast(FP8X4), scales=scales[:], in_=woven[c][:].rearrange("p n j -> p (n j)"))
-            bank = ps.tile([N, PIECE], F32, name=f"bank{c}")
             nc.tensor.matmul_mx(
-                out=bank[:],
+                out=banks[c][:],
                 lhsT=w_codes[:].bitcast(FP4X4),
                 lhsT_scale=w_scales[:],
                 rhs=codes[:].bitcast(FP8X4),
@@ -83,12 +82,47 @@ def tile_picked_idxput_add_e_kernel(tc, xT, mem, w1_words, w1_scales, offs, slot
                 start=True,
                 stop=True,
             )
-            banks.append(bank)
-            if c == 0:
-                old = sb.tile([P, S], F32, name="old", tag="picked0", align_bytes=64)
-                nc.vector.tensor_copy(old[:], store[:].indirect(slot_sb[:]))
-        for c in range(S // PIECE):
+
+        def drain(c):
             nc.scalar.copy(y[:, c * PIECE : (c + 1) * PIECE], banks[c][:])
-        for a, b in zip(PUT_CUTS[:-1], PUT_CUTS[1:]):
-            nc.vector.tensor_tensor(store[:].indirect(slot_sb[:, a // LANES : b // LANES]), old[:, a:b], y[:, a:b], ADD)
+
+        def put(old, a, b):
+            nc.vector.tensor_tensor(store[:].indirect(entries(slot_sb, a, b)), old[:, a:b], y[:, a:b], ADD)
+
+        nc.vector.memset(w_scales[:].bitcast(I32), 0)
+        load_plane(0)
+        nc.sync.dma_start(offs_sb[:], offs)
+        last = S - PIECE
+        for j in range(PACK - 1):
+            if j == 1:
+                nc.sync.dma_start(slot_sb[:], slot)
+            pick_on_vector(j, 0, PIECE)
+            pick_on_vector(j, PIECE, last if j in SHARED else S)
+            if j in SHARED:
+                pick_on_scalar(j, last, S)
+            load_plane(j + 1)
+        nc.sync.dma_start(store[:], mem)
+        nc.sync.dma_start(w_codes[:].bitcast(I32), w1_words[0].bitcast(I32))
+        for q in range(4):
+            nc.sync.dma_start(w_scales[32 * q : 32 * q + 4, :].bitcast(I32), w1_scales[0, 4 * q : 4 * q + 4, :].bitcast(I32))
+
+        for a, b in ((0, 128), (128, 256), (256, 512), (512, SPLIT)):
+            pick_on_vector(PACK - 1, a, b)
+        weave(0, 128)
+        weave(128, 256)
+        project(0)
+        old = sb.tile([P, S], F32, name="old", tag="first", align_bytes=64)
+        nc.vector.tensor_copy(old[:], store[:].indirect(slot_sb[:]))
+        weave(256, 512)
+        project(1)
+        drain(0)
+        woven[2] = sb.tile([P, PIECE, PACK], BF16, name="woven2", tag="codes0", align_bytes=64)
+        weave(512, 768)
+        project(2)
+        weave(last, S)
+        project(3)
+        for c in range(1, PIECES):
+            drain(c)
+        for a, b in ((0, 256), (256, 512), (512, 1024)):
+            put(old, a, b)
         nc.sync.dma_start(out, store[:])

@@ -19,11 +19,9 @@ COPY = mybir.ActivationFunctionType.Copy
 P = 128
 PACK = 4
 LANES = 16
-PIECE = 256
-PIECES = S // PIECE
-LOADS_OF_PLANE = [1, 1, 1, 1]
-SHARED = ()
-SPLIT = 1024
+PIECES = [(0, 128), (128, 256), (256, 512), (512, 768), (768, 1024)]
+LAST_GATHERS = [(0, 128), (128, 256), (256, 512), (512, 1024)]
+SCATTERS = [(0, 256), (256, 1024)]
 
 
 def tile_picked_idxput_add_e_kernel(tc, xT, mem, w1_words, w1_scales, offs, slot, out):
@@ -35,46 +33,35 @@ def tile_picked_idxput_add_e_kernel(tc, xT, mem, w1_words, w1_scales, offs, slot
         offs_sb = sb.tile([P, S // LANES], U16, name="offs_sb")
         slot_sb = sb.tile([P, S // LANES], U16, name="slot_sb")
         planes = [sb.tile([P, T], F32, name=f"plane{j}") for j in range(PACK)]
-        rounded = {j: sb.tile([P, T], BF16, name=f"rounded{j}") for j in SHARED}
         store = sb.tile([P, U], F32, name="store")
         w_codes = sb.tile([P, 2 * N], U8, name="w_codes", align_bytes=64)
         w_scales = sb.tile([P, N], U8, name="w_scales", align_bytes=64)
-        first = sb.tile([P, PACK, PIECE], BF16, name="first", tag="first", align_bytes=64)
-        rest = sb.tile([P, PACK, S - PIECE], BF16, name="rest", align_bytes=64)
-        woven = {c: sb.tile([P, PIECE, PACK], BF16, name=f"woven{c}", align_bytes=64) for c in (0, 1, 3)}
+        picked = sb.tile([P, PACK, S], BF16, name="picked", align_bytes=64)
+        old = sb.tile([P, S], F32, name="old")
         y = sb.tile([P, S], F32, name="y")
-        banks = [ps.tile([N, PIECE], F32, name=f"bank{c}") for c in range(PIECES)]
         x_rows = xT.rearrange("(p j) t -> p j t", j=PACK)
 
         def entries(lst, a, b):
             return lst[:, a // LANES : b // LANES]
 
-        def picked(a, b):
-            return first[:, :, a:b] if b <= PIECE else rest[:, :, a - PIECE : b - PIECE]
-
-        def load_plane(j):
-            width = T // LOADS_OF_PLANE[j]
-            for a in range(0, T, width):
-                nc.sync.dma_start(planes[j][:, a : a + width], x_rows[:, j, a : a + width])
-                if j in SHARED:
-                    nc.scalar.copy(rounded[j][:, a : a + width], planes[j][:, a : a + width])
-
-        def pick_on_vector(j, a, b):
-            nc.vector.tensor_copy(picked(a, b)[:, j, :], planes[j][:].indirect(entries(offs_sb, a, b)))
-
-        def pick_on_scalar(j, a, b):
-            nc.scalar.activation(picked(a, b)[:, j, :], rounded[j][:].indirect(entries(offs_sb, a, b)), COPY)
+        def pick(j, a, b):
+            nc.vector.tensor_copy(picked[:, j, a:b], planes[j][:].indirect(entries(offs_sb, a, b)))
 
         def weave(a, b):
-            c = a // PIECE
-            nc.scalar.copy(woven[c][:, a - c * PIECE : b - c * PIECE, :], picked(a, b).rearrange("p j n -> p n j"))
+            woven = sb.tile([P, b - a, PACK], BF16, name=f"woven{a}", align_bytes=64)
+            nc.scalar.copy(
+                woven[:].rearrange("p (c i) j -> p c j i", i=4),
+                picked[:, :, a:b].rearrange("p j (c i) -> p c j i", i=4),
+            )
+            return woven
 
-        def project(c):
-            codes = sb.tile([P, PIECE], U32, name=f"codes{c}", tag=f"codes{c}", align_bytes=64)
-            scales = sb.tile([P, PIECE], U8, name=f"scales{c}", align_bytes=64)
-            nc.vector.quantize_mx(out=codes[:].bitcast(FP8X4), scales=scales[:], in_=woven[c][:].rearrange("p n j -> p (n j)"))
+        def project(woven, a, b):
+            codes = sb.tile([P, b - a], U32, name=f"codes{a}", align_bytes=64)
+            scales = sb.tile([P, b - a], U8, name=f"scales{a}", align_bytes=64)
+            bank = ps.tile([N, b - a], F32, name=f"bank{a}")
+            nc.vector.quantize_mx(out=codes[:].bitcast(FP8X4), scales=scales[:], in_=woven[:].rearrange("p n j -> p (n j)"))
             nc.tensor.matmul_mx(
-                out=banks[c][:],
+                out=bank[:],
                 lhsT=w_codes[:].bitcast(FP4X4),
                 lhsT_scale=w_scales[:],
                 rhs=codes[:].bitcast(FP8X4),
@@ -82,47 +69,29 @@ def tile_picked_idxput_add_e_kernel(tc, xT, mem, w1_words, w1_scales, offs, slot
                 start=True,
                 stop=True,
             )
-
-        def drain(c):
-            nc.scalar.copy(y[:, c * PIECE : (c + 1) * PIECE], banks[c][:])
-
-        def put(old, a, b):
-            nc.vector.tensor_tensor(store[:].indirect(entries(slot_sb, a, b)), old[:, a:b], y[:, a:b], ADD)
+            return bank
 
         nc.vector.memset(w_scales[:].bitcast(I32), 0)
-        load_plane(0)
+        nc.sync.dma_start(planes[0][:], x_rows[:, 0, :])
         nc.sync.dma_start(offs_sb[:], offs)
-        last = S - PIECE
-        for j in range(PACK - 1):
-            if j == 1:
-                nc.sync.dma_start(slot_sb[:], slot)
-            pick_on_vector(j, 0, PIECE)
-            pick_on_vector(j, PIECE, last if j in SHARED else S)
-            if j in SHARED:
-                pick_on_scalar(j, last, S)
-            load_plane(j + 1)
+        for j in range(1, PACK):
+            nc.sync.dma_start(planes[j][:], x_rows[:, j, :])
+        nc.sync.dma_start(slot_sb[:], slot)
         nc.sync.dma_start(store[:], mem)
         nc.sync.dma_start(w_codes[:].bitcast(I32), w1_words[0].bitcast(I32))
         for q in range(4):
             nc.sync.dma_start(w_scales[32 * q : 32 * q + 4, :].bitcast(I32), w1_scales[0, 4 * q : 4 * q + 4, :].bitcast(I32))
 
-        for a, b in ((0, 128), (128, 256), (256, 512), (512, SPLIT)):
-            pick_on_vector(PACK - 1, a, b)
-        weave(0, 128)
-        weave(128, 256)
-        project(0)
-        old = sb.tile([P, S], F32, name="old", tag="first", align_bytes=64)
+        for j in range(PACK - 1):
+            pick(j, 0, S)
+        for a, b in LAST_GATHERS:
+            pick(PACK - 1, a, b)
+        woven = [weave(a, b) for a, b in PIECES]
+        banks = [project(woven[c], *PIECES[c]) for c in range(2)]
         nc.vector.tensor_copy(old[:], store[:].indirect(slot_sb[:]))
-        weave(256, 512)
-        project(1)
-        drain(0)
-        woven[2] = sb.tile([P, PIECE, PACK], BF16, name="woven2", tag="codes0", align_bytes=64)
-        weave(512, 768)
-        project(2)
-        weave(last, S)
-        project(3)
-        for c in range(1, PIECES):
-            drain(c)
-        for a, b in ((0, 256), (256, 512), (512, 1024)):
-            put(old, a, b)
+        banks = banks + [project(woven[c], *PIECES[c]) for c in range(2, len(PIECES))]
+        for (a, b), bank in zip(PIECES, banks):
+            nc.scalar.copy(y[:, a:b], bank[:])
+        for a, b in SCATTERS:
+            nc.vector.tensor_tensor(store[:].indirect(entries(slot_sb, a, b)), old[:, a:b], y[:, a:b], ADD)
         nc.sync.dma_start(out, store[:])

@@ -19,9 +19,11 @@ COPY = mybir.ActivationFunctionType.Copy
 P = 128
 PACK = 4
 LANES = 16
-PIECES = [(0, 128), (128, 256), (256, 512), (512, 768), (768, 1024)]
-LAST_GATHERS = [(0, 128), (128, 256), (256, 512), (512, 1024)]
-SCATTERS = [(0, 256), (256, 1024)]
+PIECE = 256
+PIECES = S // PIECE
+SHARE = 768
+LAST_LOADS = 4
+SCATTERS = [(0, 256), (256, 768), (768, 1024)]
 
 
 def tile_picked_idxput_add_e_kernel(tc, xT, mem, w1_words, w1_scales, offs, slot, out):
@@ -33,12 +35,15 @@ def tile_picked_idxput_add_e_kernel(tc, xT, mem, w1_words, w1_scales, offs, slot
         offs_sb = sb.tile([P, S // LANES], U16, name="offs_sb")
         slot_sb = sb.tile([P, S // LANES], U16, name="slot_sb")
         planes = [sb.tile([P, T], F32, name=f"plane{j}") for j in range(PACK)]
+        rounded = sb.tile([P, T], BF16, name="rounded")
         store = sb.tile([P, U], F32, name="store")
         w_codes = sb.tile([P, 2 * N], U8, name="w_codes", align_bytes=64)
         w_scales = sb.tile([P, N], U8, name="w_scales", align_bytes=64)
-        picked = sb.tile([P, PACK, S], BF16, name="picked", align_bytes=64)
-        old = sb.tile([P, S], F32, name="old")
+        shared = sb.tile([P, 2 * S - PIECE + PACK * S], BF16, name="shared", align_bytes=64)
+        picked = shared[:, 2 * S - PIECE :].rearrange("p (j n) -> p j n", j=PACK)
+        old = shared[:, : 2 * S].bitcast(F32)
         y = sb.tile([P, S], F32, name="y")
+        banks = [ps.tile([N, PIECE], F32, name=f"bank{c}") for c in range(PIECES)]
         x_rows = xT.rearrange("(p j) t -> p j t", j=PACK)
 
         def entries(lst, a, b):
@@ -47,21 +52,20 @@ def tile_picked_idxput_add_e_kernel(tc, xT, mem, w1_words, w1_scales, offs, slot
         def pick(j, a, b):
             nc.vector.tensor_copy(picked[:, j, a:b], planes[j][:].indirect(entries(offs_sb, a, b)))
 
-        def weave(a, b):
-            woven = sb.tile([P, b - a, PACK], BF16, name=f"woven{a}", align_bytes=64)
+        def weave(c, tag):
+            woven = sb.tile([P, PIECE, PACK], BF16, name=f"woven{c}", tag=tag, align_bytes=64)
             nc.scalar.copy(
                 woven[:].rearrange("p (c i) j -> p c j i", i=4),
-                picked[:, :, a:b].rearrange("p j (c i) -> p c j i", i=4),
+                picked[:, :, c * PIECE : (c + 1) * PIECE].rearrange("p j (c i) -> p c j i", i=4),
             )
             return woven
 
-        def project(woven, a, b):
-            codes = sb.tile([P, b - a], U32, name=f"codes{a}", align_bytes=64)
-            scales = sb.tile([P, b - a], U8, name=f"scales{a}", align_bytes=64)
-            bank = ps.tile([N, b - a], F32, name=f"bank{a}")
+        def project(c, woven):
+            codes = sb.tile([P, PIECE], U32, name=f"codes{c}", tag=f"codes{c}", align_bytes=64)
+            scales = sb.tile([P, PIECE], U8, name=f"scales{c}", align_bytes=64)
             nc.vector.quantize_mx(out=codes[:].bitcast(FP8X4), scales=scales[:], in_=woven[:].rearrange("p n j -> p (n j)"))
             nc.tensor.matmul_mx(
-                out=bank[:],
+                out=banks[c][:],
                 lhsT=w_codes[:].bitcast(FP4X4),
                 lhsT_scale=w_scales[:],
                 rhs=codes[:].bitcast(FP8X4),
@@ -69,29 +73,46 @@ def tile_picked_idxput_add_e_kernel(tc, xT, mem, w1_words, w1_scales, offs, slot
                 start=True,
                 stop=True,
             )
-            return bank
 
+        def drain(c):
+            nc.scalar.copy(y[:, c * PIECE : (c + 1) * PIECE], banks[c][:])
+
+        def put(a, b):
+            nc.vector.tensor_tensor(store[:].indirect(entries(slot_sb, a, b)), old[:, a:b], y[:, a:b], ADD)
+
+        last = PACK - 1
         nc.vector.memset(w_scales[:].bitcast(I32), 0)
         nc.sync.dma_start(planes[0][:], x_rows[:, 0, :])
         nc.sync.dma_start(offs_sb[:], offs)
-        for j in range(1, PACK):
+        for j in range(1, last):
             nc.sync.dma_start(planes[j][:], x_rows[:, j, :])
+        width = T // LAST_LOADS
+        for a in range(0, T, width):
+            nc.sync.dma_start(planes[last][:, a : a + width], x_rows[:, last, a : a + width])
+            nc.scalar.copy(rounded[:, a : a + width], planes[last][:, a : a + width])
         nc.sync.dma_start(slot_sb[:], slot)
         nc.sync.dma_start(store[:], mem)
         nc.sync.dma_start(w_codes[:].bitcast(I32), w1_words[0].bitcast(I32))
         for q in range(4):
             nc.sync.dma_start(w_scales[32 * q : 32 * q + 4, :].bitcast(I32), w1_scales[0, 4 * q : 4 * q + 4, :].bitcast(I32))
 
-        for j in range(PACK - 1):
+        for j in range(last):
             pick(j, 0, S)
-        for a, b in LAST_GATHERS:
-            pick(PACK - 1, a, b)
-        woven = [weave(a, b) for a, b in PIECES]
-        banks = [project(woven[c], *PIECES[c]) for c in range(2)]
-        nc.vector.tensor_copy(old[:], store[:].indirect(slot_sb[:]))
-        banks = banks + [project(woven[c], *PIECES[c]) for c in range(2, len(PIECES))]
-        for (a, b), bank in zip(PIECES, banks):
-            nc.scalar.copy(y[:, a:b], bank[:])
-        for a, b in SCATTERS:
-            nc.vector.tensor_tensor(store[:].indirect(entries(slot_sb, a, b)), old[:, a:b], y[:, a:b], ADD)
+        for a in range(0, SHARE, PIECE):
+            pick(last, a, min(a + PIECE, SHARE))
+        woven = [weave(0, "woven0")]
+        nc.scalar.activation(picked[:, last, SHARE:S], rounded[:].indirect(entries(offs_sb, SHARE, S)), COPY)
+        woven = woven + [weave(c, f"woven{c}") for c in range(1, PIECES - 1)]
+        project(0, woven[0])
+        nc.vector.tensor_copy(old, store[:].indirect(slot_sb[:]))
+        drain(0)
+        woven.append(weave(PIECES - 1, "codes0"))
+        project(1, woven[1])
+        project(2, woven[2])
+        put(*SCATTERS[0])
+        project(3, woven[3])
+        for c in range(1, PIECES):
+            drain(c)
+        for a, b in SCATTERS[1:]:
+            put(a, b)
         nc.sync.dma_start(out, store[:])

@@ -23,6 +23,7 @@ PIECE = 256
 PIECES = S // PIECE
 SHARE = 768
 LAST_LOADS = 4
+EARLY = 1
 SCATTERS = [(0, 256), (256, 768), (768, 1024)]
 
 
@@ -36,6 +37,7 @@ def tile_picked_idxput_add_e_kernel(tc, xT, mem, w1_words, w1_scales, offs, slot
         slot_sb = sb.tile([P, S // LANES], U16, name="slot_sb")
         planes = [sb.tile([P, T], F32, name=f"plane{j}") for j in range(PACK)]
         rounded = sb.tile([P, T], BF16, name="rounded")
+        rounded_early = sb.tile([P, T], BF16, name="rounded_early")
         store = sb.tile([P, U], F32, name="store")
         w_codes = sb.tile([P, 2 * N], U8, name="w_codes", align_bytes=64)
         w_scales = sb.tile([P, N], U8, name="w_scales", align_bytes=64)
@@ -86,6 +88,8 @@ def tile_picked_idxput_add_e_kernel(tc, xT, mem, w1_words, w1_scales, offs, slot
         nc.sync.dma_start(offs_sb[:], offs)
         for j in range(1, last):
             nc.sync.dma_start(planes[j][:], x_rows[:, j, :])
+        nc.scalar.copy(rounded_early[:], planes[EARLY][:])
+        nc.scalar.activation(picked[:, EARLY, SHARE:S], rounded_early[:].indirect(entries(offs_sb, SHARE, S)), COPY)
         width = T // LAST_LOADS
         for a in range(0, T, width):
             nc.sync.dma_start(planes[last][:, a : a + width], x_rows[:, last, a : a + width])
@@ -97,7 +101,7 @@ def tile_picked_idxput_add_e_kernel(tc, xT, mem, w1_words, w1_scales, offs, slot
             nc.sync.dma_start(w_scales[32 * q : 32 * q + 4, :].bitcast(I32), w1_scales[0, 4 * q : 4 * q + 4, :].bitcast(I32))
 
         for j in range(last):
-            pick(j, 0, S)
+            pick(j, 0, SHARE if j == EARLY else S)
         for a in range(0, SHARE, PIECE):
             pick(last, a, min(a + PIECE, SHARE))
         woven = [weave(0, "woven0")]

@@ -19,12 +19,13 @@ COPY = mybir.ActivationFunctionType.Copy
 P = 128
 PACK = 4
 LANES = 16
-PIECE = 256
-PIECES = S // PIECE
-SHARE = 768
+PIECES = [(0, 128), (128, 256), (256, 512), (512, 768), (768, 1024)]
+FIRST = 256
+SHARE = 640
+LAST_GATHERS = [(0, 128), (128, 256), (256, SHARE)]
 LAST_LOADS = 4
 EARLY = 1
-SCATTERS = [(0, 256), (256, 768), (768, 1024)]
+EARLY_SHARE = 896
 
 
 def tile_picked_idxput_add_e_kernel(tc, xT, mem, w1_words, w1_scales, offs, slot, out):
@@ -41,11 +42,12 @@ def tile_picked_idxput_add_e_kernel(tc, xT, mem, w1_words, w1_scales, offs, slot
         store = sb.tile([P, U], F32, name="store")
         w_codes = sb.tile([P, 2 * N], U8, name="w_codes", align_bytes=64)
         w_scales = sb.tile([P, N], U8, name="w_scales", align_bytes=64)
-        shared = sb.tile([P, 2 * S - PIECE + PACK * S], BF16, name="shared", align_bytes=64)
-        picked = shared[:, 2 * S - PIECE :].rearrange("p (j n) -> p j n", j=PACK)
+        shared = sb.tile([P, 2 * S - FIRST + PACK * S], BF16, name="shared", align_bytes=64)
+        picked = shared[:, 2 * S - FIRST :].rearrange("p (j n) -> p j n", j=PACK)
         old = shared[:, : 2 * S].bitcast(F32)
         y = sb.tile([P, S], F32, name="y")
-        banks = [ps.tile([N, PIECE], F32, name=f"bank{c}") for c in range(PIECES)]
+        y_second = picked[:, 1, 256:768].bitcast(F32)
+        banks = [ps.tile([N, b - a], F32, name=f"bank{a}") for a, b in PIECES]
         x_rows = xT.rearrange("(p j) t -> p j t", j=PACK)
 
         def entries(lst, a, b):
@@ -55,16 +57,18 @@ def tile_picked_idxput_add_e_kernel(tc, xT, mem, w1_words, w1_scales, offs, slot
             nc.vector.tensor_copy(picked[:, j, a:b], planes[j][:].indirect(entries(offs_sb, a, b)))
 
         def weave(c, tag):
-            woven = sb.tile([P, PIECE, PACK], BF16, name=f"woven{c}", tag=tag, align_bytes=64)
+            a, b = PIECES[c]
+            woven = sb.tile([P, b - a, PACK], BF16, name=f"woven{c}", tag=tag, align_bytes=64)
             nc.scalar.copy(
                 woven[:].rearrange("p (c i) j -> p c j i", i=4),
-                picked[:, :, c * PIECE : (c + 1) * PIECE].rearrange("p j (c i) -> p c j i", i=4),
+                picked[:, :, a:b].rearrange("p j (c i) -> p c j i", i=4),
             )
             return woven
 
         def project(c, woven):
-            codes = sb.tile([P, PIECE], U32, name=f"codes{c}", tag=f"codes{c}", align_bytes=64)
-            scales = sb.tile([P, PIECE], U8, name=f"scales{c}", align_bytes=64)
+            a, b = PIECES[c]
+            codes = sb.tile([P, b - a], U32, name=f"codes{c}", tag=f"codes{c}", align_bytes=64)
+            scales = sb.tile([P, b - a], U8, name=f"scales{c}", align_bytes=64)
             nc.vector.quantize_mx(out=codes[:].bitcast(FP8X4), scales=scales[:], in_=woven[:].rearrange("p n j -> p (n j)"))
             nc.tensor.matmul_mx(
                 out=banks[c][:],
@@ -77,10 +81,11 @@ def tile_picked_idxput_add_e_kernel(tc, xT, mem, w1_words, w1_scales, offs, slot
             )
 
         def drain(c):
-            nc.scalar.copy(y[:, c * PIECE : (c + 1) * PIECE], banks[c][:])
+            a, b = PIECES[c]
+            nc.scalar.copy(y_second if c == 2 else y[:, a:b], banks[c][:])
 
-        def put(a, b):
-            nc.vector.tensor_tensor(store[:].indirect(entries(slot_sb, a, b)), old[:, a:b], y[:, a:b], ADD)
+        def put(a, b, new):
+            nc.vector.tensor_tensor(store[:].indirect(entries(slot_sb, a, b)), old[:, a:b], new, ADD)
 
         last = PACK - 1
         nc.vector.memset(w_scales[:].bitcast(I32), 0)
@@ -89,7 +94,7 @@ def tile_picked_idxput_add_e_kernel(tc, xT, mem, w1_words, w1_scales, offs, slot
         for j in range(1, last):
             nc.sync.dma_start(planes[j][:], x_rows[:, j, :])
         nc.scalar.copy(rounded_early[:], planes[EARLY][:])
-        nc.scalar.activation(picked[:, EARLY, SHARE:S], rounded_early[:].indirect(entries(offs_sb, SHARE, S)), COPY)
+        nc.scalar.activation(picked[:, EARLY, EARLY_SHARE:S], rounded_early[:].indirect(entries(offs_sb, EARLY_SHARE, S)), COPY)
         width = T // LAST_LOADS
         for a in range(0, T, width):
             nc.sync.dma_start(planes[last][:, a : a + width], x_rows[:, last, a : a + width])
@@ -101,22 +106,25 @@ def tile_picked_idxput_add_e_kernel(tc, xT, mem, w1_words, w1_scales, offs, slot
             nc.sync.dma_start(w_scales[32 * q : 32 * q + 4, :].bitcast(I32), w1_scales[0, 4 * q : 4 * q + 4, :].bitcast(I32))
 
         for j in range(last):
-            pick(j, 0, SHARE if j == EARLY else S)
-        for a in range(0, SHARE, PIECE):
-            pick(last, a, min(a + PIECE, SHARE))
-        woven = [weave(0, "woven0")]
+            pick(j, 0, EARLY_SHARE if j == EARLY else S)
+        for a, b in LAST_GATHERS:
+            pick(last, a, b)
+        woven = [weave(c, f"woven{c}") for c in range(2)]
         nc.scalar.activation(picked[:, last, SHARE:S], rounded[:].indirect(entries(offs_sb, SHARE, S)), COPY)
-        woven = woven + [weave(c, f"woven{c}") for c in range(1, PIECES - 1)]
+        woven.append(weave(2, "woven2"))
         project(0, woven[0])
-        nc.vector.tensor_copy(old, store[:].indirect(slot_sb[:]))
-        drain(0)
-        woven.append(weave(PIECES - 1, "codes0"))
         project(1, woven[1])
+        nc.vector.tensor_copy(old, store[:].indirect(slot_sb[:]))
         project(2, woven[2])
-        put(*SCATTERS[0])
-        project(3, woven[3])
-        for c in range(1, PIECES):
-            drain(c)
-        for a, b in SCATTERS[1:]:
-            put(a, b)
+        drain(0)
+        drain(1)
+        put(0, 256, y[:, 0:256])
+        project(3, weave(3, "codes1"))
+        drain(2)
+        put(256, 512, y_second)
+        project(4, weave(4, "codes2"))
+        drain(3)
+        put(512, 768, y[:, 512:768])
+        drain(4)
+        put(768, S, y[:, 768:S])
         nc.sync.dma_start(out, store[:])

@@ -21,9 +21,10 @@ PACK = 4
 LANES = 16
 PIECES = [(0, 128), (128, 256), (256, 512), (512, 768), (768, 1024)]
 FIRST = 256
-SHARE = 640
+SHARE = 576
 LAST_GATHERS = [(0, 128), (128, 256), (256, SHARE)]
-LAST_LOADS = 4
+LAST_LOADS = [(0, T // 2), (T // 2, T)]
+VECTOR_ROUNDS = 1536
 EARLY = 1
 EARLY_SHARE = 896
 
@@ -95,10 +96,9 @@ def tile_picked_idxput_add_e_kernel(tc, xT, mem, w1_words, w1_scales, offs, slot
             nc.sync.dma_start(planes[j][:], x_rows[:, j, :])
         nc.scalar.copy(rounded_early[:], planes[EARLY][:])
         nc.scalar.activation(picked[:, EARLY, EARLY_SHARE:S], rounded_early[:].indirect(entries(offs_sb, EARLY_SHARE, S)), COPY)
-        width = T // LAST_LOADS
-        for a in range(0, T, width):
-            nc.sync.dma_start(planes[last][:, a : a + width], x_rows[:, last, a : a + width])
-            nc.scalar.copy(rounded[:, a : a + width], planes[last][:, a : a + width])
+        for a, b in LAST_LOADS:
+            nc.sync.dma_start(planes[last][:, a:b], x_rows[:, last, a:b])
+            nc.scalar.copy(rounded[:, a : min(b, VECTOR_ROUNDS)], planes[last][:, a : min(b, VECTOR_ROUNDS)])
         nc.sync.dma_start(slot_sb[:], slot)
         nc.sync.dma_start(store[:], mem)
         nc.sync.dma_start(w_codes[:].bitcast(I32), w1_words[0].bitcast(I32))
@@ -107,8 +107,10 @@ def tile_picked_idxput_add_e_kernel(tc, xT, mem, w1_words, w1_scales, offs, slot
 
         for j in range(last):
             pick(j, 0, EARLY_SHARE if j == EARLY else S)
-        for a, b in LAST_GATHERS:
+        for a, b in LAST_GATHERS[:2]:
             pick(last, a, b)
+        nc.vector.tensor_copy(rounded[:, VECTOR_ROUNDS:], planes[last][:, VECTOR_ROUNDS:])
+        pick(last, *LAST_GATHERS[2])
         woven = [weave(c, f"woven{c}") for c in range(2)]
         nc.scalar.activation(picked[:, last, SHARE:S], rounded[:].indirect(entries(offs_sb, SHARE, S)), COPY)
         woven.append(weave(2, "woven2"))

@@ -19,14 +19,12 @@ COPY = mybir.ActivationFunctionType.Copy
 P = 128
 PACK = 4
 LANES = 16
-PIECES = [(0, 128), (128, 256), (256, 512), (512, 768), (768, 1024)]
-FIRST = 256
-SHARE = 576
-LAST_GATHERS = [(0, 128), (128, 256), (256, SHARE)]
+BLOCK = 128
+GROUP = 256
 LAST_LOADS = [(0, T // 2), (T // 2, T)]
-VECTOR_ROUNDS = 1536
+FIRST_ROUND = 1408
 EARLY = 1
-EARLY_SHARE = 896
+EARLY_SHARE = 768
 
 
 def tile_picked_idxput_add_e_kernel(tc, xT, mem, w1_words, w1_scales, offs, slot, out):
@@ -43,12 +41,19 @@ def tile_picked_idxput_add_e_kernel(tc, xT, mem, w1_words, w1_scales, offs, slot
         store = sb.tile([P, U], F32, name="store")
         w_codes = sb.tile([P, 2 * N], U8, name="w_codes", align_bytes=64)
         w_scales = sb.tile([P, N], U8, name="w_scales", align_bytes=64)
-        shared = sb.tile([P, 2 * S - FIRST + PACK * S], BF16, name="shared", align_bytes=64)
-        picked = shared[:, 2 * S - FIRST :].rearrange("p (j n) -> p j n", j=PACK)
+        base = 2 * S - GROUP
+        shared = sb.tile([P, base + PACK * S + GROUP], BF16, name="shared", align_bytes=64)
+        picked = shared[:, base : base + PACK * S].rearrange("p (j n) -> p j n", j=PACK)
         old = shared[:, : 2 * S].bitcast(F32)
-        y = sb.tile([P, S], F32, name="y")
-        y_second = picked[:, 1, 256:768].bitcast(F32)
-        banks = [ps.tile([N, b - a], F32, name=f"bank{a}") for a, b in PIECES]
+        y_first = sb.tile([P, GROUP], F32, name="y_first")
+        y_last = sb.tile([P, GROUP], F32, name="y_last")
+        y = [
+            y_first[:],
+            shared[:, base + S + GROUP : base + S + 3 * GROUP].bitcast(F32),
+            shared[:, base + S + 3 * GROUP : base + 2 * S + GROUP].bitcast(F32),
+            y_last[:],
+        ]
+        banks = [ps.tile([N, GROUP], F32, name=f"bank{g}") for g in range(S // GROUP)]
         x_rows = xT.rearrange("(p j) t -> p j t", j=PACK)
 
         def entries(lst, a, b):
@@ -57,36 +62,43 @@ def tile_picked_idxput_add_e_kernel(tc, xT, mem, w1_words, w1_scales, offs, slot
         def pick(j, a, b):
             nc.vector.tensor_copy(picked[:, j, a:b], planes[j][:].indirect(entries(offs_sb, a, b)))
 
-        def weave(c, tag):
-            a, b = PIECES[c]
-            woven = sb.tile([P, b - a, PACK], BF16, name=f"woven{c}", tag=tag, align_bytes=64)
-            nc.scalar.copy(
-                woven[:].rearrange("p (c i) j -> p c j i", i=4),
+        def pick_rounded(j, window, a, b):
+            nc.scalar.activation(picked[:, j, a:b], window[:].indirect(entries(offs_sb, a, b)), COPY)
+
+        def weave(copy, woven, a, b):
+            copy(
+                woven.rearrange("p (c i j) -> p c j i", i=4, j=PACK),
                 picked[:, :, a:b].rearrange("p j (c i) -> p c j i", i=4),
             )
-            return woven
 
-        def project(c, woven):
-            a, b = PIECES[c]
-            codes = sb.tile([P, b - a], U32, name=f"codes{c}", tag=f"codes{c}", align_bytes=64)
-            scales = sb.tile([P, b - a], U8, name=f"scales{c}", align_bytes=64)
-            nc.vector.quantize_mx(out=codes[:].bitcast(FP8X4), scales=scales[:], in_=woven[:].rearrange("p n j -> p (n j)"))
+        def woven_tile(name, n, tag=None):
+            return sb.tile([P, n * PACK], BF16, name=name, tag=tag or name, align_bytes=64)[:]
+
+        def mx_tiles(name, n, tag=None):
+            codes = sb.tile([P, n], U32, name=f"codes{name}", tag=tag or f"codes{name}", align_bytes=64)
+            scales = sb.tile([P, n], U8, name=f"scales{name}", tag=f"scales{name}", align_bytes=64)
+            return codes[:], scales[:]
+
+        def quantise(codes, scales, woven):
+            nc.vector.quantize_mx(out=codes.bitcast(FP8X4), scales=scales, in_=woven)
+
+        def project(bank, codes, scales):
             nc.tensor.matmul_mx(
-                out=banks[c][:],
+                out=bank,
                 lhsT=w_codes[:].bitcast(FP4X4),
                 lhsT_scale=w_scales[:],
-                rhs=codes[:].bitcast(FP8X4),
-                rhs_scale=scales[:],
+                rhs=codes.bitcast(FP8X4),
+                rhs_scale=scales,
                 start=True,
                 stop=True,
             )
 
-        def drain(c):
-            a, b = PIECES[c]
-            nc.scalar.copy(y_second if c == 2 else y[:, a:b], banks[c][:])
+        def drain(g):
+            nc.scalar.copy(y[g], banks[g][:])
 
-        def put(a, b, new):
-            nc.vector.tensor_tensor(store[:].indirect(entries(slot_sb, a, b)), old[:, a:b], new, ADD)
+        def put(g):
+            a, b = g * GROUP, (g + 1) * GROUP
+            nc.vector.tensor_tensor(store[:].indirect(entries(slot_sb, a, b)), old[:, a:b], y[g], ADD)
 
         last = PACK - 1
         nc.vector.memset(w_scales[:].bitcast(I32), 0)
@@ -94,39 +106,62 @@ def tile_picked_idxput_add_e_kernel(tc, xT, mem, w1_words, w1_scales, offs, slot
         nc.sync.dma_start(offs_sb[:], offs)
         for j in range(1, last):
             nc.sync.dma_start(planes[j][:], x_rows[:, j, :])
-        nc.scalar.copy(rounded_early[:], planes[EARLY][:])
-        nc.scalar.activation(picked[:, EARLY, EARLY_SHARE:S], rounded_early[:].indirect(entries(offs_sb, EARLY_SHARE, S)), COPY)
         for a, b in LAST_LOADS:
             nc.sync.dma_start(planes[last][:, a:b], x_rows[:, last, a:b])
-            nc.scalar.copy(rounded[:, a : min(b, VECTOR_ROUNDS)], planes[last][:, a : min(b, VECTOR_ROUNDS)])
         nc.sync.dma_start(slot_sb[:], slot)
         nc.sync.dma_start(store[:], mem)
         nc.sync.dma_start(w_codes[:].bitcast(I32), w1_words[0].bitcast(I32))
         for q in range(4):
             nc.sync.dma_start(w_scales[32 * q : 32 * q + 4, :].bitcast(I32), w1_scales[0, 4 * q : 4 * q + 4, :].bitcast(I32))
 
+        nc.scalar.copy(rounded_early[:], planes[EARLY][:])
+        pick_rounded(EARLY, rounded_early, EARLY_SHARE, S)
+        nc.scalar.copy(rounded[:, : T // 2], planes[last][:, : T // 2])
         for j in range(last):
             pick(j, 0, EARLY_SHARE if j == EARLY else S)
-        for a, b in LAST_GATHERS[:2]:
-            pick(last, a, b)
-        nc.vector.tensor_copy(rounded[:, VECTOR_ROUNDS:], planes[last][:, VECTOR_ROUNDS:])
-        pick(last, *LAST_GATHERS[2])
-        woven = [weave(c, f"woven{c}") for c in range(2)]
-        nc.scalar.activation(picked[:, last, SHARE:S], rounded[:].indirect(entries(offs_sb, SHARE, S)), COPY)
-        woven.append(weave(2, "woven2"))
-        project(0, woven[0])
-        project(1, woven[1])
+        pick(last, 0, 128)
+        pick(last, 128, 384)
+        pick(last, 384, 512)
+
+        nc.scalar.copy(rounded[:, T // 2 : FIRST_ROUND], planes[last][:, T // 2 : FIRST_ROUND])
+        woven = [woven_tile(f"woven{c}", BLOCK) for c in range(3)]
+        woven.append(shared[:, base + PACK * S - GROUP :])
+        weave(nc.scalar.copy, woven[0], 0, 128)
+        weave(nc.scalar.copy, woven[1], 128, 256)
+        weave(nc.vector.tensor_copy, woven[2], 256, 384)
+        weave(nc.scalar.copy, woven[3], 384, 512)
+        codes_a, scales_a = mx_tiles("a", GROUP)
+        codes_b, scales_b = mx_tiles("b", BLOCK)
+        quantise(codes_a[:, :BLOCK], scales_a[:, :BLOCK], woven[0])
+        quantise(codes_b, scales_b, woven[2])
+        quantise(codes_a[:, BLOCK:], scales_a[:, BLOCK:], woven[1])
+        project(banks[0][:], codes_a, scales_a)
+        project(banks[1][:, :BLOCK], codes_b, scales_b)
         nc.vector.tensor_copy(old, store[:].indirect(slot_sb[:]))
-        project(2, woven[2])
+        nc.scalar.copy(rounded[:, FIRST_ROUND:], planes[last][:, FIRST_ROUND:])
         drain(0)
+        pick_rounded(last, rounded, 512, 768)
+        codes_c, scales_c = mx_tiles("c", BLOCK, tag="codesa")
+        quantise(codes_c, scales_c, woven[3])
+        project(banks[1][:, BLOCK:], codes_c, scales_c)
+        put(0)
+
+        woven_d = woven_tile("woven_d", GROUP, tag="scalesa")
+        weave(nc.scalar.copy, woven_d, 512, 768)
+        codes_d, scales_d = mx_tiles("d", GROUP)
+        quantise(codes_d, scales_d, woven_d)
+        project(banks[2][:], codes_d, scales_d)
         drain(1)
-        put(0, 256, y[:, 0:256])
-        project(3, weave(3, "codes1"))
+        put(1)
+
+        pick_rounded(last, rounded, 768, S)
+        woven_e = woven_tile("woven_e", GROUP)
+        weave(nc.scalar.copy, woven_e, 768, S)
+        codes_e, scales_e = mx_tiles("e", GROUP)
+        quantise(codes_e, scales_e, woven_e)
+        project(banks[3][:], codes_e, scales_e)
         drain(2)
-        put(256, 512, y_second)
-        project(4, weave(4, "codes2"))
+        put(2)
         drain(3)
-        put(512, 768, y[:, 512:768])
-        drain(4)
-        put(768, S, y[:, 768:S])
+        put(3)
         nc.sync.dma_start(out, store[:])

@@ -22,9 +22,8 @@ LANES = 16
 BLOCK = 128
 GROUP = 256
 LAST_LOADS = [(0, T // 2), (T // 2, T)]
-FIRST_ROUND = 1408
 EARLY = 1
-EARLY_SHARE = 768
+EARLY_SHARE = 832
 
 
 def tile_picked_idxput_add_e_kernel(tc, xT, mem, w1_words, w1_scales, offs, slot, out):
@@ -36,13 +35,12 @@ def tile_picked_idxput_add_e_kernel(tc, xT, mem, w1_words, w1_scales, offs, slot
         offs_sb = sb.tile([P, S // LANES], U16, name="offs_sb")
         slot_sb = sb.tile([P, S // LANES], U16, name="slot_sb")
         planes = [sb.tile([P, T], F32, name=f"plane{j}") for j in range(PACK)]
-        rounded = sb.tile([P, T], BF16, name="rounded")
-        rounded_early = sb.tile([P, T], BF16, name="rounded_early")
+        rounded_early = sb.tile([P, T], BF16, name="rounded_early", tag="rounded")
         store = sb.tile([P, U], F32, name="store")
         w_codes = sb.tile([P, 2 * N], U8, name="w_codes", align_bytes=64)
         w_scales = sb.tile([P, N], U8, name="w_scales", align_bytes=64)
         base = 2 * S - GROUP
-        shared = sb.tile([P, base + PACK * S + GROUP], BF16, name="shared", align_bytes=64)
+        shared = sb.tile([P, base + PACK * S + (PACK - 1) * GROUP], BF16, name="shared", align_bytes=64)
         picked = shared[:, base : base + PACK * S].rearrange("p (j n) -> p j n", j=PACK)
         old = shared[:, : 2 * S].bitcast(F32)
         y_first = sb.tile([P, GROUP], F32, name="y_first")
@@ -116,52 +114,40 @@ def tile_picked_idxput_add_e_kernel(tc, xT, mem, w1_words, w1_scales, offs, slot
 
         nc.scalar.copy(rounded_early[:], planes[EARLY][:])
         pick_rounded(EARLY, rounded_early, EARLY_SHARE, S)
+        rounded = sb.tile([P, T], BF16, name="rounded", tag="rounded")
         nc.scalar.copy(rounded[:, : T // 2], planes[last][:, : T // 2])
         for j in range(last):
             pick(j, 0, EARLY_SHARE if j == EARLY else S)
         pick(last, 0, 128)
-        pick(last, 128, 384)
-        pick(last, 384, 512)
+        pick(last, 128, 256)
 
-        nc.scalar.copy(rounded[:, T // 2 : FIRST_ROUND], planes[last][:, T // 2 : FIRST_ROUND])
-        woven = [woven_tile(f"woven{c}", BLOCK) for c in range(3)]
-        woven.append(shared[:, base + PACK * S - GROUP :])
-        weave(nc.scalar.copy, woven[0], 0, 128)
+        nc.scalar.copy(rounded[:, T // 2 :], planes[last][:, T // 2 :])
+        woven = [woven_tile(f"woven{c}", BLOCK) for c in range(2)]
+        weave(nc.vector.tensor_copy, woven[0], 0, 128)
+        pick(last, 256, 384)
         weave(nc.scalar.copy, woven[1], 128, 256)
-        weave(nc.vector.tensor_copy, woven[2], 256, 384)
-        weave(nc.scalar.copy, woven[3], 384, 512)
-        codes_a, scales_a = mx_tiles("a", GROUP)
-        codes_b, scales_b = mx_tiles("b", BLOCK)
-        quantise(codes_a[:, :BLOCK], scales_a[:, :BLOCK], woven[0])
-        quantise(codes_b, scales_b, woven[2])
-        quantise(codes_a[:, BLOCK:], scales_a[:, BLOCK:], woven[1])
-        project(banks[0][:], codes_a, scales_a)
-        project(banks[1][:, :BLOCK], codes_b, scales_b)
+        mx = {g: mx_tiles(g, GROUP) for g in (0, 2, 3)}
+        for c in range(2):
+            quantise(mx[0][0][:, c * BLOCK : (c + 1) * BLOCK], mx[0][1][:, c * BLOCK : (c + 1) * BLOCK], woven[c])
+        project(banks[0][:], *mx[0])
         nc.vector.tensor_copy(old, store[:].indirect(slot_sb[:]))
-        nc.scalar.copy(rounded[:, FIRST_ROUND:], planes[last][:, FIRST_ROUND:])
-        drain(0)
+        pick_rounded(last, rounded, 384, 512)
         pick_rounded(last, rounded, 512, 768)
-        codes_c, scales_c = mx_tiles("c", BLOCK, tag="codesa")
-        quantise(codes_c, scales_c, woven[3])
-        project(banks[1][:, BLOCK:], codes_c, scales_c)
+        woven_b = shared[:, base + PACK * S - GROUP :]
+        weave(nc.scalar.copy, woven_b, 256, 512)
+        drain(0)
+        codes_b, scales_b = mx_tiles("b", GROUP, tag="codes0")
+        quantise(codes_b, scales_b, woven_b)
+        project(banks[1][:], codes_b, scales_b)
         put(0)
-
-        woven_d = woven_tile("woven_d", GROUP, tag="scalesa")
-        weave(nc.scalar.copy, woven_d, 512, 768)
-        codes_d, scales_d = mx_tiles("d", GROUP)
-        quantise(codes_d, scales_d, woven_d)
-        project(banks[2][:], codes_d, scales_d)
-        drain(1)
-        put(1)
-
         pick_rounded(last, rounded, 768, S)
-        woven_e = woven_tile("woven_e", GROUP)
-        weave(nc.scalar.copy, woven_e, 768, S)
-        codes_e, scales_e = mx_tiles("e", GROUP)
-        quantise(codes_e, scales_e, woven_e)
-        project(banks[3][:], codes_e, scales_e)
-        drain(2)
-        put(2)
+        for g in (2, 3):
+            woven_g = woven_tile(f"woven_late{g}", GROUP, tag="scales0" if g == 2 else None)
+            weave(nc.scalar.copy, woven_g, g * GROUP, (g + 1) * GROUP)
+            quantise(*mx[g], woven_g)
+            project(banks[g][:], *mx[g])
+            drain(g - 1)
+            put(g - 1)
         drain(3)
         put(3)
         nc.sync.dma_start(out, store[:])

@@ -92,11 +92,11 @@ def tile_picked_idxput_add_e_kernel(tc, xT, mem, w1_words, w1_scales, offs, slot
             )
 
         def drain(g):
-            nc.scalar.copy(y[g], banks[g][:])
+            nc.vector.tensor_tensor(y[g], old[:, g * GROUP : (g + 1) * GROUP], banks[g][:], ADD)
 
         def put(g):
             a, b = g * GROUP, (g + 1) * GROUP
-            nc.vector.tensor_tensor(store[:].indirect(entries(slot_sb, a, b)), old[:, a:b], y[g], ADD)
+            nc.vector.tensor_copy(store[:].indirect(entries(slot_sb, a, b)), y[g])
 
         last = PACK - 1
         nc.vector.memset(w_scales[:].bitcast(I32), 0)
@@ -135,18 +135,18 @@ def tile_picked_idxput_add_e_kernel(tc, xT, mem, w1_words, w1_scales, offs, slot
         pick_rounded(last, rounded, 512, 768)
         woven_b = shared[:, base + PACK * S - GROUP :]
         weave(nc.scalar.copy, woven_b, 256, 512)
-        drain(0)
         codes_b, scales_b = mx_tiles("b", GROUP, tag="codes0")
         quantise(codes_b, scales_b, woven_b)
         project(banks[1][:], codes_b, scales_b)
+        drain(0)
         put(0)
         pick_rounded(last, rounded, 768, S)
         for g in (2, 3):
             woven_g = woven_tile(f"woven_late{g}", GROUP, tag="scales0" if g == 2 else None)
             weave(nc.scalar.copy, woven_g, g * GROUP, (g + 1) * GROUP)
+            drain(g - 1)
             quantise(*mx[g], woven_g)
             project(banks[g][:], *mx[g])
-            drain(g - 1)
             put(g - 1)
         drain(3)
         put(3)

@@ -21,7 +21,8 @@ PACK = 4
 LANES = 16
 BLOCK = 128
 GROUP = 256
-LAST_LOADS = [(0, T // 2), (T // 2, T)]
+HALF = 512
+LAST_LOADS = [(0, 768), (768, 1536), (1536, T)]
 EARLY = 1
 EARLY_SHARE = 832
 
@@ -35,7 +36,6 @@ def tile_picked_idxput_add_e_kernel(tc, xT, mem, w1_words, w1_scales, offs, slot
         offs_sb = sb.tile([P, S // LANES], U16, name="offs_sb")
         slot_sb = sb.tile([P, S // LANES], U16, name="slot_sb")
         planes = [sb.tile([P, T], F32, name=f"plane{j}") for j in range(PACK)]
-        rounded_early = sb.tile([P, T], BF16, name="rounded_early", tag="rounded")
         store = sb.tile([P, U], F32, name="store")
         w_codes = sb.tile([P, 2 * N], U8, name="w_codes", align_bytes=64)
         w_scales = sb.tile([P, N], U8, name="w_scales", align_bytes=64)
@@ -43,15 +43,12 @@ def tile_picked_idxput_add_e_kernel(tc, xT, mem, w1_words, w1_scales, offs, slot
         shared = sb.tile([P, base + PACK * S + (PACK - 1) * GROUP], BF16, name="shared", align_bytes=64)
         picked = shared[:, base : base + PACK * S].rearrange("p (j n) -> p j n", j=PACK)
         old = shared[:, : 2 * S].bitcast(F32)
-        y_first = sb.tile([P, GROUP], F32, name="y_first")
+        y_half = sb.tile([P, HALF], F32, name="y_half")
+        y_third = shared[:, base + S + 3 * GROUP : base + 2 * S + GROUP].bitcast(F32)
         y_last = sb.tile([P, GROUP], F32, name="y_last")
-        y = [
-            y_first[:],
-            shared[:, base + S + GROUP : base + S + 3 * GROUP].bitcast(F32),
-            shared[:, base + S + 3 * GROUP : base + 2 * S + GROUP].bitcast(F32),
-            y_last[:],
-        ]
-        banks = [ps.tile([N, GROUP], F32, name=f"bank{g}") for g in range(S // GROUP)]
+        bank_half = ps.tile([N, HALF], F32, name="bank_half")
+        bank_third = ps.tile([N, GROUP], F32, name="bank_third")
+        bank_last = ps.tile([N, GROUP], F32, name="bank_last")
         x_rows = xT.rearrange("(p j) t -> p j t", j=PACK)
 
         def entries(lst, a, b):
@@ -69,12 +66,12 @@ def tile_picked_idxput_add_e_kernel(tc, xT, mem, w1_words, w1_scales, offs, slot
                 picked[:, :, a:b].rearrange("p j (c i) -> p c j i", i=4),
             )
 
-        def woven_tile(name, n, tag=None):
-            return sb.tile([P, n * PACK], BF16, name=name, tag=tag or name, align_bytes=64)[:]
+        def woven_tile(name, n):
+            return sb.tile([P, n * PACK], BF16, name=name, align_bytes=64)[:]
 
-        def mx_tiles(name, n, tag=None):
-            codes = sb.tile([P, n], U32, name=f"codes{name}", tag=tag or f"codes{name}", align_bytes=64)
-            scales = sb.tile([P, n], U8, name=f"scales{name}", tag=f"scales{name}", align_bytes=64)
+        def mx_tiles(name, n, tag):
+            codes = sb.tile([P, n], U32, name=f"codes_{name}", tag=tag, align_bytes=64)
+            scales = sb.tile([P, n], U8, name=f"scales_{name}", align_bytes=64)
             return codes[:], scales[:]
 
         def quantise(codes, scales, woven):
@@ -82,7 +79,7 @@ def tile_picked_idxput_add_e_kernel(tc, xT, mem, w1_words, w1_scales, offs, slot
 
         def project(bank, codes, scales):
             nc.tensor.matmul_mx(
-                out=bank,
+                out=bank[:],
                 lhsT=w_codes[:].bitcast(FP4X4),
                 lhsT_scale=w_scales[:],
                 rhs=codes.bitcast(FP8X4),
@@ -91,12 +88,8 @@ def tile_picked_idxput_add_e_kernel(tc, xT, mem, w1_words, w1_scales, offs, slot
                 stop=True,
             )
 
-        def drain(g):
-            nc.vector.tensor_tensor(y[g], old[:, g * GROUP : (g + 1) * GROUP], banks[g][:], ADD)
-
-        def put(g):
-            a, b = g * GROUP, (g + 1) * GROUP
-            nc.vector.tensor_copy(store[:].indirect(entries(slot_sb, a, b)), y[g])
+        def put(a, b, y):
+            nc.vector.tensor_tensor(store[:].indirect(entries(slot_sb, a, b)), old[:, a:b], y, ADD)
 
         last = PACK - 1
         nc.vector.memset(w_scales[:].bitcast(I32), 0)
@@ -112,42 +105,45 @@ def tile_picked_idxput_add_e_kernel(tc, xT, mem, w1_words, w1_scales, offs, slot
         for q in range(4):
             nc.sync.dma_start(w_scales[32 * q : 32 * q + 4, :].bitcast(I32), w1_scales[0, 4 * q : 4 * q + 4, :].bitcast(I32))
 
+        rounded_early = sb.tile([P, T], BF16, name="rounded_early", tag="rounded")
         nc.scalar.copy(rounded_early[:], planes[EARLY][:])
         pick_rounded(EARLY, rounded_early, EARLY_SHARE, S)
         rounded = sb.tile([P, T], BF16, name="rounded", tag="rounded")
-        nc.scalar.copy(rounded[:, : T // 2], planes[last][:, : T // 2])
+        for a, b in LAST_LOADS:
+            nc.scalar.copy(rounded[:, a:b], planes[last][:, a:b])
         for j in range(last):
             pick(j, 0, EARLY_SHARE if j == EARLY else S)
-        pick(last, 0, 128)
-        pick(last, 128, 256)
+        pick(last, 0, BLOCK)
+        pick(last, GROUP, HALF)
+        pick(last, BLOCK, GROUP)
 
-        nc.scalar.copy(rounded[:, T // 2 :], planes[last][:, T // 2 :])
-        woven = [woven_tile(f"woven{c}", BLOCK) for c in range(2)]
-        weave(nc.vector.tensor_copy, woven[0], 0, 128)
-        pick(last, 256, 384)
-        weave(nc.scalar.copy, woven[1], 128, 256)
-        mx = {g: mx_tiles(g, GROUP) for g in (0, 2, 3)}
-        for c in range(2):
-            quantise(mx[0][0][:, c * BLOCK : (c + 1) * BLOCK], mx[0][1][:, c * BLOCK : (c + 1) * BLOCK], woven[c])
-        project(banks[0][:], *mx[0])
+        codes, scales = mx_tiles("half", HALF, "codes")
+        cuts = [(0, BLOCK, nc.scalar.copy), (GROUP, HALF, nc.vector.tensor_copy), (BLOCK, GROUP, nc.scalar.copy)]
+        woven = [woven_tile(f"woven{a}", b - a) for a, b, copy in cuts]
+        for (a, b, copy), tile in zip(cuts, woven):
+            weave(copy, tile, a, b)
+        for (a, b, copy), tile in zip(cuts, woven):
+            quantise(codes[:, a:b], scales[:, a:b], tile)
+        project(bank_half, codes, scales)
         nc.vector.tensor_copy(old, store[:].indirect(slot_sb[:]))
-        pick_rounded(last, rounded, 384, 512)
-        pick_rounded(last, rounded, 512, 768)
-        woven_b = shared[:, base + PACK * S - GROUP :]
-        weave(nc.scalar.copy, woven_b, 256, 512)
-        codes_b, scales_b = mx_tiles("b", GROUP, tag="codes0")
-        quantise(codes_b, scales_b, woven_b)
-        project(banks[1][:], codes_b, scales_b)
-        drain(0)
-        put(0)
-        pick_rounded(last, rounded, 768, S)
-        for g in (2, 3):
-            woven_g = woven_tile(f"woven_late{g}", GROUP, tag="scales0" if g == 2 else None)
-            weave(nc.scalar.copy, woven_g, g * GROUP, (g + 1) * GROUP)
-            drain(g - 1)
-            quantise(*mx[g], woven_g)
-            project(banks[g][:], *mx[g])
-            put(g - 1)
-        drain(3)
-        put(3)
+
+        woven_third = shared[:, base + PACK * S - GROUP :]
+        pick_rounded(last, rounded, HALF, HALF + GROUP)
+        weave(nc.scalar.copy, woven_third, HALF, HALF + GROUP)
+        nc.scalar.copy(y_half[:], bank_half[:])
+        codes, scales = mx_tiles("third", GROUP, "codes")
+        quantise(codes, scales, woven_third)
+        project(bank_third, codes, scales)
+        put(0, HALF, y_half[:])
+
+        woven_last = woven_tile("woven_last", GROUP)
+        pick_rounded(last, rounded, HALF + GROUP, S)
+        weave(nc.scalar.copy, woven_last, HALF + GROUP, S)
+        codes, scales = mx_tiles("last", GROUP, "codes_last")
+        quantise(codes, scales, woven_last)
+        project(bank_last, codes, scales)
+        nc.scalar.copy(y_third, bank_third[:])
+        put(HALF, HALF + GROUP, y_third)
+        nc.scalar.copy(y_last[:], bank_last[:])
+        put(HALF + GROUP, S, y_last[:])
         nc.sync.dma_start(out, store[:])

@@ -25,6 +25,8 @@ HALF = 512
 LAST_LOADS = [(0, 768), (768, 1536), (1536, T)]
 EARLY = 1
 EARLY_SHARE = 832
+AHEAD = 384
+SHARE = 448
 
 
 def tile_picked_idxput_add_e_kernel(tc, xT, mem, w1_words, w1_scales, offs, slot, out):
@@ -40,15 +42,15 @@ def tile_picked_idxput_add_e_kernel(tc, xT, mem, w1_words, w1_scales, offs, slot
         w_codes = sb.tile([P, 2 * N], U8, name="w_codes", align_bytes=64)
         w_scales = sb.tile([P, N], U8, name="w_scales", align_bytes=64)
         base = 2 * S - GROUP
-        shared = sb.tile([P, base + PACK * S + (PACK - 1) * GROUP], BF16, name="shared", align_bytes=64)
+        shared = sb.tile([P, base + PACK * S], BF16, name="shared", align_bytes=64)
         picked = shared[:, base : base + PACK * S].rearrange("p (j n) -> p j n", j=PACK)
         old = shared[:, : 2 * S].bitcast(F32)
-        y_half = sb.tile([P, HALF], F32, name="y_half")
-        y_third = shared[:, base + S + 3 * GROUP : base + 2 * S + GROUP].bitcast(F32)
-        y_last = sb.tile([P, GROUP], F32, name="y_last")
-        bank_half = ps.tile([N, HALF], F32, name="bank_half")
-        bank_third = ps.tile([N, GROUP], F32, name="bank_third")
-        bank_last = ps.tile([N, GROUP], F32, name="bank_last")
+        y_first = sb.tile([P, GROUP], F32, name="y_first")
+        y_second = shared[:, base + S + HALF : base + 2 * S].bitcast(F32)
+        y_rest = sb.tile([P, HALF], F32, name="y_rest")
+        bank_first = ps.tile([N, GROUP], F32, name="bank_first")
+        bank_second = ps.tile([N, GROUP], F32, name="bank_second")
+        bank_rest = ps.tile([N, HALF], F32, name="bank_rest")
         x_rows = xT.rearrange("(p j) t -> p j t", j=PACK)
 
         def entries(lst, a, b):
@@ -71,7 +73,7 @@ def tile_picked_idxput_add_e_kernel(tc, xT, mem, w1_words, w1_scales, offs, slot
 
         def mx_tiles(name, n, tag):
             codes = sb.tile([P, n], U32, name=f"codes_{name}", tag=tag, align_bytes=64)
-            scales = sb.tile([P, n], U8, name=f"scales_{name}", align_bytes=64)
+            scales = sb.tile([P, n], U8, name=f"scales_{name}", tag=f"scales_{name}", align_bytes=64)
             return codes[:], scales[:]
 
         def quantise(codes, scales, woven):
@@ -113,37 +115,34 @@ def tile_picked_idxput_add_e_kernel(tc, xT, mem, w1_words, w1_scales, offs, slot
             nc.scalar.copy(rounded[:, a:b], planes[last][:, a:b])
         for j in range(last):
             pick(j, 0, EARLY_SHARE if j == EARLY else S)
-        pick(last, 0, BLOCK)
-        pick(last, GROUP, HALF)
-        pick(last, BLOCK, GROUP)
+        pick(last, 0, GROUP)
+        pick(last, GROUP, AHEAD)
 
-        codes, scales = mx_tiles("half", HALF, "codes")
-        cuts = [(0, BLOCK, nc.scalar.copy), (GROUP, HALF, nc.vector.tensor_copy), (BLOCK, GROUP, nc.scalar.copy)]
-        woven = [woven_tile(f"woven{a}", b - a) for a, b, copy in cuts]
-        for (a, b, copy), tile in zip(cuts, woven):
-            weave(copy, tile, a, b)
-        for (a, b, copy), tile in zip(cuts, woven):
-            quantise(codes[:, a:b], scales[:, a:b], tile)
-        project(bank_half, codes, scales)
+        woven = woven_tile("woven_first", GROUP)
+        weave(nc.vector.tensor_copy, woven, 0, GROUP)
+        pick(last, AHEAD, SHARE)
+        codes, scales = mx_tiles("first", GROUP, "codes")
+        quantise(codes, scales, woven)
+        project(bank_first, codes, scales)
         nc.vector.tensor_copy(old, store[:].indirect(slot_sb[:]))
 
-        woven_third = shared[:, base + PACK * S - GROUP :]
-        pick_rounded(last, rounded, HALF, HALF + GROUP)
-        weave(nc.scalar.copy, woven_third, HALF, HALF + GROUP)
-        nc.scalar.copy(y_half[:], bank_half[:])
-        codes, scales = mx_tiles("third", GROUP, "codes")
-        quantise(codes, scales, woven_third)
-        project(bank_third, codes, scales)
-        put(0, HALF, y_half[:])
+        pick_rounded(last, rounded, SHARE, HALF + BLOCK)
+        pick_rounded(last, rounded, HALF + BLOCK, S)
+        woven = woven_tile("woven_second", GROUP)
+        weave(nc.scalar.copy, woven, GROUP, HALF)
+        nc.scalar.copy(y_first[:], bank_first[:])
+        codes, scales = mx_tiles("second", GROUP, "codes")
+        quantise(codes, scales, woven)
+        project(bank_second, codes, scales)
+        put(0, GROUP, y_first[:])
 
-        woven_last = woven_tile("woven_last", GROUP)
-        pick_rounded(last, rounded, HALF + GROUP, S)
-        weave(nc.scalar.copy, woven_last, HALF + GROUP, S)
-        codes, scales = mx_tiles("last", GROUP, "codes_last")
-        quantise(codes, scales, woven_last)
-        project(bank_last, codes, scales)
-        nc.scalar.copy(y_third, bank_third[:])
-        put(HALF, HALF + GROUP, y_third)
-        nc.scalar.copy(y_last[:], bank_last[:])
-        put(HALF + GROUP, S, y_last[:])
+        woven = sb.tile([P, HALF * PACK], BF16, name="woven_rest", tag="scales_first", align_bytes=64)[:]
+        weave(nc.scalar.copy, woven, HALF, S)
+        codes, scales = mx_tiles("rest", HALF, "codes_rest")
+        quantise(codes, scales, woven)
+        project(bank_rest, codes, scales)
+        nc.scalar.copy(y_second, bank_second[:])
+        put(GROUP, HALF, y_second)
+        nc.scalar.copy(y_rest[:], bank_rest[:])
+        put(HALF, S, y_rest[:])
         nc.sync.dma_start(out, store[:])

@@ -22,10 +22,11 @@ LANES = 16
 BLOCK = 128
 GROUP = 256
 HALF = 512
-LAST_LOADS = [(0, 768), (768, 1536), (1536, T)]
+LAST_LOADS = [(0, T // 2), (T // 2, T)]
 EARLY = 1
 EARLY_SHARE = 832
 AHEAD = 384
+SCALAR_WEAVES = 64
 SHARE = 448
 
 
@@ -50,7 +51,7 @@ def tile_picked_idxput_add_e_kernel(tc, xT, mem, w1_words, w1_scales, offs, slot
         y_rest = sb.tile([P, HALF], F32, name="y_rest")
         bank_first = ps.tile([N, GROUP], F32, name="bank_first")
         bank_second = ps.tile([N, GROUP], F32, name="bank_second")
-        bank_rest = ps.tile([N, HALF], F32, name="bank_rest")
+        banks_rest = [ps.tile([N, GROUP], F32, name=f"bank_rest{h}") for h in range(2)]
         x_rows = xT.rearrange("(p j) t -> p j t", j=PACK)
 
         def entries(lst, a, b):
@@ -119,7 +120,8 @@ def tile_picked_idxput_add_e_kernel(tc, xT, mem, w1_words, w1_scales, offs, slot
         pick(last, GROUP, AHEAD)
 
         woven = woven_tile("woven_first", GROUP)
-        weave(nc.vector.tensor_copy, woven, 0, GROUP)
+        weave(nc.scalar.copy, woven[:, : PACK * SCALAR_WEAVES], 0, SCALAR_WEAVES)
+        weave(nc.vector.tensor_copy, woven[:, PACK * SCALAR_WEAVES :], SCALAR_WEAVES, GROUP)
         pick(last, AHEAD, SHARE)
         codes, scales = mx_tiles("first", GROUP, "codes")
         quantise(codes, scales, woven)
@@ -140,9 +142,11 @@ def tile_picked_idxput_add_e_kernel(tc, xT, mem, w1_words, w1_scales, offs, slot
         weave(nc.scalar.copy, woven, HALF, S)
         codes, scales = mx_tiles("rest", HALF, "codes_rest")
         quantise(codes, scales, woven)
-        project(bank_rest, codes, scales)
+        for h in range(2):
+            project(banks_rest[h], codes[:, h * GROUP : (h + 1) * GROUP], scales[:, h * GROUP : (h + 1) * GROUP])
         nc.scalar.copy(y_second, bank_second[:])
         put(GROUP, HALF, y_second)
-        nc.scalar.copy(y_rest[:], bank_rest[:])
+        for h in range(2):
+            nc.scalar.copy(y_rest[:, h * GROUP : (h + 1) * GROUP], banks_rest[h][:])
         put(HALF, S, y_rest[:])
         nc.sync.dma_start(out, store[:])

@@ -109,7 +109,7 @@ def tile_picked_idxput_add_e_kernel(tc, xT, mem, w1_words, w1_scales, offs, slot
             nc.sync.dma_start(w_scales[32 * q : 32 * q + 4, :].bitcast(I32), w1_scales[0, 4 * q : 4 * q + 4, :].bitcast(I32))
 
         rounded_early = sb.tile([P, T], BF16, name="rounded_early", tag="rounded")
-        nc.scalar.copy(rounded_early[:], planes[EARLY][:])
+        nc.gpsimd.tensor_copy(rounded_early[:], planes[EARLY][:])
         pick_rounded(EARLY, rounded_early, EARLY_SHARE, S)
         rounded = sb.tile([P, T], BF16, name="rounded", tag="rounded")
         for a, b in LAST_LOADS:

@@ -25,9 +25,10 @@ HALF = 512
 LAST_LOADS = [(0, T // 2), (T // 2, T)]
 EARLY = 1
 EARLY_SHARE = 832
-AHEAD = 384
-SCALAR_WEAVES = 64
-SHARE = 448
+AHEAD = 320
+SHARE = 384
+SCALAR_FIRST = 768
+SCALAR_ROUNDS = 1536
 
 
 def tile_picked_idxput_add_e_kernel(tc, xT, mem, w1_words, w1_scales, offs, slot, out):
@@ -46,12 +47,9 @@ def tile_picked_idxput_add_e_kernel(tc, xT, mem, w1_words, w1_scales, offs, slot
         shared = sb.tile([P, base + PACK * S], BF16, name="shared", align_bytes=64)
         picked = shared[:, base : base + PACK * S].rearrange("p (j n) -> p j n", j=PACK)
         old = shared[:, : 2 * S].bitcast(F32)
-        y_first = sb.tile([P, GROUP], F32, name="y_first")
-        y_second = shared[:, base + S + HALF : base + 2 * S].bitcast(F32)
-        y_rest = sb.tile([P, HALF], F32, name="y_rest")
-        bank_first = ps.tile([N, GROUP], F32, name="bank_first")
-        bank_second = ps.tile([N, GROUP], F32, name="bank_second")
-        banks_rest = [ps.tile([N, GROUP], F32, name=f"bank_rest{h}") for h in range(2)]
+        y_first = shared[:, base + S + 3 * GROUP : base + 2 * S + GROUP].bitcast(F32)
+        y_rest = sb.tile([P, S - GROUP], F32, name="y_rest")
+        banks = [ps.tile([N, GROUP], F32, name=f"bank{g}") for g in range(S // GROUP)]
         x_rows = xT.rearrange("(p j) t -> p j t", j=PACK)
 
         def entries(lst, a, b):
@@ -112,41 +110,40 @@ def tile_picked_idxput_add_e_kernel(tc, xT, mem, w1_words, w1_scales, offs, slot
         nc.gpsimd.tensor_copy(rounded_early[:], planes[EARLY][:])
         pick_rounded(EARLY, rounded_early, EARLY_SHARE, S)
         rounded = sb.tile([P, T], BF16, name="rounded", tag="rounded")
-        for a, b in LAST_LOADS:
-            nc.scalar.copy(rounded[:, a:b], planes[last][:, a:b])
+        nc.scalar.copy(rounded[:, : T // 2], planes[last][:, : T // 2])
+        nc.scalar.copy(rounded[:, T // 2 : SCALAR_ROUNDS], planes[last][:, T // 2 : SCALAR_ROUNDS])
+        nc.gpsimd.tensor_copy(rounded[:, SCALAR_ROUNDS:], planes[last][:, SCALAR_ROUNDS:])
         for j in range(last):
             pick(j, 0, EARLY_SHARE if j == EARLY else S)
         pick(last, 0, GROUP)
         pick(last, GROUP, AHEAD)
 
-        woven = woven_tile("woven_first", GROUP)
-        weave(nc.scalar.copy, woven[:, : PACK * SCALAR_WEAVES], 0, SCALAR_WEAVES)
-        weave(nc.vector.tensor_copy, woven[:, PACK * SCALAR_WEAVES :], SCALAR_WEAVES, GROUP)
+        woven_middle = woven_tile("woven_middle", HALF)
+        woven_first = woven_middle[:, PACK * GROUP :]
+        weave(nc.vector.tensor_copy, woven_first, 0, GROUP)
         pick(last, AHEAD, SHARE)
-        codes, scales = mx_tiles("first", GROUP, "codes")
-        quantise(codes, scales, woven)
-        project(bank_first, codes, scales)
+        codes, scales = mx_tiles("first", GROUP, "codes_first")
+        quantise(codes, scales, woven_first)
+        project(banks[0], codes, scales)
         nc.vector.tensor_copy(old, store[:].indirect(slot_sb[:]))
 
-        pick_rounded(last, rounded, SHARE, HALF + BLOCK)
-        pick_rounded(last, rounded, HALF + BLOCK, S)
-        woven = woven_tile("woven_second", GROUP)
-        weave(nc.scalar.copy, woven, GROUP, HALF)
-        nc.scalar.copy(y_first[:], bank_first[:])
-        codes, scales = mx_tiles("second", GROUP, "codes")
-        quantise(codes, scales, woven)
-        project(bank_second, codes, scales)
-        put(0, GROUP, y_first[:])
-
-        woven = sb.tile([P, HALF * PACK], BF16, name="woven_rest", tag="scales_first", align_bytes=64)[:]
-        weave(nc.scalar.copy, woven, HALF, S)
-        codes, scales = mx_tiles("rest", HALF, "codes_rest")
-        quantise(codes, scales, woven)
-        for h in range(2):
-            project(banks_rest[h], codes[:, h * GROUP : (h + 1) * GROUP], scales[:, h * GROUP : (h + 1) * GROUP])
-        nc.scalar.copy(y_second, bank_second[:])
-        put(GROUP, HALF, y_second)
-        for h in range(2):
-            nc.scalar.copy(y_rest[:, h * GROUP : (h + 1) * GROUP], banks_rest[h][:])
-        put(HALF, S, y_rest[:])
+        pick_rounded(last, rounded, SHARE, SCALAR_FIRST)
+        pick_rounded(last, rounded, SCALAR_FIRST, S)
+        weave(nc.scalar.copy, woven_middle[:, : PACK * GROUP], GROUP, HALF)
+        nc.gpsimd.tensor_copy(
+            woven_middle[:, PACK * GROUP :].rearrange("p (n j) -> p n j", j=PACK),
+            picked[:, :, HALF : HALF + GROUP].rearrange("p j n -> p n j"),
+        )
+        woven_last = woven_tile("woven_last", GROUP)
+        weave(nc.scalar.copy, woven_last, HALF + GROUP, S)
+        codes, scales = mx_tiles("rest", S - GROUP, "codes_first")
+        quantise(codes[:, :HALF], scales[:, :HALF], woven_middle)
+        quantise(codes[:, HALF:], scales[:, HALF:], woven_last)
+        for g in range(1, S // GROUP):
+            project(banks[g], codes[:, (g - 1) * GROUP : g * GROUP], scales[:, (g - 1) * GROUP : g * GROUP])
+        nc.scalar.copy(y_first, banks[0][:])
+        put(0, GROUP, y_first)
+        for g in range(1, S // GROUP):
+            nc.scalar.copy(y_rest[:, (g - 1) * GROUP : g * GROUP], banks[g][:])
+        put(GROUP, S, y_rest[:])
         nc.sync.dma_start(out, store[:])

@@ -22,13 +22,13 @@ LANES = 16
 BLOCK = 128
 GROUP = 256
 HALF = 512
-LAST_LOADS = [(0, T // 2), (T // 2, T)]
+LAST_LOADS = [(0, 1024), (1024, 1536), (1536, T)]
 EARLY = 1
 EARLY_SHARE = 832
-AHEAD = 320
-SHARE = 384
+AHEAD = 384
+SHARE = 448
 SCALAR_FIRST = 768
-SCALAR_ROUNDS = 1536
+SCALAR_ROUNDS = 1792
 
 
 def tile_picked_idxput_add_e_kernel(tc, xT, mem, w1_words, w1_scales, offs, slot, out):
@@ -111,7 +111,8 @@ def tile_picked_idxput_add_e_kernel(tc, xT, mem, w1_words, w1_scales, offs, slot
         pick_rounded(EARLY, rounded_early, EARLY_SHARE, S)
         rounded = sb.tile([P, T], BF16, name="rounded", tag="rounded")
         nc.scalar.copy(rounded[:, : T // 2], planes[last][:, : T // 2])
-        nc.scalar.copy(rounded[:, T // 2 : SCALAR_ROUNDS], planes[last][:, T // 2 : SCALAR_ROUNDS])
+        nc.gpsimd.tensor_copy(rounded[:, 1024:1536], planes[last][:, 1024:1536])
+        nc.scalar.copy(rounded[:, 1536:SCALAR_ROUNDS], planes[last][:, 1536:SCALAR_ROUNDS])
         nc.gpsimd.tensor_copy(rounded[:, SCALAR_ROUNDS:], planes[last][:, SCALAR_ROUNDS:])
         for j in range(last):
             pick(j, 0, EARLY_SHARE if j == EARLY else S)

@@ -29,6 +29,7 @@ AHEAD = 384
 SHARE = 448
 SCALAR_FIRST = 768
 SCALAR_ROUNDS = 1792
+GPSIMD_WEAVES = 192
 
 
 def tile_picked_idxput_add_e_kernel(tc, xT, mem, w1_words, w1_scales, offs, slot, out):
@@ -119,8 +120,10 @@ def tile_picked_idxput_add_e_kernel(tc, xT, mem, w1_words, w1_scales, offs, slot
         pick(last, 0, GROUP)
         pick(last, GROUP, AHEAD)
 
-        woven_middle = woven_tile("woven_middle", HALF)
-        woven_first = woven_middle[:, PACK * GROUP :]
+        cut = HALF + GROUP - GPSIMD_WEAVES
+        woven = woven_tile("woven", cut)
+        woven_middle = woven[:, : PACK * HALF]
+        woven_first = woven[:, PACK * (cut - GROUP) :]
         weave(nc.vector.tensor_copy, woven_first, 0, GROUP)
         pick(last, AHEAD, SHARE)
         codes, scales = mx_tiles("first", GROUP, "codes_first")
@@ -130,18 +133,19 @@ def tile_picked_idxput_add_e_kernel(tc, xT, mem, w1_words, w1_scales, offs, slot
 
         pick_rounded(last, rounded, SHARE, SCALAR_FIRST)
         pick_rounded(last, rounded, SCALAR_FIRST, S)
-        weave(nc.scalar.copy, woven_middle[:, : PACK * GROUP], GROUP, HALF)
+        weave(nc.scalar.copy, woven_middle[:, : PACK * (cut - GROUP)], GROUP, cut)
         nc.gpsimd.tensor_copy(
-            woven_middle[:, PACK * GROUP :].rearrange("p (n j) -> p n j", j=PACK),
-            picked[:, :, HALF : HALF + GROUP].rearrange("p j n -> p n j"),
+            woven_middle[:, PACK * (cut - GROUP) :].rearrange("p (n j) -> p n j", j=PACK),
+            picked[:, :, cut : HALF + GROUP].rearrange("p j n -> p n j"),
         )
         woven_last = woven_tile("woven_last", GROUP)
         weave(nc.scalar.copy, woven_last, HALF + GROUP, S)
         codes, scales = mx_tiles("rest", S - GROUP, "codes_first")
-        quantise(codes[:, :HALF], scales[:, :HALF], woven_middle)
-        quantise(codes[:, HALF:], scales[:, HALF:], woven_last)
+        late = [woven_middle[:, : PACK * GROUP], woven_middle[:, PACK * GROUP :], woven_last]
         for g in range(1, S // GROUP):
-            project(banks[g], codes[:, (g - 1) * GROUP : g * GROUP], scales[:, (g - 1) * GROUP : g * GROUP])
+            cols = slice((g - 1) * GROUP, g * GROUP)
+            quantise(codes[:, cols], scales[:, cols], late[g - 1])
+            project(banks[g], codes[:, cols], scales[:, cols])
         nc.scalar.copy(y_first, banks[0][:])
         put(0, GROUP, y_first)
         for g in range(1, S // GROUP):

@@ -22,13 +22,13 @@ LANES = 16
 BLOCK = 128
 GROUP = 256
 HALF = 512
-LAST_LOADS = [(0, 1024), (1024, 1536), (1536, T)]
+LAST_LOADS = [(0, T // 2), (T // 2, T)]
 EARLY = 1
 EARLY_SHARE = 832
-AHEAD = 384
-SHARE = 448
+AHEAD = 320
+SHARE = 384
 SCALAR_FIRST = 768
-SCALAR_ROUNDS = 1792
+SCALAR_ROUNDS = 1536
 GPSIMD_WEAVES = 192
 
 
@@ -48,7 +48,7 @@ def tile_picked_idxput_add_e_kernel(tc, xT, mem, w1_words, w1_scales, offs, slot
         shared = sb.tile([P, base + PACK * S], BF16, name="shared", align_bytes=64)
         picked = shared[:, base : base + PACK * S].rearrange("p (j n) -> p j n", j=PACK)
         old = shared[:, : 2 * S].bitcast(F32)
-        y_first = shared[:, base + S + 3 * GROUP : base + 2 * S + GROUP].bitcast(F32)
+        y_first = shared[:, base + 2 * S + 3 * GROUP : base + 3 * S + GROUP].bitcast(F32)
         y_rest = sb.tile([P, S - GROUP], F32, name="y_rest")
         banks = [ps.tile([N, GROUP], F32, name=f"bank{g}") for g in range(S // GROUP)]
         x_rows = xT.rearrange("(p j) t -> p j t", j=PACK)
@@ -62,10 +62,10 @@ def tile_picked_idxput_add_e_kernel(tc, xT, mem, w1_words, w1_scales, offs, slot
         def pick_rounded(j, window, a, b):
             nc.scalar.activation(picked[:, j, a:b], window[:].indirect(entries(offs_sb, a, b)), COPY)
 
-        def weave(copy, woven, a, b):
+        def weave(copy, woven, a, b, lanes=slice(0, PACK)):
             copy(
-                woven.rearrange("p (c i j) -> p c j i", i=4, j=PACK),
-                picked[:, :, a:b].rearrange("p j (c i) -> p c j i", i=4),
+                woven.rearrange("p (c i j) -> p c j i", i=4, j=PACK)[:, :, lanes, :],
+                picked[:, lanes, a:b].rearrange("p j (c i) -> p c j i", i=4),
             )
 
         def woven_tile(name, n):
@@ -107,23 +107,29 @@ def tile_picked_idxput_add_e_kernel(tc, xT, mem, w1_words, w1_scales, offs, slot
         for q in range(4):
             nc.sync.dma_start(w_scales[32 * q : 32 * q + 4, :].bitcast(I32), w1_scales[0, 4 * q : 4 * q + 4, :].bitcast(I32))
 
-        rounded_early = sb.tile([P, T], BF16, name="rounded_early", tag="rounded")
-        nc.gpsimd.tensor_copy(rounded_early[:], planes[EARLY][:])
+        rounded_early = sb.tile([P, T], BF16, name="rounded_early")
+        nc.scalar.copy(rounded_early[:, : T // 2], planes[EARLY][:, : T // 2])
+        nc.gpsimd.tensor_copy(rounded_early[:, T // 2 :], planes[EARLY][:, T // 2 :])
         pick_rounded(EARLY, rounded_early, EARLY_SHARE, S)
-        rounded = sb.tile([P, T], BF16, name="rounded", tag="rounded")
-        nc.scalar.copy(rounded[:, : T // 2], planes[last][:, : T // 2])
-        nc.gpsimd.tensor_copy(rounded[:, 1024:1536], planes[last][:, 1024:1536])
-        nc.scalar.copy(rounded[:, 1536:SCALAR_ROUNDS], planes[last][:, 1536:SCALAR_ROUNDS])
-        nc.gpsimd.tensor_copy(rounded[:, SCALAR_ROUNDS:], planes[last][:, SCALAR_ROUNDS:])
         for j in range(last):
             pick(j, 0, EARLY_SHARE if j == EARLY else S)
+
+        cut = GROUP + GPSIMD_WEAVES
+        woven = woven_tile("woven", S - GPSIMD_WEAVES)
+        woven_first = woven[:, : PACK * GROUP]
+        woven_rest = woven[:, PACK * (GROUP - GPSIMD_WEAVES) :]
+
+        def rest(a, b):
+            return woven_rest[:, PACK * (a - GROUP) : PACK * (b - GROUP)]
+
+        weave(nc.scalar.copy, rest(cut, S), cut, S, slice(0, 2))
+        rounded = sb.tile([P, T], BF16, name="rounded")
+        nc.gpsimd.tensor_copy(rounded[:, : T // 2], planes[last][:, : T // 2])
+        nc.scalar.copy(rounded[:, T // 2 : SCALAR_ROUNDS], planes[last][:, T // 2 : SCALAR_ROUNDS])
+        nc.gpsimd.tensor_copy(rounded[:, SCALAR_ROUNDS:], planes[last][:, SCALAR_ROUNDS:])
         pick(last, 0, GROUP)
         pick(last, GROUP, AHEAD)
 
-        cut = HALF + GROUP - GPSIMD_WEAVES
-        woven = woven_tile("woven", cut)
-        woven_middle = woven[:, : PACK * HALF]
-        woven_first = woven[:, PACK * (cut - GROUP) :]
         weave(nc.vector.tensor_copy, woven_first, 0, GROUP)
         pick(last, AHEAD, SHARE)
         codes, scales = mx_tiles("first", GROUP, "codes_first")
@@ -133,18 +139,16 @@ def tile_picked_idxput_add_e_kernel(tc, xT, mem, w1_words, w1_scales, offs, slot
 
         pick_rounded(last, rounded, SHARE, SCALAR_FIRST)
         pick_rounded(last, rounded, SCALAR_FIRST, S)
-        weave(nc.scalar.copy, woven_middle[:, : PACK * (cut - GROUP)], GROUP, cut)
         nc.gpsimd.tensor_copy(
-            woven_middle[:, PACK * (cut - GROUP) :].rearrange("p (n j) -> p n j", j=PACK),
-            picked[:, :, cut : HALF + GROUP].rearrange("p j n -> p n j"),
+            rest(GROUP, cut).rearrange("p (n j) -> p n j", j=PACK),
+            picked[:, :, GROUP:cut].rearrange("p j n -> p n j"),
         )
-        woven_last = woven_tile("woven_last", GROUP)
-        weave(nc.scalar.copy, woven_last, HALF + GROUP, S)
+        weave(nc.scalar.copy, rest(cut, SCALAR_FIRST), cut, SCALAR_FIRST, slice(2, 4))
+        weave(nc.scalar.copy, rest(SCALAR_FIRST, S), SCALAR_FIRST, S, slice(2, 4))
         codes, scales = mx_tiles("rest", S - GROUP, "codes_first")
-        late = [woven_middle[:, : PACK * GROUP], woven_middle[:, PACK * GROUP :], woven_last]
         for g in range(1, S // GROUP):
             cols = slice((g - 1) * GROUP, g * GROUP)
-            quantise(codes[:, cols], scales[:, cols], late[g - 1])
+            quantise(codes[:, cols], scales[:, cols], rest(g * GROUP, (g + 1) * GROUP))
             project(banks[g], codes[:, cols], scales[:, cols])
         nc.scalar.copy(y_first, banks[0][:])
         put(0, GROUP, y_first)

@@ -19,17 +19,11 @@ COPY = mybir.ActivationFunctionType.Copy
 P = 128
 PACK = 4
 LANES = 16
-BLOCK = 128
 GROUP = 256
-HALF = 512
-LAST_LOADS = [(0, T // 2), (T // 2, T)]
-EARLY = 1
-EARLY_SHARE = 832
-AHEAD = 320
-SHARE = 384
-SCALAR_FIRST = 768
-SCALAR_ROUNDS = 1536
-GPSIMD_WEAVES = 192
+ORDER = [2, 0, 1, 3]
+SECOND_SHARE = 640
+LAST_LOADS = [(0, 1280), (1280, T)]
+SCALAR_ROUNDS = [704, 416]
 
 
 def tile_picked_idxput_add_e_kernel(tc, xT, mem, w1_words, w1_scales, offs, slot, out):
@@ -38,66 +32,69 @@ def tile_picked_idxput_add_e_kernel(tc, xT, mem, w1_words, w1_scales, offs, slot
         sb = ctx.enter_context(tc.tile_pool(name="sb", bufs=1))
         ps = ctx.enter_context(tc.psum_pool(name="ps", bufs=1))
 
+        g1, g2, g3 = GROUP, 2 * GROUP, 3 * GROUP
         offs_sb = sb.tile([P, S // LANES], U16, name="offs_sb")
         slot_sb = sb.tile([P, S // LANES], U16, name="slot_sb")
         planes = [sb.tile([P, T], F32, name=f"plane{j}") for j in range(PACK)]
+        rounded = sb.tile([P, T], BF16, name="rounded")
         store = sb.tile([P, U], F32, name="store")
         w_codes = sb.tile([P, 2 * N], U8, name="w_codes", align_bytes=64)
         w_scales = sb.tile([P, N], U8, name="w_scales", align_bytes=64)
-        base = 2 * S - GROUP
+        picked = sb.tile([P, PACK * (S - g2)], BF16, name="picked")[:].rearrange("p (j n) -> p j n", j=PACK)
+        base = 2 * S - PACK * (GROUP + GROUP // 2)
         shared = sb.tile([P, base + PACK * S], BF16, name="shared", align_bytes=64)
-        picked = shared[:, base : base + PACK * S].rearrange("p (j n) -> p j n", j=PACK)
+        woven = shared[:, base:]
         old = shared[:, : 2 * S].bitcast(F32)
-        y_first = shared[:, base + 2 * S + 3 * GROUP : base + 3 * S + GROUP].bitcast(F32)
-        y_rest = sb.tile([P, S - GROUP], F32, name="y_rest")
+        lanes = woven.rearrange("p (n j) -> p n j", j=PACK)
+        codes = sb.tile([P, 2 * GROUP], U32, name="codes", align_bytes=64)
+        scales = sb.tile([P, S], U8, name="scales", align_bytes=64)
+        y = sb.tile([P, S], F32, name="y")
         banks = [ps.tile([N, GROUP], F32, name=f"bank{g}") for g in range(S // GROUP)]
         x_rows = xT.rearrange("(p j) t -> p j t", j=PACK)
 
         def entries(lst, a, b):
             return lst[:, a // LANES : b // LANES]
 
+        def place(j, a, b):
+            return lanes[:, a:b, j] if b <= g2 else picked[:, j, a - g2 : b - g2]
+
         def pick(j, a, b):
-            nc.vector.tensor_copy(picked[:, j, a:b], planes[j][:].indirect(entries(offs_sb, a, b)))
+            nc.vector.tensor_copy(place(j, a, b), planes[j][:].indirect(entries(offs_sb, a, b)))
 
-        def pick_rounded(j, window, a, b):
-            nc.scalar.activation(picked[:, j, a:b], window[:].indirect(entries(offs_sb, a, b)), COPY)
+        def pick_rounded(j, a, b):
+            nc.scalar.activation(place(j, a, b), rounded[:].indirect(entries(offs_sb, a, b)), COPY)
 
-        def weave(copy, woven, a, b, lanes=slice(0, PACK)):
-            copy(
-                woven.rearrange("p (c i j) -> p c j i", i=4, j=PACK)[:, :, lanes, :],
-                picked[:, lanes, a:b].rearrange("p j (c i) -> p c j i", i=4),
+        def round_columns(j, a, cut, b):
+            nc.scalar.copy(rounded[:, a:cut], planes[j][:, a:cut])
+            nc.gpsimd.tensor_copy(rounded[:, cut:b], planes[j][:, cut:b])
+
+        def quantise(a, b):
+            at = a % g2
+            nc.vector.quantize_mx(
+                out=codes[:, at : at + b - a].bitcast(FP8X4), scales=scales[:, a:b], in_=woven[:, PACK * a : PACK * b]
             )
 
-        def woven_tile(name, n):
-            return sb.tile([P, n * PACK], BF16, name=name, align_bytes=64)[:]
-
-        def mx_tiles(name, n, tag):
-            codes = sb.tile([P, n], U32, name=f"codes_{name}", tag=tag, align_bytes=64)
-            scales = sb.tile([P, n], U8, name=f"scales_{name}", tag=f"scales_{name}", align_bytes=64)
-            return codes[:], scales[:]
-
-        def quantise(codes, scales, woven):
-            nc.vector.quantize_mx(out=codes.bitcast(FP8X4), scales=scales, in_=woven)
-
-        def project(bank, codes, scales):
+        def project(g):
+            at = g * GROUP % g2
             nc.tensor.matmul_mx(
-                out=bank[:],
+                out=banks[g][:],
                 lhsT=w_codes[:].bitcast(FP4X4),
                 lhsT_scale=w_scales[:],
-                rhs=codes.bitcast(FP8X4),
-                rhs_scale=scales,
+                rhs=codes[:, at : at + GROUP].bitcast(FP8X4),
+                rhs_scale=scales[:, g * GROUP : (g + 1) * GROUP],
                 start=True,
                 stop=True,
             )
+            nc.scalar.copy(y[:, g * GROUP : (g + 1) * GROUP], banks[g][:])
 
-        def put(a, b, y):
-            nc.vector.tensor_tensor(store[:].indirect(entries(slot_sb, a, b)), old[:, a:b], y, ADD)
+        def put(a, b):
+            nc.vector.tensor_tensor(store[:].indirect(entries(slot_sb, a, b)), old[:, a:b], y[:, a:b], ADD)
 
-        last = PACK - 1
+        first, second, third, last = ORDER
         nc.vector.memset(w_scales[:].bitcast(I32), 0)
-        nc.sync.dma_start(planes[0][:], x_rows[:, 0, :])
+        nc.sync.dma_start(planes[first][:], x_rows[:, first, :])
         nc.sync.dma_start(offs_sb[:], offs)
-        for j in range(1, last):
+        for j in (second, third):
             nc.sync.dma_start(planes[j][:], x_rows[:, j, :])
         for a, b in LAST_LOADS:
             nc.sync.dma_start(planes[last][:, a:b], x_rows[:, last, a:b])
@@ -107,52 +104,39 @@ def tile_picked_idxput_add_e_kernel(tc, xT, mem, w1_words, w1_scales, offs, slot
         for q in range(4):
             nc.sync.dma_start(w_scales[32 * q : 32 * q + 4, :].bitcast(I32), w1_scales[0, 4 * q : 4 * q + 4, :].bitcast(I32))
 
-        rounded_early = sb.tile([P, T], BF16, name="rounded_early")
-        nc.scalar.copy(rounded_early[:, : T // 2], planes[EARLY][:, : T // 2])
-        nc.gpsimd.tensor_copy(rounded_early[:, T // 2 :], planes[EARLY][:, T // 2 :])
-        pick_rounded(EARLY, rounded_early, EARLY_SHARE, S)
-        for j in range(last):
-            pick(j, 0, EARLY_SHARE if j == EARLY else S)
+        round_columns(first, 0, 1120, T)
+        pick_rounded(first, g1, g2)
+        pick(first, 0, g1)
+        pick(first, g2, S)
 
-        cut = GROUP + GPSIMD_WEAVES
-        woven = woven_tile("woven", S - GPSIMD_WEAVES)
-        woven_first = woven[:, : PACK * GROUP]
-        woven_rest = woven[:, PACK * (GROUP - GPSIMD_WEAVES) :]
+        round_columns(second, 0, 1120, T)
+        pick_rounded(second, SECOND_SHARE, S)
+        pick(second, 0, g2)
+        pick(second, g2, SECOND_SHARE)
 
-        def rest(a, b):
-            return woven_rest[:, PACK * (a - GROUP) : PACK * (b - GROUP)]
+        pick(third, 0, g2)
+        pick(third, g2, S)
 
-        weave(nc.scalar.copy, rest(cut, S), cut, S, slice(0, 2))
-        rounded = sb.tile([P, T], BF16, name="rounded")
-        nc.gpsimd.tensor_copy(rounded[:, : T // 2], planes[last][:, : T // 2])
-        nc.scalar.copy(rounded[:, T // 2 : SCALAR_ROUNDS], planes[last][:, T // 2 : SCALAR_ROUNDS])
-        nc.gpsimd.tensor_copy(rounded[:, SCALAR_ROUNDS:], planes[last][:, SCALAR_ROUNDS:])
-        pick(last, 0, GROUP)
-        pick(last, GROUP, AHEAD)
-
-        weave(nc.vector.tensor_copy, woven_first, 0, GROUP)
-        pick(last, AHEAD, SHARE)
-        codes, scales = mx_tiles("first", GROUP, "codes_first")
-        quantise(codes, scales, woven_first)
-        project(banks[0], codes, scales)
+        for (a, b), n in zip(LAST_LOADS, SCALAR_ROUNDS):
+            round_columns(last, a, a + n, b)
+        pick(last, 0, g1)
+        for g in range(1, S // GROUP):
+            pick_rounded(last, g * GROUP, (g + 1) * GROUP)
+        quantise(0, g1)
+        quantise(g1, g1 + GROUP // 2)
+        quantise(g1 + GROUP // 2, g2)
         nc.vector.tensor_copy(old, store[:].indirect(slot_sb[:]))
-
-        pick_rounded(last, rounded, SHARE, SCALAR_FIRST)
-        pick_rounded(last, rounded, SCALAR_FIRST, S)
-        nc.gpsimd.tensor_copy(
-            rest(GROUP, cut).rearrange("p (n j) -> p n j", j=PACK),
-            picked[:, :, GROUP:cut].rearrange("p j n -> p n j"),
+        nc.gpsimd.tensor_copy(lanes[:, g2:g3, :], picked[:, :, :GROUP].rearrange("p j n -> p n j"))
+        nc.scalar.copy(
+            woven[:, PACK * g3 :].rearrange("p (c i j) -> p c j i", i=4, j=PACK),
+            picked[:, :, GROUP:].rearrange("p j (c i) -> p c j i", i=4),
         )
-        weave(nc.scalar.copy, rest(cut, SCALAR_FIRST), cut, SCALAR_FIRST, slice(2, 4))
-        weave(nc.scalar.copy, rest(SCALAR_FIRST, S), SCALAR_FIRST, S, slice(2, 4))
-        codes, scales = mx_tiles("rest", S - GROUP, "codes_first")
-        for g in range(1, S // GROUP):
-            cols = slice((g - 1) * GROUP, g * GROUP)
-            quantise(codes[:, cols], scales[:, cols], rest(g * GROUP, (g + 1) * GROUP))
-            project(banks[g], codes[:, cols], scales[:, cols])
-        nc.scalar.copy(y_first, banks[0][:])
-        put(0, GROUP, y_first)
-        for g in range(1, S // GROUP):
-            nc.scalar.copy(y_rest[:, (g - 1) * GROUP : g * GROUP], banks[g][:])
-        put(GROUP, S, y_rest[:])
+        project(0)
+        project(1)
+        quantise(g2, g3)
+        quantise(g3, S)
+        put(0, g2)
+        project(2)
+        project(3)
+        put(g2, S)
         nc.sync.dma_start(out, store[:])

@@ -19,11 +19,12 @@ COPY = mybir.ActivationFunctionType.Copy
 P = 128
 PACK = 4
 LANES = 16
+BLOCK = 128
 GROUP = 256
 ORDER = [2, 0, 1, 3]
 SECOND_SHARE = 640
-LAST_LOADS = [(0, 1280), (1280, T)]
-SCALAR_ROUNDS = [704, 416]
+LAST_LOADS = [(0, 1024), (1024, 1664), (1664, T)]
+SCALAR_ROUNDS = [544, 368, 160]
 
 
 def tile_picked_idxput_add_e_kernel(tc, xT, mem, w1_words, w1_scales, offs, slot, out):
@@ -35,13 +36,17 @@ def tile_picked_idxput_add_e_kernel(tc, xT, mem, w1_words, w1_scales, offs, slot
         g1, g2, g3 = GROUP, 2 * GROUP, 3 * GROUP
         offs_sb = sb.tile([P, S // LANES], U16, name="offs_sb")
         slot_sb = sb.tile([P, S // LANES], U16, name="slot_sb")
-        planes = [sb.tile([P, T], F32, name=f"plane{j}") for j in range(PACK)]
-        rounded = sb.tile([P, T], BF16, name="rounded")
+        first, second, third, last = ORDER
+        wide = sb.tile([P, 2 * T], F32, name="wide")
+        planes = {j: sb.tile([P, T], F32, name=f"plane{j}")[:] for j in (first, second)}
+        planes[third] = wide[:, :T]
+        planes[last] = wide[:, T:]
+        rounded = sb.tile([P, T], BF16, name="rounded")[:]
         store = sb.tile([P, U], F32, name="store")
         w_codes = sb.tile([P, 2 * N], U8, name="w_codes", align_bytes=64)
         w_scales = sb.tile([P, N], U8, name="w_scales", align_bytes=64)
-        picked = sb.tile([P, PACK * (S - g2)], BF16, name="picked")[:].rearrange("p (j n) -> p j n", j=PACK)
-        base = 2 * S - PACK * (GROUP + GROUP // 2)
+        picked = sb.tile([P, PACK * (S - g2)], BF16, name="picked")[:].rearrange("p (b j n) -> p b j n", j=PACK, n=BLOCK)
+        base = 2 * S - PACK * GROUP
         shared = sb.tile([P, base + PACK * S], BF16, name="shared", align_bytes=64)
         woven = shared[:, base:]
         old = shared[:, : 2 * S].bitcast(F32)
@@ -56,13 +61,13 @@ def tile_picked_idxput_add_e_kernel(tc, xT, mem, w1_words, w1_scales, offs, slot
             return lst[:, a // LANES : b // LANES]
 
         def place(j, a, b):
-            return lanes[:, a:b, j] if b <= g2 else picked[:, j, a - g2 : b - g2]
+            return lanes[:, a:b, j] if b <= g2 else picked[:, (a - g2) // BLOCK : (b - g2) // BLOCK, j, :]
 
         def pick(j, a, b):
-            nc.vector.tensor_copy(place(j, a, b), planes[j][:].indirect(entries(offs_sb, a, b)))
+            nc.vector.tensor_copy(place(j, a, b), planes[j].indirect(entries(offs_sb, a, b)))
 
         def pick_rounded(j, a, b):
-            nc.scalar.activation(place(j, a, b), rounded[:].indirect(entries(offs_sb, a, b)), COPY)
+            nc.scalar.activation(place(j, a, b), rounded.indirect(entries(offs_sb, a, b)), COPY)
 
         def round_columns(j, a, cut, b):
             nc.scalar.copy(rounded[:, a:cut], planes[j][:, a:cut])
@@ -90,12 +95,11 @@ def tile_picked_idxput_add_e_kernel(tc, xT, mem, w1_words, w1_scales, offs, slot
         def put(a, b):
             nc.vector.tensor_tensor(store[:].indirect(entries(slot_sb, a, b)), old[:, a:b], y[:, a:b], ADD)
 
-        first, second, third, last = ORDER
         nc.vector.memset(w_scales[:].bitcast(I32), 0)
-        nc.sync.dma_start(planes[first][:], x_rows[:, first, :])
+        nc.sync.dma_start(planes[first], x_rows[:, first, :])
         nc.sync.dma_start(offs_sb[:], offs)
         for j in (second, third):
-            nc.sync.dma_start(planes[j][:], x_rows[:, j, :])
+            nc.sync.dma_start(planes[j], x_rows[:, j, :])
         for a, b in LAST_LOADS:
             nc.sync.dma_start(planes[last][:, a:b], x_rows[:, last, a:b])
         nc.sync.dma_start(slot_sb[:], slot)
@@ -115,21 +119,23 @@ def tile_picked_idxput_add_e_kernel(tc, xT, mem, w1_words, w1_scales, offs, slot
         pick(second, g2, SECOND_SHARE)
 
         pick(third, 0, g2)
-        pick(third, g2, S)
+        pick(third, g2, S - BLOCK)
 
         for (a, b), n in zip(LAST_LOADS, SCALAR_ROUNDS):
             round_columns(last, a, a + n, b)
         pick(last, 0, g1)
+        nc.vector.tensor_copy(picked[:, PACK - 1, third, :], wide[:].indirect(entries(offs_sb, S - BLOCK, S)))
         for g in range(1, S // GROUP):
             pick_rounded(last, g * GROUP, (g + 1) * GROUP)
         quantise(0, g1)
-        quantise(g1, g1 + GROUP // 2)
-        quantise(g1 + GROUP // 2, g2)
+        quantise(g1, g2)
         nc.vector.tensor_copy(old, store[:].indirect(slot_sb[:]))
-        nc.gpsimd.tensor_copy(lanes[:, g2:g3, :], picked[:, :, :GROUP].rearrange("p j n -> p n j"))
+        nc.gpsimd.tensor_copy(
+            lanes[:, g2:g3, :].rearrange("p (b n) j -> p b n j", n=BLOCK), picked[:, :2].rearrange("p b j n -> p b n j")
+        )
         nc.scalar.copy(
-            woven[:, PACK * g3 :].rearrange("p (c i j) -> p c j i", i=4, j=PACK),
-            picked[:, :, GROUP:].rearrange("p j (c i) -> p c j i", i=4),
+            woven[:, PACK * g3 :].rearrange("p (b c i j) -> p b c j i", b=2, i=4, j=PACK),
+            picked[:, 2:].rearrange("p b j (c i) -> p b c j i", i=4),
         )
         project(0)
         project(1)

@@ -23,8 +23,8 @@ BLOCK = 128
 GROUP = 256
 ORDER = [2, 0, 1, 3]
 SECOND_SHARE = 640
-LAST_LOADS = [(0, 1024), (1024, 1664), (1664, T)]
-SCALAR_ROUNDS = [544, 368, 160]
+LAST_LOADS = [(0, 1280), (1280, T)]
+SCALAR_ROUNDS = [672, 352]
 
 
 def tile_picked_idxput_add_e_kernel(tc, xT, mem, w1_words, w1_scales, offs, slot, out):
@@ -133,16 +133,19 @@ def tile_picked_idxput_add_e_kernel(tc, xT, mem, w1_words, w1_scales, offs, slot
         nc.gpsimd.tensor_copy(
             lanes[:, g2:g3, :].rearrange("p (b n) j -> p b n j", n=BLOCK), picked[:, :2].rearrange("p b j n -> p b n j")
         )
-        nc.scalar.copy(
-            woven[:, PACK * g3 :].rearrange("p (b c i j) -> p b c j i", b=2, i=4, j=PACK),
-            picked[:, 2:].rearrange("p b j (c i) -> p b c j i", i=4),
-        )
+        for block in (2, 3):
+            a = g2 + block * BLOCK
+            nc.scalar.copy(
+                woven[:, PACK * a : PACK * (a + BLOCK)].rearrange("p (c i j) -> p c j i", i=4, j=PACK),
+                picked[:, block].rearrange("p j (c i) -> p c j i", i=4),
+            )
         project(0)
         project(1)
+        quantise(g3, g3 + BLOCK)
         quantise(g2, g3)
-        quantise(g3, S)
-        put(0, g2)
+        quantise(g3 + BLOCK, S)
+        put(0, g1)
         project(2)
         project(3)
-        put(g2, S)
+        put(g1, S)
         nc.sync.dma_start(out, store[:])

@@ -19,12 +19,8 @@ COPY = mybir.ActivationFunctionType.Copy
 P = 128
 PACK = 4
 LANES = 16
-BLOCK = 128
 GROUP = 256
-ORDER = [2, 0, 1, 3]
-SECOND_SHARE = 640
-LAST_LOADS = [(0, 1280), (1280, T)]
-SCALAR_ROUNDS = [672, 352]
+VECTOR_OLD = 448
 
 
 def tile_picked_idxput_add_e_kernel(tc, xT, mem, w1_words, w1_scales, offs, slot, out):
@@ -36,51 +32,45 @@ def tile_picked_idxput_add_e_kernel(tc, xT, mem, w1_words, w1_scales, offs, slot
         g1, g2, g3 = GROUP, 2 * GROUP, 3 * GROUP
         offs_sb = sb.tile([P, S // LANES], U16, name="offs_sb")
         slot_sb = sb.tile([P, S // LANES], U16, name="slot_sb")
-        first, second, third, last = ORDER
-        wide = sb.tile([P, 2 * T], F32, name="wide")
-        planes = {j: sb.tile([P, T], F32, name=f"plane{j}")[:] for j in (first, second)}
-        planes[third] = wide[:, :T]
-        planes[last] = wide[:, T:]
-        rounded = sb.tile([P, T], BF16, name="rounded")[:]
+        planes = [sb.tile([P, T], F32, name=f"plane{j}") for j in range(PACK)]
         store = sb.tile([P, U], F32, name="store")
         w_codes = sb.tile([P, 2 * N], U8, name="w_codes", align_bytes=64)
         w_scales = sb.tile([P, N], U8, name="w_scales", align_bytes=64)
-        picked = sb.tile([P, PACK * (S - g2)], BF16, name="picked")[:].rearrange("p (b j n) -> p b j n", j=PACK, n=BLOCK)
-        base = 2 * S - PACK * GROUP
-        shared = sb.tile([P, base + PACK * S], BF16, name="shared", align_bytes=64)
-        woven = shared[:, base:]
-        old = shared[:, : 2 * S].bitcast(F32)
-        lanes = woven.rearrange("p (n j) -> p n j", j=PACK)
-        codes = sb.tile([P, 2 * GROUP], U32, name="codes", align_bytes=64)
+        early = sb.tile([P, PACK * g2], BF16, name="early", align_bytes=64)
+        late = [sb.tile([P, PACK * GROUP], BF16, name=f"late{h}", align_bytes=64) for h in range(2)]
+        picked = [sb.tile([P, PACK, GROUP], BF16, name=f"picked{h}") for h in range(2)]
+        codes = sb.tile([P, g3], U32, name="codes", align_bytes=64)
         scales = sb.tile([P, S], U8, name="scales", align_bytes=64)
+        old = sb.tile([P, S], F32, name="old")
         y = sb.tile([P, S], F32, name="y")
         banks = [ps.tile([N, GROUP], F32, name=f"bank{g}") for g in range(S // GROUP)]
         x_rows = xT.rearrange("(p j) t -> p j t", j=PACK)
+        early_lanes = early[:].rearrange("p (n j) -> p n j", j=PACK)
 
         def entries(lst, a, b):
             return lst[:, a // LANES : b // LANES]
 
-        def place(j, a, b):
-            return lanes[:, a:b, j] if b <= g2 else picked[:, (a - g2) // BLOCK : (b - g2) // BLOCK, j, :]
+        def pick_early(j, a, b):
+            nc.vector.tensor_copy(early_lanes[:, a:b, j], planes[j][:].indirect(entries(offs_sb, a, b)))
 
-        def pick(j, a, b):
-            nc.vector.tensor_copy(place(j, a, b), planes[j].indirect(entries(offs_sb, a, b)))
+        def pick_late(j, h):
+            a = g2 + h * GROUP
+            nc.scalar.activation(picked[h][:, j, :], planes[j][:].indirect(entries(offs_sb, a, a + GROUP)), COPY)
 
-        def pick_rounded(j, a, b):
-            nc.scalar.activation(place(j, a, b), rounded.indirect(entries(offs_sb, a, b)), COPY)
+        def lay(copy, h, j):
+            copy(
+                late[h][:].rearrange("p (n j) -> p n j", j=PACK)[:, :, j : j + 2],
+                picked[h][:, j : j + 2, :].rearrange("p j n -> p n j"),
+            )
 
-        def round_columns(j, a, cut, b):
-            nc.scalar.copy(rounded[:, a:cut], planes[j][:, a:cut])
-            nc.gpsimd.tensor_copy(rounded[:, cut:b], planes[j][:, cut:b])
-
-        def quantise(a, b):
-            at = a % g2
+        def quantise(g, woven):
+            at = g * GROUP % g3
             nc.vector.quantize_mx(
-                out=codes[:, at : at + b - a].bitcast(FP8X4), scales=scales[:, a:b], in_=woven[:, PACK * a : PACK * b]
+                out=codes[:, at : at + GROUP].bitcast(FP8X4), scales=scales[:, g * GROUP : (g + 1) * GROUP], in_=woven
             )
 
         def project(g):
-            at = g * GROUP % g2
+            at = g * GROUP % g3
             nc.tensor.matmul_mx(
                 out=banks[g][:],
                 lhsT=w_codes[:].bitcast(FP4X4),
@@ -96,56 +86,41 @@ def tile_picked_idxput_add_e_kernel(tc, xT, mem, w1_words, w1_scales, offs, slot
             nc.vector.tensor_tensor(store[:].indirect(entries(slot_sb, a, b)), old[:, a:b], y[:, a:b], ADD)
 
         nc.vector.memset(w_scales[:].bitcast(I32), 0)
-        nc.sync.dma_start(planes[first], x_rows[:, first, :])
+        nc.sync.dma_start(planes[0][:], x_rows[:, 0, :])
         nc.sync.dma_start(offs_sb[:], offs)
-        for j in (second, third):
-            nc.sync.dma_start(planes[j], x_rows[:, j, :])
-        for a, b in LAST_LOADS:
-            nc.sync.dma_start(planes[last][:, a:b], x_rows[:, last, a:b])
+        for j in range(1, PACK):
+            nc.sync.dma_start(planes[j][:], x_rows[:, j, :])
         nc.sync.dma_start(slot_sb[:], slot)
         nc.sync.dma_start(store[:], mem)
         nc.sync.dma_start(w_codes[:].bitcast(I32), w1_words[0].bitcast(I32))
         for q in range(4):
             nc.sync.dma_start(w_scales[32 * q : 32 * q + 4, :].bitcast(I32), w1_scales[0, 4 * q : 4 * q + 4, :].bitcast(I32))
 
-        round_columns(first, 0, 1120, T)
-        pick_rounded(first, g1, g2)
-        pick(first, 0, g1)
-        pick(first, g2, S)
-
-        round_columns(second, 0, 1120, T)
-        pick_rounded(second, SECOND_SHARE, S)
-        pick(second, 0, g2)
-        pick(second, g2, SECOND_SHARE)
-
-        pick(third, 0, g2)
-        pick(third, g2, S - BLOCK)
-
-        for (a, b), n in zip(LAST_LOADS, SCALAR_ROUNDS):
-            round_columns(last, a, a + n, b)
-        pick(last, 0, g1)
-        nc.vector.tensor_copy(picked[:, PACK - 1, third, :], wide[:].indirect(entries(offs_sb, S - BLOCK, S)))
-        for g in range(1, S // GROUP):
-            pick_rounded(last, g * GROUP, (g + 1) * GROUP)
-        quantise(0, g1)
-        quantise(g1, g2)
-        nc.vector.tensor_copy(old, store[:].indirect(slot_sb[:]))
-        nc.gpsimd.tensor_copy(
-            lanes[:, g2:g3, :].rearrange("p (b n) j -> p b n j", n=BLOCK), picked[:, :2].rearrange("p b j n -> p b n j")
-        )
-        for block in (2, 3):
-            a = g2 + block * BLOCK
-            nc.scalar.copy(
-                woven[:, PACK * a : PACK * (a + BLOCK)].rearrange("p (c i j) -> p c j i", i=4, j=PACK),
-                picked[:, block].rearrange("p j (c i) -> p c j i", i=4),
-            )
+        for j in range(PACK - 1):
+            pick_early(j, 0, g2)
+            pick_late(j, 0)
+            pick_late(j, 1)
+            if j == 1:
+                lay(nc.gpsimd.tensor_copy, 0, 0)
+                lay(nc.gpsimd.tensor_copy, 1, 0)
+        pick_early(PACK - 1, 0, g1)
+        pick_early(PACK - 1, g1, g2)
+        pick_late(PACK - 1, 0)
+        pick_late(PACK - 1, 1)
+        lay(nc.gpsimd.tensor_copy, 0, 2)
+        lay(nc.scalar.copy, 1, 2)
+        quantise(0, early[:, : PACK * g1])
+        quantise(1, early[:, PACK * g1 :])
+        quantise(2, late[0][:])
+        half = (S - VECTOR_OLD) // 2
+        nc.scalar.activation(old[:, :half], store[:].indirect(entries(slot_sb, 0, half)), COPY)
+        nc.vector.tensor_copy(old[:, 2 * half :], store[:].indirect(entries(slot_sb, 2 * half, S)))
         project(0)
+        nc.scalar.activation(old[:, half : 2 * half], store[:].indirect(entries(slot_sb, half, 2 * half)), COPY)
+        quantise(3, late[1][:])
         project(1)
-        quantise(g3, g3 + BLOCK)
-        quantise(g2, g3)
-        quantise(g3 + BLOCK, S)
-        put(0, g1)
         project(2)
         project(3)
+        put(0, g1)
         put(g1, S)
         nc.sync.dma_start(out, store[:])

@@ -20,7 +20,10 @@ P = 128
 PACK = 4
 LANES = 16
 GROUP = 256
+EARLY = 384
 VECTOR_OLD = 448
+FIRST_PUT = 320
+BLOCK = 128
 
 
 def tile_picked_idxput_add_e_kernel(tc, xT, mem, w1_words, w1_scales, offs, slot, out):
@@ -29,61 +32,54 @@ def tile_picked_idxput_add_e_kernel(tc, xT, mem, w1_words, w1_scales, offs, slot
         sb = ctx.enter_context(tc.tile_pool(name="sb", bufs=1))
         ps = ctx.enter_context(tc.psum_pool(name="ps", bufs=1))
 
-        g1, g2, g3 = GROUP, 2 * GROUP, 3 * GROUP
+        middle = EARLY + GROUP
         offs_sb = sb.tile([P, S // LANES], U16, name="offs_sb")
         slot_sb = sb.tile([P, S // LANES], U16, name="slot_sb")
         planes = [sb.tile([P, T], F32, name=f"plane{j}") for j in range(PACK)]
         store = sb.tile([P, U], F32, name="store")
         w_codes = sb.tile([P, 2 * N], U8, name="w_codes", align_bytes=64)
         w_scales = sb.tile([P, N], U8, name="w_scales", align_bytes=64)
-        early = sb.tile([P, PACK * g2], BF16, name="early", align_bytes=64)
-        late = [sb.tile([P, PACK * GROUP], BF16, name=f"late{h}", align_bytes=64) for h in range(2)]
-        picked = [sb.tile([P, PACK, GROUP], BF16, name=f"picked{h}") for h in range(2)]
-        codes = sb.tile([P, g3], U32, name="codes", align_bytes=64)
+        outer = sb.tile([P, PACK * EARLY], BF16, name="outer", align_bytes=64)
+        inner = sb.tile([P, PACK * GROUP], BF16, name="inner", align_bytes=64)
+        picked_inner = sb.tile([P, PACK, GROUP], BF16, name="picked_inner")
+        picked_last = sb.tile([P, PACK, EARLY], BF16, name="picked_last")
+        codes = sb.tile([P, middle], U32, name="codes", align_bytes=64)
         scales = sb.tile([P, S], U8, name="scales", align_bytes=64)
         old = sb.tile([P, S], F32, name="old")
-        y = sb.tile([P, S], F32, name="y")
-        banks = [ps.tile([N, GROUP], F32, name=f"bank{g}") for g in range(S // GROUP)]
+        new = sb.tile([P, S], F32, name="new")
+        spans = [(0, EARLY, 0), (EARLY, middle, 0), (middle, S, GROUP)]
+        banks = [ps.tile([N, b - a], F32, name=f"bank{a}") for a, b, at in spans]
         x_rows = xT.rearrange("(p j) t -> p j t", j=PACK)
-        early_lanes = early[:].rearrange("p (n j) -> p n j", j=PACK)
+        outer_lanes = outer[:].rearrange("p (n j) -> p n j", j=PACK)
+        inner_lanes = inner[:].rearrange("p (n j) -> p n j", j=PACK)
 
         def entries(lst, a, b):
             return lst[:, a // LANES : b // LANES]
 
-        def pick_early(j, a, b):
-            nc.vector.tensor_copy(early_lanes[:, a:b, j], planes[j][:].indirect(entries(offs_sb, a, b)))
-
-        def pick_late(j, h):
-            a = g2 + h * GROUP
-            nc.scalar.activation(picked[h][:, j, :], planes[j][:].indirect(entries(offs_sb, a, a + GROUP)), COPY)
-
-        def lay(copy, h, j):
-            copy(
-                late[h][:].rearrange("p (n j) -> p n j", j=PACK)[:, :, j : j + 2],
-                picked[h][:, j : j + 2, :].rearrange("p j n -> p n j"),
-            )
+        def lay_inner(j):
+            nc.gpsimd.tensor_copy(inner_lanes[:, :, j : j + 2], picked_inner[:, j : j + 2, :].rearrange("p j n -> p n j"))
 
         def quantise(g, woven):
-            at = g * GROUP % g3
-            nc.vector.quantize_mx(
-                out=codes[:, at : at + GROUP].bitcast(FP8X4), scales=scales[:, g * GROUP : (g + 1) * GROUP], in_=woven
-            )
+            a, b, at = spans[g]
+            nc.vector.quantize_mx(out=codes[:, at : at + b - a].bitcast(FP8X4), scales=scales[:, a:b], in_=woven)
 
         def project(g):
-            at = g * GROUP % g3
-            nc.tensor.matmul_mx(
-                out=banks[g][:],
-                lhsT=w_codes[:].bitcast(FP4X4),
-                lhsT_scale=w_scales[:],
-                rhs=codes[:, at : at + GROUP].bitcast(FP8X4),
-                rhs_scale=scales[:, g * GROUP : (g + 1) * GROUP],
-                start=True,
-                stop=True,
-            )
-            nc.scalar.copy(y[:, g * GROUP : (g + 1) * GROUP], banks[g][:])
+            a, b, at = spans[g]
+            for d in range((b - a - 1) % GROUP + 1, b - a + 1, GROUP):
+                c = max(d - GROUP, 0)
+                nc.tensor.matmul_mx(
+                    out=banks[g][:, c:d],
+                    lhsT=w_codes[:].bitcast(FP4X4),
+                    lhsT_scale=w_scales[:],
+                    rhs=codes[:, at + c : at + d].bitcast(FP8X4),
+                    rhs_scale=scales[:, a + c : a + d],
+                    start=True,
+                    stop=True,
+                )
 
-        def put(a, b):
-            nc.vector.tensor_tensor(store[:].indirect(entries(slot_sb, a, b)), old[:, a:b], y[:, a:b], ADD)
+        def add(g, a, b):
+            first = spans[g][0]
+            nc.vector.tensor_tensor(new[:, a:b], banks[g][:, a - first : b - first], old[:, a:b], ADD)
 
         nc.vector.memset(w_scales[:].bitcast(I32), 0)
         nc.sync.dma_start(planes[0][:], x_rows[:, 0, :])
@@ -96,31 +92,27 @@ def tile_picked_idxput_add_e_kernel(tc, xT, mem, w1_words, w1_scales, offs, slot
         for q in range(4):
             nc.sync.dma_start(w_scales[32 * q : 32 * q + 4, :].bitcast(I32), w1_scales[0, 4 * q : 4 * q + 4, :].bitcast(I32))
 
-        for j in range(PACK - 1):
-            pick_early(j, 0, g2)
-            pick_late(j, 0)
-            pick_late(j, 1)
-            if j == 1:
-                lay(nc.gpsimd.tensor_copy, 0, 0)
-                lay(nc.gpsimd.tensor_copy, 1, 0)
-        pick_early(PACK - 1, 0, g1)
-        pick_early(PACK - 1, g1, g2)
-        pick_late(PACK - 1, 0)
-        pick_late(PACK - 1, 1)
-        lay(nc.gpsimd.tensor_copy, 0, 2)
-        lay(nc.scalar.copy, 1, 2)
-        quantise(0, early[:, : PACK * g1])
-        quantise(1, early[:, PACK * g1 :])
-        quantise(2, late[0][:])
-        half = (S - VECTOR_OLD) // 2
-        nc.scalar.activation(old[:, :half], store[:].indirect(entries(slot_sb, 0, half)), COPY)
-        nc.vector.tensor_copy(old[:, 2 * half :], store[:].indirect(entries(slot_sb, 2 * half, S)))
+        for j in range(PACK):
+            nc.vector.tensor_copy(outer_lanes[:, :, j], planes[j][:].indirect(entries(offs_sb, 0, EARLY)))
+            nc.scalar.activation(picked_inner[:, j, :], planes[j][:].indirect(entries(offs_sb, EARLY, middle)), COPY)
+            nc.scalar.activation(picked_last[:, j, :], planes[j][:].indirect(entries(offs_sb, middle, S)), COPY)
+            if j % 2:
+                lay_inner(j - 1)
+        quantise(0, outer[:])
+        for c in range(0, EARLY, BLOCK):
+            nc.gpsimd.tensor_copy(outer_lanes[:, c : c + BLOCK, :], picked_last[:, :, c : c + BLOCK].rearrange("p j n -> p n j"))
+        nc.vector.tensor_copy(old[:, :FIRST_PUT], store[:].indirect(entries(slot_sb, 0, FIRST_PUT)))
+        nc.vector.tensor_copy(old[:, FIRST_PUT:VECTOR_OLD], store[:].indirect(entries(slot_sb, FIRST_PUT, VECTOR_OLD)))
+        nc.scalar.activation(old[:, VECTOR_OLD:], store[:].indirect(entries(slot_sb, VECTOR_OLD, S)), COPY)
         project(0)
-        nc.scalar.activation(old[:, half : 2 * half], store[:].indirect(entries(slot_sb, half, 2 * half)), COPY)
-        quantise(3, late[1][:])
+        add(0, 0, FIRST_PUT)
+        nc.scalar.activation(store[:].indirect(entries(slot_sb, 0, FIRST_PUT)), new[:, :FIRST_PUT], COPY)
+        quantise(1, inner[:])
         project(1)
+        quantise(2, outer[:])
         project(2)
-        project(3)
-        put(0, g1)
-        put(g1, S)
+        add(0, FIRST_PUT, EARLY)
+        add(1, EARLY, middle)
+        add(2, middle, S)
+        nc.vector.tensor_copy(store[:].indirect(entries(slot_sb, FIRST_PUT, S)), new[:, FIRST_PUT:])
         nc.sync.dma_start(out, store[:])

@@ -21,9 +21,10 @@ PACK = 4
 LANES = 16
 GROUP = 256
 EARLY = 384
+MIDDLE = 384
+FILL = 128
+GPSIMD_LAYS = 192
 VECTOR_OLD = 448
-FIRST_PUT = 320
-BLOCK = 128
 
 
 def tile_picked_idxput_add_e_kernel(tc, xT, mem, w1_words, w1_scales, offs, slot, out):
@@ -32,54 +33,50 @@ def tile_picked_idxput_add_e_kernel(tc, xT, mem, w1_words, w1_scales, offs, slot
         sb = ctx.enter_context(tc.tile_pool(name="sb", bufs=1))
         ps = ctx.enter_context(tc.psum_pool(name="ps", bufs=1))
 
-        middle = EARLY + GROUP
+        last_from = EARLY + MIDDLE
+        last = S - last_from
         offs_sb = sb.tile([P, S // LANES], U16, name="offs_sb")
         slot_sb = sb.tile([P, S // LANES], U16, name="slot_sb")
         planes = [sb.tile([P, T], F32, name=f"plane{j}") for j in range(PACK)]
         store = sb.tile([P, U], F32, name="store")
         w_codes = sb.tile([P, 2 * N], U8, name="w_codes", align_bytes=64)
         w_scales = sb.tile([P, N], U8, name="w_scales", align_bytes=64)
-        outer = sb.tile([P, PACK * EARLY], BF16, name="outer", align_bytes=64)
-        inner = sb.tile([P, PACK * GROUP], BF16, name="inner", align_bytes=64)
-        picked_inner = sb.tile([P, PACK, GROUP], BF16, name="picked_inner")
-        picked_last = sb.tile([P, PACK, EARLY], BF16, name="picked_last")
-        codes = sb.tile([P, middle], U32, name="codes", align_bytes=64)
-        scales = sb.tile([P, S], U8, name="scales", align_bytes=64)
+        early_in = sb.tile([P, EARLY, PACK], BF16, name="early_in", align_bytes=64)
+        middle_in = sb.tile([P, MIDDLE, PACK], BF16, name="middle_in", align_bytes=64)
+        picked_a = sb.tile([P, PACK, GPSIMD_LAYS], BF16, name="picked_a")
+        picked_b = sb.tile([P, PACK, MIDDLE - GPSIMD_LAYS], BF16, name="picked_b")
+        picked_last = sb.tile([P, PACK, last], BF16, name="picked_last")
         old = sb.tile([P, S], F32, name="old")
         new = sb.tile([P, S], F32, name="new")
-        spans = [(0, EARLY, 0), (EARLY, middle, 0), (middle, S, GROUP)]
-        banks = [ps.tile([N, b - a], F32, name=f"bank{a}") for a, b, at in spans]
         x_rows = xT.rearrange("(p j) t -> p j t", j=PACK)
-        outer_lanes = outer[:].rearrange("p (n j) -> p n j", j=PACK)
-        inner_lanes = inner[:].rearrange("p (n j) -> p n j", j=PACK)
 
         def entries(lst, a, b):
             return lst[:, a // LANES : b // LANES]
 
-        def lay_inner(j):
-            nc.gpsimd.tensor_copy(inner_lanes[:, :, j : j + 2], picked_inner[:, j : j + 2, :].rearrange("p j n -> p n j"))
+        def pick(to, j, a, b):
+            nc.scalar.activation(to, planes[j][:].indirect(entries(offs_sb, a, b)), COPY)
 
-        def quantise(g, woven):
-            a, b, at = spans[g]
-            nc.vector.quantize_mx(out=codes[:, at : at + b - a].bitcast(FP8X4), scales=scales[:, a:b], in_=woven)
+        def lay(copy, woven, picked, j):
+            copy(woven[:, :, j : j + 2], picked[:, j : j + 2, :].rearrange("p j n -> p n j"))
 
-        def project(g):
-            a, b, at = spans[g]
-            for d in range((b - a - 1) % GROUP + 1, b - a + 1, GROUP):
+        def quantise(woven, codes, scales):
+            nc.vector.quantize_mx(out=codes[:].bitcast(FP8X4), scales=scales[:], in_=woven[:].rearrange("p n j -> p (n j)"))
+
+        def project(bank, codes, scales, n):
+            for d in range((n - 1) % GROUP + 1, n + 1, GROUP):
                 c = max(d - GROUP, 0)
                 nc.tensor.matmul_mx(
-                    out=banks[g][:, c:d],
+                    out=bank[:, c:d],
                     lhsT=w_codes[:].bitcast(FP4X4),
                     lhsT_scale=w_scales[:],
-                    rhs=codes[:, at + c : at + d].bitcast(FP8X4),
-                    rhs_scale=scales[:, a + c : a + d],
+                    rhs=codes[:, c:d].bitcast(FP8X4),
+                    rhs_scale=scales[:, c:d],
                     start=True,
                     stop=True,
                 )
 
-        def add(g, a, b):
-            first = spans[g][0]
-            nc.vector.tensor_tensor(new[:, a:b], banks[g][:, a - first : b - first], old[:, a:b], ADD)
+        def add(bank, first, a, b):
+            nc.vector.tensor_tensor(new[:, a:b], bank[:, a - first : b - first], old[:, a:b], ADD)
 
         nc.vector.memset(w_scales[:].bitcast(I32), 0)
         nc.sync.dma_start(planes[0][:], x_rows[:, 0, :])
@@ -92,27 +89,44 @@ def tile_picked_idxput_add_e_kernel(tc, xT, mem, w1_words, w1_scales, offs, slot
         for q in range(4):
             nc.sync.dma_start(w_scales[32 * q : 32 * q + 4, :].bitcast(I32), w1_scales[0, 4 * q : 4 * q + 4, :].bitcast(I32))
 
+        cut = EARLY + GPSIMD_LAYS
         for j in range(PACK):
-            nc.vector.tensor_copy(outer_lanes[:, :, j], planes[j][:].indirect(entries(offs_sb, 0, EARLY)))
-            nc.scalar.activation(picked_inner[:, j, :], planes[j][:].indirect(entries(offs_sb, EARLY, middle)), COPY)
-            nc.scalar.activation(picked_last[:, j, :], planes[j][:].indirect(entries(offs_sb, middle, S)), COPY)
+            nc.vector.tensor_copy(early_in[:, :, j], planes[j][:].indirect(entries(offs_sb, 0, EARLY)))
+            nc.vector.tensor_copy(picked_last[:, j, last - FILL :], planes[j][:].indirect(entries(offs_sb, S - FILL, S)))
+            pick(picked_a[:, j, :], j, EARLY, cut)
+            pick(picked_b[:, j, :], j, cut, last_from)
+            pick(picked_last[:, j, : last - FILL], j, last_from, S - FILL)
             if j % 2:
-                lay_inner(j - 1)
-        quantise(0, outer[:])
-        for c in range(0, EARLY, BLOCK):
-            nc.gpsimd.tensor_copy(outer_lanes[:, c : c + BLOCK, :], picked_last[:, :, c : c + BLOCK].rearrange("p j n -> p n j"))
-        nc.vector.tensor_copy(old[:, :FIRST_PUT], store[:].indirect(entries(slot_sb, 0, FIRST_PUT)))
-        nc.vector.tensor_copy(old[:, FIRST_PUT:VECTOR_OLD], store[:].indirect(entries(slot_sb, FIRST_PUT, VECTOR_OLD)))
+                lay(nc.gpsimd.tensor_copy, middle_in[:, :GPSIMD_LAYS, :], picked_a, j - 1)
+                lay(nc.scalar.copy if j == PACK - 1 else nc.gpsimd.tensor_copy, middle_in[:, GPSIMD_LAYS:, :], picked_b, j - 1)
+
+        early_codes = sb.tile([P, EARLY], U32, name="early_codes", tag="held_a", align_bytes=64)
+        early_scales = sb.tile([P, EARLY], U8, name="early_scales", tag="held_b", align_bytes=64)
+        early_bank = ps.tile([N, EARLY], F32, name="early_bank")
+        quantise(early_in, early_codes, early_scales)
+        nc.vector.tensor_copy(old[:, :GROUP], store[:].indirect(entries(slot_sb, 0, GROUP)))
+        nc.vector.tensor_copy(old[:, GROUP:VECTOR_OLD], store[:].indirect(entries(slot_sb, GROUP, VECTOR_OLD)))
         nc.scalar.activation(old[:, VECTOR_OLD:], store[:].indirect(entries(slot_sb, VECTOR_OLD, S)), COPY)
-        project(0)
-        add(0, 0, FIRST_PUT)
-        nc.scalar.activation(store[:].indirect(entries(slot_sb, 0, FIRST_PUT)), new[:, :FIRST_PUT], COPY)
-        quantise(1, inner[:])
-        project(1)
-        quantise(2, outer[:])
-        project(2)
-        add(0, FIRST_PUT, EARLY)
-        add(1, EARLY, middle)
-        add(2, middle, S)
-        nc.vector.tensor_copy(store[:].indirect(entries(slot_sb, FIRST_PUT, S)), new[:, FIRST_PUT:])
+        project(early_bank, early_codes, early_scales, EARLY)
+        add(early_bank, 0, 0, GROUP)
+        add(early_bank, 0, GROUP, EARLY)
+        nc.scalar.activation(store[:].indirect(entries(slot_sb, 0, EARLY)), new[:, :EARLY], COPY)
+
+        last_in = sb.tile([P, last, PACK], BF16, name="last_in", tag="held_a", align_bytes=64)
+        middle_codes = sb.tile([P, MIDDLE], U32, name="middle_codes", align_bytes=64)
+        middle_scales = sb.tile([P, MIDDLE], U8, name="middle_scales", tag="held_b", align_bytes=64)
+        last_codes = sb.tile([P, last], U32, name="last_codes", align_bytes=64)
+        last_scales = sb.tile([P, last], U8, name="last_scales", align_bytes=64)
+        middle_bank = ps.tile([N, MIDDLE], F32, name="middle_bank")
+        last_bank = ps.tile([N, last], F32, name="last_bank")
+        nc.vector.tensor_copy(
+            last_in[:].rearrange("p (c i) j -> p c j i", i=4), picked_last[:].rearrange("p j (c i) -> p c j i", i=4)
+        )
+        quantise(middle_in, middle_codes, middle_scales)
+        quantise(last_in, last_codes, last_scales)
+        project(middle_bank, middle_codes, middle_scales, MIDDLE)
+        project(last_bank, last_codes, last_scales, last)
+        add(middle_bank, EARLY, EARLY, last_from)
+        add(last_bank, last_from, last_from, S)
+        nc.vector.tensor_copy(store[:].indirect(entries(slot_sb, EARLY, S)), new[:, EARLY:])
         nc.sync.dma_start(out, store[:])

@@ -20,10 +20,8 @@ P = 128
 PACK = 4
 LANES = 16
 GROUP = 256
+BLOCK = 128
 EARLY = 384
-MIDDLE = 384
-FILL = 128
-GPSIMD_LAYS = 192
 VECTOR_OLD = 448
 
 
@@ -33,8 +31,7 @@ def tile_picked_idxput_add_e_kernel(tc, xT, mem, w1_words, w1_scales, offs, slot
         sb = ctx.enter_context(tc.tile_pool(name="sb", bufs=1))
         ps = ctx.enter_context(tc.psum_pool(name="ps", bufs=1))
 
-        last_from = EARLY + MIDDLE
-        last = S - last_from
+        second, third, last = EARLY, EARLY + GROUP, S - BLOCK
         offs_sb = sb.tile([P, S // LANES], U16, name="offs_sb")
         slot_sb = sb.tile([P, S // LANES], U16, name="slot_sb")
         planes = [sb.tile([P, T], F32, name=f"plane{j}") for j in range(PACK)]
@@ -42,10 +39,11 @@ def tile_picked_idxput_add_e_kernel(tc, xT, mem, w1_words, w1_scales, offs, slot
         w_codes = sb.tile([P, 2 * N], U8, name="w_codes", align_bytes=64)
         w_scales = sb.tile([P, N], U8, name="w_scales", align_bytes=64)
         early_in = sb.tile([P, EARLY, PACK], BF16, name="early_in", align_bytes=64)
-        middle_in = sb.tile([P, MIDDLE, PACK], BF16, name="middle_in", align_bytes=64)
-        picked_a = sb.tile([P, PACK, GPSIMD_LAYS], BF16, name="picked_a")
-        picked_b = sb.tile([P, PACK, MIDDLE - GPSIMD_LAYS], BF16, name="picked_b")
-        picked_last = sb.tile([P, PACK, last], BF16, name="picked_last")
+        second_in = sb.tile([P, GROUP, PACK], BF16, name="second_in", align_bytes=64)
+        third_in = sb.tile([P, GROUP, PACK], BF16, name="third_in", align_bytes=64)
+        second_picked = [sb.tile([P, PACK, BLOCK], BF16, name=f"second_picked{h}") for h in range(2)]
+        third_picked = sb.tile([P, PACK, GROUP], BF16, name="third_picked")
+        last_picked = sb.tile([P, PACK, BLOCK], BF16, name="last_picked")
         old = sb.tile([P, S], F32, name="old")
         new = sb.tile([P, S], F32, name="new")
         x_rows = xT.rearrange("(p j) t -> p j t", j=PACK)
@@ -60,23 +58,21 @@ def tile_picked_idxput_add_e_kernel(tc, xT, mem, w1_words, w1_scales, offs, slot
             copy(woven[:, :, j : j + 2], picked[:, j : j + 2, :].rearrange("p j n -> p n j"))
 
         def quantise(woven, codes, scales):
-            nc.vector.quantize_mx(out=codes[:].bitcast(FP8X4), scales=scales[:], in_=woven[:].rearrange("p n j -> p (n j)"))
+            nc.vector.quantize_mx(out=codes.bitcast(FP8X4), scales=scales, in_=woven[:].rearrange("p n j -> p (n j)"))
 
-        def project(bank, codes, scales, n):
-            for d in range((n - 1) % GROUP + 1, n + 1, GROUP):
-                c = max(d - GROUP, 0)
-                nc.tensor.matmul_mx(
-                    out=bank[:, c:d],
-                    lhsT=w_codes[:].bitcast(FP4X4),
-                    lhsT_scale=w_scales[:],
-                    rhs=codes[:, c:d].bitcast(FP8X4),
-                    rhs_scale=scales[:, c:d],
-                    start=True,
-                    stop=True,
-                )
+        def project(bank, codes, scales):
+            nc.tensor.matmul_mx(
+                out=bank,
+                lhsT=w_codes[:].bitcast(FP4X4),
+                lhsT_scale=w_scales[:],
+                rhs=codes.bitcast(FP8X4),
+                rhs_scale=scales,
+                start=True,
+                stop=True,
+            )
 
-        def add(bank, first, a, b):
-            nc.vector.tensor_tensor(new[:, a:b], bank[:, a - first : b - first], old[:, a:b], ADD)
+        def add(bank, a, b):
+            nc.vector.tensor_tensor(new[:, a:b], bank, old[:, a:b], ADD)
 
         nc.vector.memset(w_scales[:].bitcast(I32), 0)
         nc.sync.dma_start(planes[0][:], x_rows[:, 0, :])
@@ -89,44 +85,42 @@ def tile_picked_idxput_add_e_kernel(tc, xT, mem, w1_words, w1_scales, offs, slot
         for q in range(4):
             nc.sync.dma_start(w_scales[32 * q : 32 * q + 4, :].bitcast(I32), w1_scales[0, 4 * q : 4 * q + 4, :].bitcast(I32))
 
-        cut = EARLY + GPSIMD_LAYS
         for j in range(PACK):
             nc.vector.tensor_copy(early_in[:, :, j], planes[j][:].indirect(entries(offs_sb, 0, EARLY)))
-            nc.vector.tensor_copy(picked_last[:, j, last - FILL :], planes[j][:].indirect(entries(offs_sb, S - FILL, S)))
-            pick(picked_a[:, j, :], j, EARLY, cut)
-            pick(picked_b[:, j, :], j, cut, last_from)
-            pick(picked_last[:, j, : last - FILL], j, last_from, S - FILL)
+            nc.vector.tensor_copy(last_picked[:, j, :], planes[j][:].indirect(entries(offs_sb, last, S)))
+            for h in range(2):
+                pick(second_picked[h][:, j, :], j, second + h * BLOCK, second + (h + 1) * BLOCK)
+            pick(third_picked[:, j, :], j, third, last)
             if j % 2:
-                lay(nc.gpsimd.tensor_copy, middle_in[:, :GPSIMD_LAYS, :], picked_a, j - 1)
-                lay(nc.scalar.copy if j == PACK - 1 else nc.gpsimd.tensor_copy, middle_in[:, GPSIMD_LAYS:, :], picked_b, j - 1)
+                for h in range(2):
+                    lay(nc.gpsimd.tensor_copy, second_in[:, h * BLOCK : (h + 1) * BLOCK, :], second_picked[h], j - 1)
+                lay(nc.scalar.copy if j == PACK - 1 else nc.gpsimd.tensor_copy, third_in, third_picked, j - 1)
 
         early_codes = sb.tile([P, EARLY], U32, name="early_codes", tag="held_a", align_bytes=64)
         early_scales = sb.tile([P, EARLY], U8, name="early_scales", tag="held_b", align_bytes=64)
         early_bank = ps.tile([N, EARLY], F32, name="early_bank")
-        quantise(early_in, early_codes, early_scales)
+        quantise(early_in, early_codes[:], early_scales[:])
         nc.vector.tensor_copy(old[:, :GROUP], store[:].indirect(entries(slot_sb, 0, GROUP)))
         nc.vector.tensor_copy(old[:, GROUP:VECTOR_OLD], store[:].indirect(entries(slot_sb, GROUP, VECTOR_OLD)))
         nc.scalar.activation(old[:, VECTOR_OLD:], store[:].indirect(entries(slot_sb, VECTOR_OLD, S)), COPY)
-        project(early_bank, early_codes, early_scales, EARLY)
-        add(early_bank, 0, 0, GROUP)
-        add(early_bank, 0, GROUP, EARLY)
+        project(early_bank[:, :GROUP], early_codes[:, :GROUP], early_scales[:, :GROUP])
+        project(early_bank[:, GROUP:], early_codes[:, GROUP:], early_scales[:, GROUP:])
+        add(early_bank[:, :GROUP], 0, GROUP)
+        add(early_bank[:, GROUP:], GROUP, EARLY)
         nc.scalar.activation(store[:].indirect(entries(slot_sb, 0, EARLY)), new[:, :EARLY], COPY)
 
-        last_in = sb.tile([P, last, PACK], BF16, name="last_in", tag="held_a", align_bytes=64)
-        middle_codes = sb.tile([P, MIDDLE], U32, name="middle_codes", align_bytes=64)
-        middle_scales = sb.tile([P, MIDDLE], U8, name="middle_scales", tag="held_b", align_bytes=64)
-        last_codes = sb.tile([P, last], U32, name="last_codes", align_bytes=64)
-        last_scales = sb.tile([P, last], U8, name="last_scales", align_bytes=64)
-        middle_bank = ps.tile([N, MIDDLE], F32, name="middle_bank")
-        last_bank = ps.tile([N, last], F32, name="last_bank")
+        last_in = sb.tile([P, BLOCK, PACK], BF16, name="last_in", tag="held_a", align_bytes=64)
+        late_codes = sb.tile([P, S - EARLY], U32, name="late_codes", align_bytes=64)
+        late_scales = sb.tile([P, S - EARLY], U8, name="late_scales", tag="held_b", align_bytes=64)
         nc.vector.tensor_copy(
-            last_in[:].rearrange("p (c i) j -> p c j i", i=4), picked_last[:].rearrange("p j (c i) -> p c j i", i=4)
+            last_in[:].rearrange("p (c i) j -> p c j i", i=4), last_picked[:].rearrange("p j (c i) -> p c j i", i=4)
         )
-        quantise(middle_in, middle_codes, middle_scales)
-        quantise(last_in, last_codes, last_scales)
-        project(middle_bank, middle_codes, middle_scales, MIDDLE)
-        project(last_bank, last_codes, last_scales, last)
-        add(middle_bank, EARLY, EARLY, last_from)
-        add(last_bank, last_from, last_from, S)
+        late = [(second_in, second, third), (third_in, third, last), (last_in, last, S)]
+        late_banks = [ps.tile([N, b - a], F32, name=f"bank{a}") for woven, a, b in late]
+        for (woven, a, b), bank in zip(late, late_banks):
+            quantise(woven, late_codes[:, a - EARLY : b - EARLY], late_scales[:, a - EARLY : b - EARLY])
+            project(bank[:], late_codes[:, a - EARLY : b - EARLY], late_scales[:, a - EARLY : b - EARLY])
+        for (woven, a, b), bank in zip(late, late_banks):
+            add(bank[:], a, b)
         nc.vector.tensor_copy(store[:].indirect(entries(slot_sb, EARLY, S)), new[:, EARLY:])
         nc.sync.dma_start(out, store[:])

@@ -22,13 +22,15 @@ LANES = 16
 GROUP = 256
 BLOCK = 128
 EARLY = 384
-VECTOR_OLD = 448
+VECTOR_OLD = 384
+LOADED_TWICE = 1280
 
 
 def tile_picked_idxput_add_e_kernel(tc, xT, mem, w1_words, w1_scales, offs, slot, out):
     nc = tc.nc
     with ExitStack() as ctx:
         sb = ctx.enter_context(tc.tile_pool(name="sb", bufs=1))
+        turns = ctx.enter_context(tc.tile_pool(name="turns", bufs=1))
         ps = ctx.enter_context(tc.psum_pool(name="ps", bufs=1))
 
         second, third, last = EARLY, EARLY + GROUP, S - BLOCK
@@ -36,6 +38,7 @@ def tile_picked_idxput_add_e_kernel(tc, xT, mem, w1_words, w1_scales, offs, slot
         slot_sb = sb.tile([P, S // LANES], U16, name="slot_sb")
         planes = [sb.tile([P, T], F32, name=f"plane{j}") for j in range(PACK)]
         store = sb.tile([P, U], F32, name="store")
+        before = sb.tile([P, U], F32, name="before")
         w_codes = sb.tile([P, 2 * N], U8, name="w_codes", align_bytes=64)
         w_scales = sb.tile([P, N], U8, name="w_scales", align_bytes=64)
         early_in = sb.tile([P, EARLY, PACK], BF16, name="early_in", align_bytes=64)
@@ -44,7 +47,7 @@ def tile_picked_idxput_add_e_kernel(tc, xT, mem, w1_words, w1_scales, offs, slot
         second_picked = [sb.tile([P, PACK, BLOCK], BF16, name=f"second_picked{h}") for h in range(2)]
         third_picked = sb.tile([P, PACK, GROUP], BF16, name="third_picked")
         last_picked = sb.tile([P, PACK, BLOCK], BF16, name="last_picked")
-        old = sb.tile([P, S], F32, name="old")
+        old = sb.tile([P, last], F32, name="old")
         new = sb.tile([P, S], F32, name="new")
         x_rows = xT.rearrange("(p j) t -> p j t", j=PACK)
 
@@ -71,8 +74,10 @@ def tile_picked_idxput_add_e_kernel(tc, xT, mem, w1_words, w1_scales, offs, slot
                 stop=True,
             )
 
+        last_old = turns.tile([P, BLOCK], F32, name="last_old", offset=2 * PACK * BLOCK, align_bytes=64)
+
         def add(bank, a, b):
-            nc.vector.tensor_tensor(new[:, a:b], bank, old[:, a:b], ADD)
+            nc.vector.tensor_tensor(new[:, a:b], bank, old[:, a:b] if b <= last else last_old[:], ADD)
 
         nc.vector.memset(w_scales[:].bitcast(I32), 0)
         nc.sync.dma_start(planes[0][:], x_rows[:, 0, :])
@@ -80,10 +85,11 @@ def tile_picked_idxput_add_e_kernel(tc, xT, mem, w1_words, w1_scales, offs, slot
         for j in range(1, PACK):
             nc.sync.dma_start(planes[j][:], x_rows[:, j, :])
         nc.sync.dma_start(slot_sb[:], slot)
-        nc.sync.dma_start(store[:], mem)
+        nc.sync.dma_start(before[:], mem)
         nc.sync.dma_start(w_codes[:].bitcast(I32), w1_words[0].bitcast(I32))
         for q in range(4):
             nc.sync.dma_start(w_scales[32 * q : 32 * q + 4, :].bitcast(I32), w1_scales[0, 4 * q : 4 * q + 4, :].bitcast(I32))
+        nc.sync.dma_start(store[:, :LOADED_TWICE], mem[:, :LOADED_TWICE])
 
         for j in range(PACK):
             nc.vector.tensor_copy(early_in[:, :, j], planes[j][:].indirect(entries(offs_sb, 0, EARLY)))
@@ -96,20 +102,21 @@ def tile_picked_idxput_add_e_kernel(tc, xT, mem, w1_words, w1_scales, offs, slot
                     lay(nc.gpsimd.tensor_copy, second_in[:, h * BLOCK : (h + 1) * BLOCK, :], second_picked[h], j - 1)
                 lay(nc.scalar.copy if j == PACK - 1 else nc.gpsimd.tensor_copy, third_in, third_picked, j - 1)
 
-        early_codes = sb.tile([P, EARLY], U32, name="early_codes", tag="held_a", align_bytes=64)
+        early_codes = turns.tile([P, EARLY], U32, name="early_codes", offset=0, align_bytes=64)
         early_scales = sb.tile([P, EARLY], U8, name="early_scales", tag="held_b", align_bytes=64)
-        early_bank = ps.tile([N, EARLY], F32, name="early_bank")
+        early_banks = [ps.tile([N, n], F32, name=f"early_bank{n}") for n in (GROUP, BLOCK)]
         quantise(early_in, early_codes[:], early_scales[:])
-        nc.vector.tensor_copy(old[:, :GROUP], store[:].indirect(entries(slot_sb, 0, GROUP)))
-        nc.vector.tensor_copy(old[:, GROUP:VECTOR_OLD], store[:].indirect(entries(slot_sb, GROUP, VECTOR_OLD)))
-        nc.scalar.activation(old[:, VECTOR_OLD:], store[:].indirect(entries(slot_sb, VECTOR_OLD, S)), COPY)
-        project(early_bank[:, :GROUP], early_codes[:, :GROUP], early_scales[:, :GROUP])
-        project(early_bank[:, GROUP:], early_codes[:, GROUP:], early_scales[:, GROUP:])
-        add(early_bank[:, :GROUP], 0, GROUP)
-        add(early_bank[:, GROUP:], GROUP, EARLY)
+        nc.gpsimd.tensor_copy(store[:, LOADED_TWICE:], before[:, LOADED_TWICE:])
+        nc.vector.tensor_copy(old[:, :GROUP], before[:].indirect(entries(slot_sb, 0, GROUP)))
+        nc.vector.tensor_copy(old[:, GROUP:VECTOR_OLD], before[:].indirect(entries(slot_sb, GROUP, VECTOR_OLD)))
+        nc.scalar.activation(old[:, VECTOR_OLD:], before[:].indirect(entries(slot_sb, VECTOR_OLD, last)), COPY)
+        project(early_banks[0][:], early_codes[:, :GROUP], early_scales[:, :GROUP])
+        project(early_banks[1][:], early_codes[:, GROUP:], early_scales[:, GROUP:])
+        add(early_banks[0][:], 0, GROUP)
+        add(early_banks[1][:], GROUP, EARLY)
         nc.scalar.activation(store[:].indirect(entries(slot_sb, 0, EARLY)), new[:, :EARLY], COPY)
 
-        last_in = sb.tile([P, BLOCK, PACK], BF16, name="last_in", tag="held_a", align_bytes=64)
+        last_in = turns.tile([P, BLOCK, PACK], BF16, name="last_in", offset=0, align_bytes=64)
         late_codes = sb.tile([P, S - EARLY], U32, name="late_codes", align_bytes=64)
         late_scales = sb.tile([P, S - EARLY], U8, name="late_scales", tag="held_b", align_bytes=64)
         nc.vector.tensor_copy(
@@ -120,6 +127,7 @@ def tile_picked_idxput_add_e_kernel(tc, xT, mem, w1_words, w1_scales, offs, slot
         for (woven, a, b), bank in zip(late, late_banks):
             quantise(woven, late_codes[:, a - EARLY : b - EARLY], late_scales[:, a - EARLY : b - EARLY])
             project(bank[:], late_codes[:, a - EARLY : b - EARLY], late_scales[:, a - EARLY : b - EARLY])
+        nc.vector.tensor_copy(last_old[:], before[:].indirect(entries(slot_sb, last, S)))
         for (woven, a, b), bank in zip(late, late_banks):
             add(bank[:], a, b)
         nc.vector.tensor_copy(store[:].indirect(entries(slot_sb, EARLY, S)), new[:, EARLY:])

@@ -14,6 +14,8 @@ U8 = mybir.dt.uint8
 FP8X4 = mybir.dt.float8_e4m3fn_x4
 FP4X4 = mybir.dt.float4_e2m1fn_x4
 ADD = mybir.AluOpType.add
+MULT = mybir.AluOpType.mult
+SUBTRACT = mybir.AluOpType.subtract
 COPY = mybir.ActivationFunctionType.Copy
 
 P = 128
@@ -22,8 +24,9 @@ LANES = 16
 GROUP = 256
 BLOCK = 128
 EARLY = 384
-VECTOR_OLD = 384
-LOADED_TWICE = 1280
+VECTOR_OLD = 256
+SCALAR_PUT = 704
+CHUNKS = (256, 512, 512, 512, 256)
 
 
 def tile_picked_idxput_add_e_kernel(tc, xT, mem, w1_words, w1_scales, offs, slot, out):
@@ -37,8 +40,9 @@ def tile_picked_idxput_add_e_kernel(tc, xT, mem, w1_words, w1_scales, offs, slot
         offs_sb = sb.tile([P, S // LANES], U16, name="offs_sb")
         slot_sb = sb.tile([P, S // LANES], U16, name="slot_sb")
         planes = [sb.tile([P, T], F32, name=f"plane{j}") for j in range(PACK)]
-        store = sb.tile([P, U], F32, name="store")
-        before = sb.tile([P, U], F32, name="before")
+        doubled = sb.tile([P, U], F32, name="doubled")
+        taken = sb.tile([P, U], F32, name="taken")
+        merged = sb.tile([P, U], F32, name="merged")
         w_codes = sb.tile([P, 2 * N], U8, name="w_codes", align_bytes=64)
         w_scales = sb.tile([P, N], U8, name="w_scales", align_bytes=64)
         early_in = sb.tile([P, EARLY, PACK], BF16, name="early_in", align_bytes=64)
@@ -47,8 +51,8 @@ def tile_picked_idxput_add_e_kernel(tc, xT, mem, w1_words, w1_scales, offs, slot
         second_picked = [sb.tile([P, PACK, BLOCK], BF16, name=f"second_picked{h}") for h in range(2)]
         third_picked = sb.tile([P, PACK, GROUP], BF16, name="third_picked")
         last_picked = sb.tile([P, PACK, BLOCK], BF16, name="last_picked")
-        old = sb.tile([P, last], F32, name="old")
-        new = sb.tile([P, S], F32, name="new")
+        old = sb.tile([P, S], F32, name="old")
+        put = sb.tile([P, S], F32, name="put")
         x_rows = xT.rearrange("(p j) t -> p j t", j=PACK)
 
         def entries(lst, a, b):
@@ -74,10 +78,9 @@ def tile_picked_idxput_add_e_kernel(tc, xT, mem, w1_words, w1_scales, offs, slot
                 stop=True,
             )
 
-        last_old = turns.tile([P, BLOCK], F32, name="last_old", offset=2 * PACK * BLOCK, align_bytes=64)
-
-        def add(bank, a, b):
-            nc.vector.tensor_tensor(new[:, a:b], bank, old[:, a:b] if b <= last else last_old[:], ADD)
+        def add(bank, first, a, b):
+            share = 0.5 if b <= SCALAR_PUT else -1.0
+            nc.vector.scalar_tensor_tensor(put[:, a:b], bank[:, a - first : b - first], share, old[:, a:b], MULT, ADD)
 
         nc.vector.memset(w_scales[:].bitcast(I32), 0)
         nc.sync.dma_start(planes[0][:], x_rows[:, 0, :])
@@ -85,11 +88,11 @@ def tile_picked_idxput_add_e_kernel(tc, xT, mem, w1_words, w1_scales, offs, slot
         for j in range(1, PACK):
             nc.sync.dma_start(planes[j][:], x_rows[:, j, :])
         nc.sync.dma_start(slot_sb[:], slot)
-        nc.sync.dma_start(before[:], mem)
+        nc.sync.dma_start(doubled[:], mem)
         nc.sync.dma_start(w_codes[:].bitcast(I32), w1_words[0].bitcast(I32))
         for q in range(4):
             nc.sync.dma_start(w_scales[32 * q : 32 * q + 4, :].bitcast(I32), w1_scales[0, 4 * q : 4 * q + 4, :].bitcast(I32))
-        nc.sync.dma_start(store[:, :LOADED_TWICE], mem[:, :LOADED_TWICE])
+        nc.sync.dma_start(taken[:], mem)
 
         for j in range(PACK):
             nc.vector.tensor_copy(early_in[:, :, j], planes[j][:].indirect(entries(offs_sb, 0, EARLY)))
@@ -106,29 +109,41 @@ def tile_picked_idxput_add_e_kernel(tc, xT, mem, w1_words, w1_scales, offs, slot
         early_scales = sb.tile([P, EARLY], U8, name="early_scales", tag="held_b", align_bytes=64)
         early_banks = [ps.tile([N, n], F32, name=f"early_bank{n}") for n in (GROUP, BLOCK)]
         quantise(early_in, early_codes[:], early_scales[:])
-        nc.gpsimd.tensor_copy(store[:, LOADED_TWICE:], before[:, LOADED_TWICE:])
-        nc.vector.tensor_copy(old[:, :GROUP], before[:].indirect(entries(slot_sb, 0, GROUP)))
-        nc.vector.tensor_copy(old[:, GROUP:VECTOR_OLD], before[:].indirect(entries(slot_sb, GROUP, VECTOR_OLD)))
-        nc.scalar.activation(old[:, VECTOR_OLD:], before[:].indirect(entries(slot_sb, VECTOR_OLD, last)), COPY)
+        nc.vector.tensor_copy(old[:, :VECTOR_OLD], doubled[:].indirect(entries(slot_sb, 0, VECTOR_OLD)))
+        nc.scalar.activation(old[:, VECTOR_OLD:EARLY], doubled[:].indirect(entries(slot_sb, VECTOR_OLD, EARLY)), COPY)
+        nc.scalar.activation(old[:, EARLY:SCALAR_PUT], doubled[:].indirect(entries(slot_sb, EARLY, SCALAR_PUT)), COPY)
+        second_codes = sb.tile([P, GROUP], U32, name="second_codes", align_bytes=64)
+        second_scales = sb.tile([P, GROUP], U8, name="second_scales", align_bytes=64)
+        second_bank = ps.tile([N, GROUP], F32, name="second_bank")
+        quantise(second_in, second_codes[:], second_scales[:])
         project(early_banks[0][:], early_codes[:, :GROUP], early_scales[:, :GROUP])
         project(early_banks[1][:], early_codes[:, GROUP:], early_scales[:, GROUP:])
-        add(early_banks[0][:], 0, GROUP)
-        add(early_banks[1][:], GROUP, EARLY)
-        nc.scalar.activation(store[:].indirect(entries(slot_sb, 0, EARLY)), new[:, :EARLY], COPY)
+        project(second_bank[:], second_codes[:], second_scales[:])
+        add(early_banks[0], 0, 0, GROUP)
+        add(early_banks[1], GROUP, GROUP, EARLY)
+        nc.scalar.activation(doubled[:].indirect(entries(slot_sb, 0, EARLY)), put[:, :EARLY], COPY)
 
         last_in = turns.tile([P, BLOCK, PACK], BF16, name="last_in", offset=0, align_bytes=64)
-        late_codes = sb.tile([P, S - EARLY], U32, name="late_codes", align_bytes=64)
-        late_scales = sb.tile([P, S - EARLY], U8, name="late_scales", tag="held_b", align_bytes=64)
+        late_codes = sb.tile([P, S - third], U32, name="late_codes", align_bytes=64)
+        late_scales = sb.tile([P, S - third], U8, name="late_scales", tag="held_b", align_bytes=64)
+        third_bank = ps.tile([N, GROUP], F32, name="third_bank")
+        last_bank = ps.tile([N, BLOCK], F32, name="last_bank")
+        quantise(third_in, late_codes[:, :GROUP], late_scales[:, :GROUP])
+        project(third_bank[:], late_codes[:, :GROUP], late_scales[:, :GROUP])
         nc.vector.tensor_copy(
             last_in[:].rearrange("p (c i) j -> p c j i", i=4), last_picked[:].rearrange("p j (c i) -> p c j i", i=4)
         )
-        late = [(second_in, second, third), (third_in, third, last), (last_in, last, S)]
-        late_banks = [ps.tile([N, b - a], F32, name=f"bank{a}") for woven, a, b in late]
-        for (woven, a, b), bank in zip(late, late_banks):
-            quantise(woven, late_codes[:, a - EARLY : b - EARLY], late_scales[:, a - EARLY : b - EARLY])
-            project(bank[:], late_codes[:, a - EARLY : b - EARLY], late_scales[:, a - EARLY : b - EARLY])
-        nc.vector.tensor_copy(last_old[:], before[:].indirect(entries(slot_sb, last, S)))
-        for (woven, a, b), bank in zip(late, late_banks):
-            add(bank[:], a, b)
-        nc.vector.tensor_copy(store[:].indirect(entries(slot_sb, EARLY, S)), new[:, EARLY:])
-        nc.sync.dma_start(out, store[:])
+        add(second_bank, second, second, third)
+        quantise(last_in, late_codes[:, GROUP:], late_scales[:, GROUP:])
+        project(last_bank[:], late_codes[:, GROUP:], late_scales[:, GROUP:])
+        add(third_bank, third, third, SCALAR_PUT)
+        nc.scalar.activation(doubled[:].indirect(entries(slot_sb, EARLY, SCALAR_PUT)), put[:, EARLY:SCALAR_PUT], COPY)
+        nc.vector.tensor_copy(old[:, SCALAR_PUT:], taken[:].indirect(entries(slot_sb, SCALAR_PUT, S)))
+        add(third_bank, third, SCALAR_PUT, last)
+        add(last_bank, last, last, S)
+        nc.vector.tensor_copy(taken[:].indirect(entries(slot_sb, SCALAR_PUT, S)), put[:, SCALAR_PUT:])
+        a = 0
+        for n in CHUNKS:
+            nc.vector.scalar_tensor_tensor(merged[:, a : a + n], doubled[:, a : a + n], 2.0, taken[:, a : a + n], MULT, SUBTRACT)
+            nc.sync.dma_start(out[:, a : a + n], merged[:, a : a + n])
+            a = a + n

@@ -21,11 +21,13 @@ COPY = mybir.ActivationFunctionType.Copy
 P = 128
 PACK = 4
 LANES = 16
-GROUP = 256
 BLOCK = 128
 EARLY = 384
-VECTOR_OLD = 256
-SCALAR_PUT = 704
+MIDDLE = 384
+LATE = S - EARLY - MIDDLE
+VECTOR_OLD = 416
+FIRST_PUT = 256
+SECOND_PUT = 384
 CHUNKS = (256, 512, 512, 512, 256)
 
 
@@ -36,7 +38,8 @@ def tile_picked_idxput_add_e_kernel(tc, xT, mem, w1_words, w1_scales, offs, slot
         turns = ctx.enter_context(tc.tile_pool(name="turns", bufs=1))
         ps = ctx.enter_context(tc.psum_pool(name="ps", bufs=1))
 
-        second, third, last = EARLY, EARLY + GROUP, S - BLOCK
+        middle, late = EARLY, EARLY + MIDDLE
+        second, third = FIRST_PUT, FIRST_PUT + SECOND_PUT
         offs_sb = sb.tile([P, S // LANES], U16, name="offs_sb")
         slot_sb = sb.tile([P, S // LANES], U16, name="slot_sb")
         planes = [sb.tile([P, T], F32, name=f"plane{j}") for j in range(PACK)]
@@ -46,41 +49,37 @@ def tile_picked_idxput_add_e_kernel(tc, xT, mem, w1_words, w1_scales, offs, slot
         w_codes = sb.tile([P, 2 * N], U8, name="w_codes", align_bytes=64)
         w_scales = sb.tile([P, N], U8, name="w_scales", align_bytes=64)
         early_in = sb.tile([P, EARLY, PACK], BF16, name="early_in", align_bytes=64)
-        second_in = sb.tile([P, GROUP, PACK], BF16, name="second_in", align_bytes=64)
-        third_in = sb.tile([P, GROUP, PACK], BF16, name="third_in", align_bytes=64)
-        second_picked = [sb.tile([P, PACK, BLOCK], BF16, name=f"second_picked{h}") for h in range(2)]
-        third_picked = sb.tile([P, PACK, GROUP], BF16, name="third_picked")
-        last_picked = sb.tile([P, PACK, BLOCK], BF16, name="last_picked")
+        middle_in = turns.tile([P, MIDDLE, PACK], BF16, name="middle_in", offset=0, align_bytes=64)
+        middle_picked = [sb.tile([P, PACK, BLOCK], BF16, name=f"middle_picked{h}") for h in range(MIDDLE // BLOCK)]
+        late_picked = sb.tile([P, PACK, LATE], BF16, name="late_picked")
+        early_codes = sb.tile([P, EARLY], U32, name="early_codes", tag="codes_in_turn", align_bytes=64)
+        middle_codes = sb.tile([P, MIDDLE], U32, name="middle_codes", align_bytes=64)
+        scales = sb.tile([P, S], U8, name="scales", align_bytes=64)
         old = sb.tile([P, S], F32, name="old")
-        put = sb.tile([P, S], F32, name="put")
         x_rows = xT.rearrange("(p j) t -> p j t", j=PACK)
 
         def entries(lst, a, b):
             return lst[:, a // LANES : b // LANES]
 
-        def pick(to, j, a, b):
-            nc.scalar.activation(to, planes[j][:].indirect(entries(offs_sb, a, b)), COPY)
+        def scalar_copy(to, src):
+            nc.scalar.activation(to, src, COPY)
 
-        def lay(copy, woven, picked, j):
-            copy(woven[:, :, j : j + 2], picked[:, j : j + 2, :].rearrange("p j n -> p n j"))
+        def quantise(woven, codes, a, b):
+            nc.vector.quantize_mx(out=codes[:].bitcast(FP8X4), scales=scales[:, a:b], in_=woven[:].rearrange("p n j -> p (n j)"))
 
-        def quantise(woven, codes, scales):
-            nc.vector.quantize_mx(out=codes.bitcast(FP8X4), scales=scales, in_=woven[:].rearrange("p n j -> p (n j)"))
-
-        def project(bank, codes, scales):
+        def project(bank, first, codes, group, a, b):
             nc.tensor.matmul_mx(
-                out=bank,
+                out=bank[:, a - first : b - first],
                 lhsT=w_codes[:].bitcast(FP4X4),
                 lhsT_scale=w_scales[:],
-                rhs=codes.bitcast(FP8X4),
-                rhs_scale=scales,
+                rhs=codes[:, a - group : b - group].bitcast(FP8X4),
+                rhs_scale=scales[:, a:b],
                 start=True,
                 stop=True,
             )
 
-        def add(bank, first, a, b):
-            share = 0.5 if b <= SCALAR_PUT else -1.0
-            nc.vector.scalar_tensor_tensor(put[:, a:b], bank[:, a - first : b - first], share, old[:, a:b], MULT, ADD)
+        def add(put, bank, share, a, b):
+            nc.vector.scalar_tensor_tensor(put[:], bank[:], share, old[:, a:b], MULT, ADD)
 
         nc.vector.memset(w_scales[:].bitcast(I32), 0)
         nc.sync.dma_start(planes[0][:], x_rows[:, 0, :])
@@ -96,52 +95,45 @@ def tile_picked_idxput_add_e_kernel(tc, xT, mem, w1_words, w1_scales, offs, slot
 
         for j in range(PACK):
             nc.vector.tensor_copy(early_in[:, :, j], planes[j][:].indirect(entries(offs_sb, 0, EARLY)))
-            nc.vector.tensor_copy(last_picked[:, j, :], planes[j][:].indirect(entries(offs_sb, last, S)))
-            for h in range(2):
-                pick(second_picked[h][:, j, :], j, second + h * BLOCK, second + (h + 1) * BLOCK)
-            pick(third_picked[:, j, :], j, third, last)
+            nc.vector.tensor_copy(middle_picked[-1][:, j, :], planes[j][:].indirect(entries(offs_sb, late - BLOCK, late)))
+            for h, picked in enumerate(middle_picked[:-1]):
+                a = middle + h * BLOCK
+                scalar_copy(picked[:, j, :], planes[j][:].indirect(entries(offs_sb, a, a + BLOCK)))
+            scalar_copy(late_picked[:, j, :], planes[j][:].indirect(entries(offs_sb, late, S)))
             if j % 2:
-                for h in range(2):
-                    lay(nc.gpsimd.tensor_copy, second_in[:, h * BLOCK : (h + 1) * BLOCK, :], second_picked[h], j - 1)
-                lay(nc.scalar.copy if j == PACK - 1 else nc.gpsimd.tensor_copy, third_in, third_picked, j - 1)
+                nc.scalar.copy(
+                    middle_in[:, MIDDLE - BLOCK :, j - 1 : j + 1], middle_picked[-1][:, j - 1 : j + 1, :].rearrange("p j n -> p n j")
+                )
+        for h, picked in enumerate(middle_picked[:-1]):
+            nc.gpsimd.tensor_copy(middle_in[:, h * BLOCK : (h + 1) * BLOCK, :], picked[:].rearrange("p j n -> p n j"))
 
-        early_codes = turns.tile([P, EARLY], U32, name="early_codes", offset=0, align_bytes=64)
-        early_scales = sb.tile([P, EARLY], U8, name="early_scales", tag="held_b", align_bytes=64)
-        early_banks = [ps.tile([N, n], F32, name=f"early_bank{n}") for n in (GROUP, BLOCK)]
-        quantise(early_in, early_codes[:], early_scales[:])
-        nc.vector.tensor_copy(old[:, :VECTOR_OLD], doubled[:].indirect(entries(slot_sb, 0, VECTOR_OLD)))
-        nc.scalar.activation(old[:, VECTOR_OLD:EARLY], doubled[:].indirect(entries(slot_sb, VECTOR_OLD, EARLY)), COPY)
-        nc.scalar.activation(old[:, EARLY:SCALAR_PUT], doubled[:].indirect(entries(slot_sb, EARLY, SCALAR_PUT)), COPY)
-        second_codes = sb.tile([P, GROUP], U32, name="second_codes", align_bytes=64)
-        second_scales = sb.tile([P, GROUP], U8, name="second_scales", align_bytes=64)
-        second_bank = ps.tile([N, GROUP], F32, name="second_bank")
-        quantise(second_in, second_codes[:], second_scales[:])
-        project(early_banks[0][:], early_codes[:, :GROUP], early_scales[:, :GROUP])
-        project(early_banks[1][:], early_codes[:, GROUP:], early_scales[:, GROUP:])
-        project(second_bank[:], second_codes[:], second_scales[:])
-        add(early_banks[0], 0, 0, GROUP)
-        add(early_banks[1], GROUP, GROUP, EARLY)
-        nc.scalar.activation(doubled[:].indirect(entries(slot_sb, 0, EARLY)), put[:, :EARLY], COPY)
+        quantise(early_in, early_codes, 0, EARLY)
+        quantise(middle_in, middle_codes, middle, late)
+        late_in = turns.tile([P, LATE, PACK], BF16, name="late_in", offset=0, align_bytes=64)
+        nc.gpsimd.tensor_copy(late_in[:], late_picked[:].rearrange("p j n -> p n j"))
+        nc.vector.tensor_copy(old[:, :second], doubled[:].indirect(entries(slot_sb, 0, second)))
+        nc.vector.tensor_copy(old[:, second:VECTOR_OLD], doubled[:].indirect(entries(slot_sb, second, VECTOR_OLD)))
+        scalar_copy(old[:, VECTOR_OLD:], doubled[:].indirect(entries(slot_sb, VECTOR_OLD, S)))
 
-        last_in = turns.tile([P, BLOCK, PACK], BF16, name="last_in", offset=0, align_bytes=64)
-        late_codes = sb.tile([P, S - third], U32, name="late_codes", align_bytes=64)
-        late_scales = sb.tile([P, S - third], U8, name="late_scales", tag="held_b", align_bytes=64)
-        third_bank = ps.tile([N, GROUP], F32, name="third_bank")
-        last_bank = ps.tile([N, BLOCK], F32, name="last_bank")
-        quantise(third_in, late_codes[:, :GROUP], late_scales[:, :GROUP])
-        project(third_bank[:], late_codes[:, :GROUP], late_scales[:, :GROUP])
-        nc.vector.tensor_copy(
-            last_in[:].rearrange("p (c i) j -> p c j i", i=4), last_picked[:].rearrange("p j (c i) -> p c j i", i=4)
-        )
-        add(second_bank, second, second, third)
-        quantise(last_in, late_codes[:, GROUP:], late_scales[:, GROUP:])
-        project(last_bank[:], late_codes[:, GROUP:], late_scales[:, GROUP:])
-        add(third_bank, third, third, SCALAR_PUT)
-        nc.scalar.activation(doubled[:].indirect(entries(slot_sb, EARLY, SCALAR_PUT)), put[:, EARLY:SCALAR_PUT], COPY)
-        nc.vector.tensor_copy(old[:, SCALAR_PUT:], taken[:].indirect(entries(slot_sb, SCALAR_PUT, S)))
-        add(third_bank, third, SCALAR_PUT, last)
-        add(last_bank, last, last, S)
-        nc.vector.tensor_copy(taken[:].indirect(entries(slot_sb, SCALAR_PUT, S)), put[:, SCALAR_PUT:])
+        first_bank = ps.tile([N, second], F32, name="first_bank")
+        second_bank = ps.tile([N, third - second], F32, name="second_bank")
+        third_bank = ps.tile([N, S - third], F32, name="third_bank")
+        first_put = sb.tile([P, second], F32, name="first_put")
+        third_put = sb.tile([P, S - third], F32, name="third_put")
+        project(first_bank, 0, early_codes, 0, 0, second)
+        project(second_bank, second, early_codes, 0, second, middle)
+        project(second_bank, second, middle_codes, middle, middle, third)
+        project(third_bank, third, middle_codes, middle, third, late)
+        add(first_put, first_bank, 0.5, 0, second)
+        scalar_copy(doubled[:].indirect(entries(slot_sb, 0, second)), first_put[:])
+        late_codes = sb.tile([P, LATE], U32, name="late_codes", tag="codes_in_turn", align_bytes=64)
+        quantise(late_in, late_codes, late, S)
+        project(third_bank, third, late_codes, late, late, S)
+        second_put = sb.tile([P, third - second], F32, name="second_put")
+        add(second_put, second_bank, 0.5, second, third)
+        add(third_put, third_bank, -1.0, third, S)
+        scalar_copy(taken[:].indirect(entries(slot_sb, third, S)), third_put[:])
+        nc.vector.tensor_copy(doubled[:].indirect(entries(slot_sb, second, third)), second_put[:])
         a = 0
         for n in CHUNKS:
             nc.vector.scalar_tensor_tensor(merged[:, a : a + n], doubled[:, a : a + n], 2.0, taken[:, a : a + n], MULT, SUBTRACT)

@@ -22,11 +22,8 @@ P = 128
 PACK = 4
 LANES = 16
 BLOCK = 128
-EARLY = 384
-MIDDLE = 384
-LATE = S - EARLY - MIDDLE
+GROUP = 256
 VECTOR_OLD = 416
-FIRST_PUT = 256
 SECOND_PUT = 384
 CHUNKS = (256, 512, 512, 512, 256)
 
@@ -35,11 +32,10 @@ def tile_picked_idxput_add_e_kernel(tc, xT, mem, w1_words, w1_scales, offs, slot
     nc = tc.nc
     with ExitStack() as ctx:
         sb = ctx.enter_context(tc.tile_pool(name="sb", bufs=1))
-        turns = ctx.enter_context(tc.tile_pool(name="turns", bufs=1))
         ps = ctx.enter_context(tc.psum_pool(name="ps", bufs=1))
 
-        middle, late = EARLY, EARLY + MIDDLE
-        second, third = FIRST_PUT, FIRST_PUT + SECOND_PUT
+        middle, late = 2 * GROUP, 3 * GROUP
+        second, third = GROUP, GROUP + SECOND_PUT
         offs_sb = sb.tile([P, S // LANES], U16, name="offs_sb")
         slot_sb = sb.tile([P, S // LANES], U16, name="slot_sb")
         planes = [sb.tile([P, T], F32, name=f"plane{j}") for j in range(PACK)]
@@ -48,12 +44,13 @@ def tile_picked_idxput_add_e_kernel(tc, xT, mem, w1_words, w1_scales, offs, slot
         merged = sb.tile([P, U], F32, name="merged")
         w_codes = sb.tile([P, 2 * N], U8, name="w_codes", align_bytes=64)
         w_scales = sb.tile([P, N], U8, name="w_scales", align_bytes=64)
-        early_in = sb.tile([P, EARLY, PACK], BF16, name="early_in", align_bytes=64)
-        middle_in = turns.tile([P, MIDDLE, PACK], BF16, name="middle_in", offset=0, align_bytes=64)
-        middle_picked = [sb.tile([P, PACK, BLOCK], BF16, name=f"middle_picked{h}") for h in range(MIDDLE // BLOCK)]
-        late_picked = sb.tile([P, PACK, LATE], BF16, name="late_picked")
-        early_codes = sb.tile([P, EARLY], U32, name="early_codes", tag="codes_in_turn", align_bytes=64)
-        middle_codes = sb.tile([P, MIDDLE], U32, name="middle_codes", align_bytes=64)
+        early_in = [sb.tile([P, GROUP, PACK], BF16, name=f"early_in{g}", align_bytes=64) for g in range(2)]
+        middle_in = sb.tile([P, GROUP, PACK], BF16, name="middle_in", tag="woven_in_turn", align_bytes=64)
+        middle_picked = [sb.tile([P, PACK, BLOCK], BF16, name=f"middle_picked{h}") for h in range(2)]
+        late_picked = sb.tile([P, PACK, GROUP], BF16, name="late_picked")
+        first_codes = sb.tile([P, GROUP], U32, name="first_codes", tag="codes_in_turn", align_bytes=64)
+        second_codes = sb.tile([P, GROUP], U32, name="second_codes", align_bytes=64)
+        middle_codes = sb.tile([P, GROUP], U32, name="middle_codes", align_bytes=64)
         scales = sb.tile([P, S], U8, name="scales", align_bytes=64)
         old = sb.tile([P, S], F32, name="old")
         x_rows = xT.rearrange("(p j) t -> p j t", j=PACK)
@@ -64,8 +61,10 @@ def tile_picked_idxput_add_e_kernel(tc, xT, mem, w1_words, w1_scales, offs, slot
         def scalar_copy(to, src):
             nc.scalar.activation(to, src, COPY)
 
-        def quantise(woven, codes, a, b):
-            nc.vector.quantize_mx(out=codes[:].bitcast(FP8X4), scales=scales[:, a:b], in_=woven[:].rearrange("p n j -> p (n j)"))
+        def quantise(woven, codes, a):
+            nc.vector.quantize_mx(
+                out=codes[:].bitcast(FP8X4), scales=scales[:, a : a + GROUP], in_=woven[:].rearrange("p n j -> p (n j)")
+            )
 
         def project(bank, first, codes, group, a, b):
             nc.tensor.matmul_mx(
@@ -94,22 +93,20 @@ def tile_picked_idxput_add_e_kernel(tc, xT, mem, w1_words, w1_scales, offs, slot
         nc.sync.dma_start(taken[:], mem)
 
         for j in range(PACK):
-            nc.vector.tensor_copy(early_in[:, :, j], planes[j][:].indirect(entries(offs_sb, 0, EARLY)))
-            nc.vector.tensor_copy(middle_picked[-1][:, j, :], planes[j][:].indirect(entries(offs_sb, late - BLOCK, late)))
-            for h, picked in enumerate(middle_picked[:-1]):
+            for g, woven in enumerate(early_in):
+                nc.vector.tensor_copy(woven[:, :, j], planes[j][:].indirect(entries(offs_sb, g * GROUP, (g + 1) * GROUP)))
+            for h, picked in enumerate(middle_picked):
                 a = middle + h * BLOCK
                 scalar_copy(picked[:, j, :], planes[j][:].indirect(entries(offs_sb, a, a + BLOCK)))
             scalar_copy(late_picked[:, j, :], planes[j][:].indirect(entries(offs_sb, late, S)))
             if j % 2:
-                nc.scalar.copy(
-                    middle_in[:, MIDDLE - BLOCK :, j - 1 : j + 1], middle_picked[-1][:, j - 1 : j + 1, :].rearrange("p j n -> p n j")
-                )
-        for h, picked in enumerate(middle_picked[:-1]):
-            nc.gpsimd.tensor_copy(middle_in[:, h * BLOCK : (h + 1) * BLOCK, :], picked[:].rearrange("p j n -> p n j"))
+                nc.scalar.copy(middle_in[:, BLOCK:, j - 1 : j + 1], middle_picked[1][:, j - 1 : j + 1, :].rearrange("p j n -> p n j"))
+        nc.gpsimd.tensor_copy(middle_in[:, :BLOCK, :], middle_picked[0][:].rearrange("p j n -> p n j"))
 
-        quantise(early_in, early_codes, 0, EARLY)
-        quantise(middle_in, middle_codes, middle, late)
-        late_in = turns.tile([P, LATE, PACK], BF16, name="late_in", offset=0, align_bytes=64)
+        quantise(early_in[0], first_codes, 0)
+        quantise(early_in[1], second_codes, second)
+        quantise(middle_in, middle_codes, middle)
+        late_in = sb.tile([P, GROUP, PACK], BF16, name="late_in", tag="woven_in_turn", align_bytes=64)
         nc.gpsimd.tensor_copy(late_in[:], late_picked[:].rearrange("p j n -> p n j"))
         nc.vector.tensor_copy(old[:, :second], doubled[:].indirect(entries(slot_sb, 0, second)))
         nc.vector.tensor_copy(old[:, second:VECTOR_OLD], doubled[:].indirect(entries(slot_sb, second, VECTOR_OLD)))
@@ -119,17 +116,17 @@ def tile_picked_idxput_add_e_kernel(tc, xT, mem, w1_words, w1_scales, offs, slot
         second_bank = ps.tile([N, third - second], F32, name="second_bank")
         third_bank = ps.tile([N, S - third], F32, name="third_bank")
         first_put = sb.tile([P, second], F32, name="first_put")
+        second_put = sb.tile([P, third - second], F32, name="second_put")
         third_put = sb.tile([P, S - third], F32, name="third_put")
-        project(first_bank, 0, early_codes, 0, 0, second)
-        project(second_bank, second, early_codes, 0, second, middle)
+        project(first_bank, 0, first_codes, 0, 0, second)
+        project(second_bank, second, second_codes, second, second, middle)
         project(second_bank, second, middle_codes, middle, middle, third)
         project(third_bank, third, middle_codes, middle, third, late)
         add(first_put, first_bank, 0.5, 0, second)
         scalar_copy(doubled[:].indirect(entries(slot_sb, 0, second)), first_put[:])
-        late_codes = sb.tile([P, LATE], U32, name="late_codes", tag="codes_in_turn", align_bytes=64)
-        quantise(late_in, late_codes, late, S)
+        late_codes = sb.tile([P, GROUP], U32, name="late_codes", tag="codes_in_turn", align_bytes=64)
+        quantise(late_in, late_codes, late)
         project(third_bank, third, late_codes, late, late, S)
-        second_put = sb.tile([P, third - second], F32, name="second_put")
         add(second_put, second_bank, 0.5, second, third)
         add(third_put, third_bank, -1.0, third, S)
         scalar_copy(taken[:].indirect(entries(slot_sb, third, S)), third_put[:])

@@ -23,8 +23,8 @@ PACK = 4
 LANES = 16
 BLOCK = 128
 GROUP = 256
-VECTOR_OLD = 416
-SECOND_PUT = 384
+VECTOR_OLD = 448
+VECTOR_PUT = 448
 CHUNKS = (256, 512, 512, 512, 256)
 
 
@@ -34,8 +34,9 @@ def tile_picked_idxput_add_e_kernel(tc, xT, mem, w1_words, w1_scales, offs, slot
         sb = ctx.enter_context(tc.tile_pool(name="sb", bufs=1))
         ps = ctx.enter_context(tc.psum_pool(name="ps", bufs=1))
 
-        middle, late = 2 * GROUP, 3 * GROUP
-        second, third = GROUP, GROUP + SECOND_PUT
+        middle, late = 2 * GROUP, S - BLOCK
+        second, third = GROUP, 3 * GROUP
+        cut = second + VECTOR_PUT
         offs_sb = sb.tile([P, S // LANES], U16, name="offs_sb")
         slot_sb = sb.tile([P, S // LANES], U16, name="slot_sb")
         planes = [sb.tile([P, T], F32, name=f"plane{j}") for j in range(PACK)]
@@ -46,13 +47,15 @@ def tile_picked_idxput_add_e_kernel(tc, xT, mem, w1_words, w1_scales, offs, slot
         w_scales = sb.tile([P, N], U8, name="w_scales", align_bytes=64)
         early_in = [sb.tile([P, GROUP, PACK], BF16, name=f"early_in{g}", align_bytes=64) for g in range(2)]
         middle_in = sb.tile([P, GROUP, PACK], BF16, name="middle_in", tag="woven_in_turn", align_bytes=64)
-        middle_picked = [sb.tile([P, PACK, BLOCK], BF16, name=f"middle_picked{h}") for h in range(2)]
-        late_picked = sb.tile([P, PACK, GROUP], BF16, name="late_picked")
+        laid_in = sb.tile([P, BLOCK, PACK], BF16, name="laid_in", align_bytes=64)
+        middle_picked = [sb.tile([P, PACK, BLOCK], BF16, name=f"middle_picked{h}") for h in range(3)]
+        late_picked = sb.tile([P, PACK, BLOCK], BF16, name="late_picked")
         first_codes = sb.tile([P, GROUP], U32, name="first_codes", tag="codes_in_turn", align_bytes=64)
         second_codes = sb.tile([P, GROUP], U32, name="second_codes", align_bytes=64)
         middle_codes = sb.tile([P, GROUP], U32, name="middle_codes", align_bytes=64)
         scales = sb.tile([P, S], U8, name="scales", align_bytes=64)
         old = sb.tile([P, S], F32, name="old")
+        put = sb.tile([P, S], F32, name="put")
         x_rows = xT.rearrange("(p j) t -> p j t", j=PACK)
 
         def entries(lst, a, b):
@@ -63,7 +66,7 @@ def tile_picked_idxput_add_e_kernel(tc, xT, mem, w1_words, w1_scales, offs, slot
 
         def quantise(woven, codes, a):
             nc.vector.quantize_mx(
-                out=codes[:].bitcast(FP8X4), scales=scales[:, a : a + GROUP], in_=woven[:].rearrange("p n j -> p (n j)")
+                out=codes.bitcast(FP8X4), scales=scales[:, a : a + codes.shape[1]], in_=woven[:].rearrange("p n j -> p (n j)")
             )
 
         def project(bank, first, codes, group, a, b):
@@ -77,8 +80,8 @@ def tile_picked_idxput_add_e_kernel(tc, xT, mem, w1_words, w1_scales, offs, slot
                 stop=True,
             )
 
-        def add(put, bank, share, a, b):
-            nc.vector.scalar_tensor_tensor(put[:], bank[:], share, old[:, a:b], MULT, ADD)
+        def add(bank, first, share, a, b):
+            nc.vector.scalar_tensor_tensor(put[:, a:b], bank[:, a - first : b - first], share, old[:, a:b], MULT, ADD)
 
         nc.vector.memset(w_scales[:].bitcast(I32), 0)
         nc.sync.dma_start(planes[0][:], x_rows[:, 0, :])
@@ -98,15 +101,17 @@ def tile_picked_idxput_add_e_kernel(tc, xT, mem, w1_words, w1_scales, offs, slot
             for h, picked in enumerate(middle_picked):
                 a = middle + h * BLOCK
                 scalar_copy(picked[:, j, :], planes[j][:].indirect(entries(offs_sb, a, a + BLOCK)))
-            scalar_copy(late_picked[:, j, :], planes[j][:].indirect(entries(offs_sb, late, S)))
             if j % 2:
-                nc.scalar.copy(middle_in[:, BLOCK:, j - 1 : j + 1], middle_picked[1][:, j - 1 : j + 1, :].rearrange("p j n -> p n j"))
+                lay = nc.scalar.copy if j == PACK - 1 else nc.gpsimd.tensor_copy
+                for woven, picked in zip((middle_in[:, BLOCK:, :], laid_in[:]), middle_picked[1:]):
+                    lay(woven[:, :, j - 1 : j + 1], picked[:, j - 1 : j + 1, :].rearrange("p j n -> p n j"))
+            scalar_copy(late_picked[:, j, :], planes[j][:].indirect(entries(offs_sb, late, S)))
         nc.gpsimd.tensor_copy(middle_in[:, :BLOCK, :], middle_picked[0][:].rearrange("p j n -> p n j"))
 
-        quantise(early_in[0], first_codes, 0)
-        quantise(early_in[1], second_codes, second)
-        quantise(middle_in, middle_codes, middle)
-        late_in = sb.tile([P, GROUP, PACK], BF16, name="late_in", tag="woven_in_turn", align_bytes=64)
+        quantise(early_in[0], first_codes[:], 0)
+        quantise(early_in[1], second_codes[:], second)
+        quantise(middle_in, middle_codes[:], middle)
+        late_in = sb.tile([P, BLOCK, PACK], BF16, name="late_in", tag="woven_in_turn", align_bytes=64)
         nc.gpsimd.tensor_copy(late_in[:], late_picked[:].rearrange("p j n -> p n j"))
         nc.vector.tensor_copy(old[:, :second], doubled[:].indirect(entries(slot_sb, 0, second)))
         nc.vector.tensor_copy(old[:, second:VECTOR_OLD], doubled[:].indirect(entries(slot_sb, second, VECTOR_OLD)))
@@ -115,22 +120,20 @@ def tile_picked_idxput_add_e_kernel(tc, xT, mem, w1_words, w1_scales, offs, slot
         first_bank = ps.tile([N, second], F32, name="first_bank")
         second_bank = ps.tile([N, third - second], F32, name="second_bank")
         third_bank = ps.tile([N, S - third], F32, name="third_bank")
-        first_put = sb.tile([P, second], F32, name="first_put")
-        second_put = sb.tile([P, third - second], F32, name="second_put")
-        third_put = sb.tile([P, S - third], F32, name="third_put")
         project(first_bank, 0, first_codes, 0, 0, second)
         project(second_bank, second, second_codes, second, second, middle)
         project(second_bank, second, middle_codes, middle, middle, third)
-        project(third_bank, third, middle_codes, middle, third, late)
-        add(first_put, first_bank, 0.5, 0, second)
-        scalar_copy(doubled[:].indirect(entries(slot_sb, 0, second)), first_put[:])
+        add(first_bank, 0, 0.5, 0, second)
+        scalar_copy(doubled[:].indirect(entries(slot_sb, 0, second)), put[:, :second])
         late_codes = sb.tile([P, GROUP], U32, name="late_codes", tag="codes_in_turn", align_bytes=64)
-        quantise(late_in, late_codes, late)
-        project(third_bank, third, late_codes, late, late, S)
-        add(second_put, second_bank, 0.5, second, third)
-        add(third_put, third_bank, -1.0, third, S)
-        scalar_copy(taken[:].indirect(entries(slot_sb, third, S)), third_put[:])
-        nc.vector.tensor_copy(doubled[:].indirect(entries(slot_sb, second, third)), second_put[:])
+        quantise(laid_in, late_codes[:, :BLOCK], third)
+        quantise(late_in, late_codes[:, BLOCK:], late)
+        project(third_bank, third, late_codes, third, third, S)
+        add(second_bank, second, -1.0, second, cut)
+        add(second_bank, second, 0.5, cut, third)
+        add(third_bank, third, 0.5, third, S)
+        scalar_copy(doubled[:].indirect(entries(slot_sb, cut, S)), put[:, cut:])
+        nc.vector.tensor_copy(taken[:].indirect(entries(slot_sb, second, cut)), put[:, second:cut])
         a = 0
         for n in CHUNKS:
             nc.vector.scalar_tensor_tensor(merged[:, a : a + n], doubled[:, a : a + n], 2.0, taken[:, a : a + n], MULT, SUBTRACT)

@@ -24,7 +24,7 @@ LANES = 16
 BLOCK = 128
 GROUP = 256
 VECTOR_OLD = 448
-VECTOR_PUT = 448
+VECTOR_PUT = 480
 CHUNKS = (256, 512, 512, 512, 256)
 
 
@@ -36,7 +36,7 @@ def tile_picked_idxput_add_e_kernel(tc, xT, mem, w1_words, w1_scales, offs, slot
 
         middle, late = 2 * GROUP, S - BLOCK
         second, third = GROUP, 3 * GROUP
-        cut = second + VECTOR_PUT
+        cut = S - VECTOR_PUT
         offs_sb = sb.tile([P, S // LANES], U16, name="offs_sb")
         slot_sb = sb.tile([P, S // LANES], U16, name="slot_sb")
         planes = [sb.tile([P, T], F32, name=f"plane{j}") for j in range(PACK)]
@@ -55,7 +55,7 @@ def tile_picked_idxput_add_e_kernel(tc, xT, mem, w1_words, w1_scales, offs, slot
         middle_codes = sb.tile([P, GROUP], U32, name="middle_codes", align_bytes=64)
         scales = sb.tile([P, S], U8, name="scales", align_bytes=64)
         old = sb.tile([P, S], F32, name="old")
-        put = sb.tile([P, S], F32, name="put")
+        put = sb.tile([P, cut], F32, name="put")
         x_rows = xT.rearrange("(p j) t -> p j t", j=PACK)
 
         def entries(lst, a, b):
@@ -117,23 +117,24 @@ def tile_picked_idxput_add_e_kernel(tc, xT, mem, w1_words, w1_scales, offs, slot
         nc.vector.tensor_copy(old[:, second:VECTOR_OLD], doubled[:].indirect(entries(slot_sb, second, VECTOR_OLD)))
         scalar_copy(old[:, VECTOR_OLD:], doubled[:].indirect(entries(slot_sb, VECTOR_OLD, S)))
 
-        first_bank = ps.tile([N, second], F32, name="first_bank")
-        second_bank = ps.tile([N, third - second], F32, name="second_bank")
-        third_bank = ps.tile([N, S - third], F32, name="third_bank")
-        project(first_bank, 0, first_codes, 0, 0, second)
-        project(second_bank, second, second_codes, second, second, middle)
-        project(second_bank, second, middle_codes, middle, middle, third)
-        add(first_bank, 0, 0.5, 0, second)
+        banks = [ps.tile([N, GROUP], F32, name=f"bank{g}") for g in range(4)]
+        minus = sb.tile([P, S - cut], F32, name="minus")
+        project(banks[0], 0, first_codes, 0, 0, second)
+        project(banks[2], middle, middle_codes, middle, middle, third)
+        project(banks[1], second, second_codes, second, second, middle)
+        nc.scalar.activation(minus[:, : third - cut], banks[2][:, cut - middle :], COPY, scale=-1.0)
+        add(banks[0], 0, 0.5, 0, second)
         scalar_copy(doubled[:].indirect(entries(slot_sb, 0, second)), put[:, :second])
         late_codes = sb.tile([P, GROUP], U32, name="late_codes", tag="codes_in_turn", align_bytes=64)
         quantise(laid_in, late_codes[:, :BLOCK], third)
         quantise(late_in, late_codes[:, BLOCK:], late)
-        project(third_bank, third, late_codes, third, third, S)
-        add(second_bank, second, -1.0, second, cut)
-        add(second_bank, second, 0.5, cut, third)
-        add(third_bank, third, 0.5, third, S)
-        scalar_copy(doubled[:].indirect(entries(slot_sb, cut, S)), put[:, cut:])
-        nc.vector.tensor_copy(taken[:].indirect(entries(slot_sb, second, cut)), put[:, second:cut])
+        project(banks[3], third, late_codes, third, third, S)
+        nc.scalar.activation(minus[:, third - cut :], banks[3][:], COPY, scale=-1.0)
+        add(banks[1], second, 0.5, second, middle)
+        add(banks[2], middle, 0.5, middle, cut)
+        scalar_copy(doubled[:].indirect(entries(slot_sb, second, cut)), put[:, second:cut])
+        for a, b in ((cut, third), (third, S)):
+            nc.vector.tensor_tensor(taken[:].indirect(entries(slot_sb, a, b)), old[:, a:b], minus[:, a - cut : b - cut], ADD)
         a = 0
         for n in CHUNKS:
             nc.vector.scalar_tensor_tensor(merged[:, a : a + n], doubled[:, a : a + n], 2.0, taken[:, a : a + n], MULT, SUBTRACT)

@@ -25,7 +25,7 @@ BLOCK = 128
 GROUP = 256
 VECTOR_OLD = 448
 VECTOR_PUT = 480
-CHUNKS = (256, 512, 512, 512, 256)
+CHUNKS = (256,) * 8
 
 
 def tile_picked_idxput_add_e_kernel(tc, xT, mem, w1_words, w1_scales, offs, slot, out):

@@ -14,18 +14,13 @@ U8 = mybir.dt.uint8
 FP8X4 = mybir.dt.float8_e4m3fn_x4
 FP4X4 = mybir.dt.float4_e2m1fn_x4
 ADD = mybir.AluOpType.add
-MULT = mybir.AluOpType.mult
-SUBTRACT = mybir.AluOpType.subtract
 COPY = mybir.ActivationFunctionType.Copy
 
 P = 128
 PACK = 4
 LANES = 16
-BLOCK = 128
-GROUP = 256
-VECTOR_OLD = 448
-VECTOR_PUT = 480
-CHUNKS = (256,) * 8
+B = 128
+CUT = 608
 
 
 def tile_picked_idxput_add_e_kernel(tc, xT, mem, w1_words, w1_scales, offs, slot, out):
@@ -34,28 +29,28 @@ def tile_picked_idxput_add_e_kernel(tc, xT, mem, w1_words, w1_scales, offs, slot
         sb = ctx.enter_context(tc.tile_pool(name="sb", bufs=1))
         ps = ctx.enter_context(tc.psum_pool(name="ps", bufs=1))
 
-        middle, late = 2 * GROUP, S - BLOCK
-        second, third = GROUP, 3 * GROUP
-        cut = S - VECTOR_PUT
         offs_sb = sb.tile([P, S // LANES], U16, name="offs_sb")
         slot_sb = sb.tile([P, S // LANES], U16, name="slot_sb")
         planes = [sb.tile([P, T], F32, name=f"plane{j}") for j in range(PACK)]
-        doubled = sb.tile([P, U], F32, name="doubled")
-        taken = sb.tile([P, U], F32, name="taken")
-        merged = sb.tile([P, U], F32, name="merged")
+        window = sb.tile([P, U], F32, name="window")
+        source = sb.tile([P, U], F32, name="source")
         w_codes = sb.tile([P, 2 * N], U8, name="w_codes", align_bytes=64)
         w_scales = sb.tile([P, N], U8, name="w_scales", align_bytes=64)
-        early_in = [sb.tile([P, GROUP, PACK], BF16, name=f"early_in{g}", align_bytes=64) for g in range(2)]
-        middle_in = sb.tile([P, GROUP, PACK], BF16, name="middle_in", tag="woven_in_turn", align_bytes=64)
-        laid_in = sb.tile([P, BLOCK, PACK], BF16, name="laid_in", align_bytes=64)
-        middle_picked = [sb.tile([P, PACK, BLOCK], BF16, name=f"middle_picked{h}") for h in range(3)]
-        late_picked = sb.tile([P, PACK, BLOCK], BF16, name="late_picked")
-        first_codes = sb.tile([P, GROUP], U32, name="first_codes", tag="codes_in_turn", align_bytes=64)
-        second_codes = sb.tile([P, GROUP], U32, name="second_codes", align_bytes=64)
-        middle_codes = sb.tile([P, GROUP], U32, name="middle_codes", align_bytes=64)
+        scale_rows = sb.tile([P, 4, N // 4], I32, name="scale_rows")
+        woven = sb.tile([P, 4 * B, PACK], BF16, name="woven", align_bytes=64)
+        third = sb.tile([P, PACK, B], BF16, name="third")
+        fourth = sb.tile([P, PACK, B], BF16, name="fourth")
+        fifth = sb.tile([P, PACK, B], BF16, name="fifth")
+        sixth = sb.tile([P, PACK, B], BF16, name="sixth")
+        rest = sb.tile([P, PACK, 2 * B], BF16, name="rest")
+        first_codes = sb.tile([P, 2 * B], U32, name="first_codes", align_bytes=64)
         scales = sb.tile([P, S], U8, name="scales", align_bytes=64)
-        old = sb.tile([P, S], F32, name="old")
-        put = sb.tile([P, cut], F32, name="put")
+        old_first = sb.tile([P, B], F32, name="old_first", tag="turn_a", align_bytes=64)
+        old_second = sb.tile([P, B], F32, name="old_second", tag="turn_b", align_bytes=64)
+        old_third = sb.tile([P, B], F32, name="old_third", tag="turn_c", align_bytes=64)
+        old_middle = sb.tile([P, CUT - 3 * B], F32, name="old_middle", tag="turn_d")
+        put = sb.tile([P, S], F32, name="put")
+        banks = [ps.tile([N, 3 * B], F32, name=f"bank{g}") for g in range(6)]
         x_rows = xT.rearrange("(p j) t -> p j t", j=PACK)
 
         def entries(lst, a, b):
@@ -64,79 +59,95 @@ def tile_picked_idxput_add_e_kernel(tc, xT, mem, w1_words, w1_scales, offs, slot
         def scalar_copy(to, src):
             nc.scalar.activation(to, src, COPY)
 
-        def quantise(woven, codes, a):
-            nc.vector.quantize_mx(
-                out=codes.bitcast(FP8X4), scales=scales[:, a : a + codes.shape[1]], in_=woven[:].rearrange("p n j -> p (n j)")
-            )
+        def quantise(codes, plane, values):
+            nc.vector.quantize_mx(out=codes.bitcast(FP8X4), scales=plane, in_=values.rearrange("p n j -> p (n j)"))
 
-        def project(bank, first, codes, group, a, b):
+        def project(to, codes, plane):
             nc.tensor.matmul_mx(
-                out=bank[:, a - first : b - first],
+                out=to,
                 lhsT=w_codes[:].bitcast(FP4X4),
                 lhsT_scale=w_scales[:],
-                rhs=codes[:, a - group : b - group].bitcast(FP8X4),
-                rhs_scale=scales[:, a:b],
+                rhs=codes.bitcast(FP8X4),
+                rhs_scale=plane,
                 start=True,
                 stop=True,
             )
 
-        def add(bank, first, share, a, b):
-            nc.vector.scalar_tensor_tensor(put[:, a:b], bank[:, a - first : b - first], share, old[:, a:b], MULT, ADD)
+        def weave(copy, to, picked):
+            copy(to, picked[:].rearrange("p j n -> p n j"))
+
+        def pick(copy, to, j, a):
+            copy(to, planes[j][:].indirect(entries(offs_sb, a, a + to.shape[1])))
+
+        def look_up(copy, old, tile, a):
+            copy(old, tile[:].indirect(entries(slot_sb, a, a + old.shape[1])))
+
+        def add(y, old, a):
+            nc.vector.tensor_tensor(put[:, a : a + old.shape[1]], y, old, ADD)
+
+        def scatter(copy, a, b):
+            copy(window[:].indirect(entries(slot_sb, a, b)), put[:, a:b])
 
         nc.vector.memset(w_scales[:].bitcast(I32), 0)
         nc.sync.dma_start(planes[0][:], x_rows[:, 0, :])
         nc.sync.dma_start(offs_sb[:], offs)
+        nc.sync.dma_start(scale_rows[0:4, :, :], w1_scales[0].bitcast(I32).rearrange("(q r) c -> r q c", r=4))
+        nc.sync.dma_start(w_codes[:].bitcast(I32), w1_words[0].bitcast(I32))
         for j in range(1, PACK):
             nc.sync.dma_start(planes[j][:], x_rows[:, j, :])
         nc.sync.dma_start(slot_sb[:], slot)
-        nc.sync.dma_start(doubled[:], mem)
-        nc.sync.dma_start(w_codes[:].bitcast(I32), w1_words[0].bitcast(I32))
+        nc.sync.dma_start(window[:], mem)
+        nc.sync.dma_start(source[:], mem)
         for q in range(4):
-            nc.sync.dma_start(w_scales[32 * q : 32 * q + 4, :].bitcast(I32), w1_scales[0, 4 * q : 4 * q + 4, :].bitcast(I32))
-        nc.sync.dma_start(taken[:], mem)
+            nc.vector.tensor_copy(w_scales[32 * q : 32 * q + 4, :].bitcast(I32), scale_rows[0:4, q, :])
 
         for j in range(PACK):
-            for g, woven in enumerate(early_in):
-                nc.vector.tensor_copy(woven[:, :, j], planes[j][:].indirect(entries(offs_sb, g * GROUP, (g + 1) * GROUP)))
-            for h, picked in enumerate(middle_picked):
-                a = middle + h * BLOCK
-                scalar_copy(picked[:, j, :], planes[j][:].indirect(entries(offs_sb, a, a + BLOCK)))
-            if j % 2:
-                lay = nc.scalar.copy if j == PACK - 1 else nc.gpsimd.tensor_copy
-                for woven, picked in zip((middle_in[:, BLOCK:, :], laid_in[:]), middle_picked[1:]):
-                    lay(woven[:, :, j - 1 : j + 1], picked[:, j - 1 : j + 1, :].rearrange("p j n -> p n j"))
-            scalar_copy(late_picked[:, j, :], planes[j][:].indirect(entries(offs_sb, late, S)))
-        nc.gpsimd.tensor_copy(middle_in[:, :BLOCK, :], middle_picked[0][:].rearrange("p j n -> p n j"))
+            pick(nc.vector.tensor_copy, woven[:, : 2 * B, j], j, 0)
+            pick(nc.vector.tensor_copy, third[:, j, :], j, 2 * B)
+            pick(scalar_copy, fourth[:, j, :], j, 3 * B)
+            pick(scalar_copy, fifth[:, j, :], j, 4 * B)
+            pick(scalar_copy, sixth[:, j, :], j, 5 * B)
+            if j < PACK - 1:
+                pick(scalar_copy, rest[:, j, :B], j, 6 * B)
+                pick(nc.vector.tensor_copy, rest[:, j, B:], j, 7 * B)
+            else:
+                pick(scalar_copy, rest[:, j, :], j, 6 * B)
+        weave(nc.gpsimd.tensor_copy, woven[:, 3 * B :, :], fourth)
+        quantise(first_codes[:], scales[:, : 2 * B], woven[:, : 2 * B, :])
+        weave(nc.vector.tensor_copy, woven[:, 2 * B : 3 * B, :], third)
+        weave(nc.gpsimd.tensor_copy, woven[:, B : 2 * B, :], fifth)
+        project(banks[0][:, :B], first_codes[:, :B], scales[:, :B])
+        project(banks[1][:, :B], first_codes[:, B:], scales[:, B : 2 * B])
+        look_up(nc.vector.tensor_copy, old_first[:], window, 0)
+        look_up(scalar_copy, old_second[:], window, B)
+        look_up(nc.vector.tensor_copy, old_third[:], window, 2 * B)
+        look_up(scalar_copy, old_middle[:], window, 3 * B)
+        add(banks[0][:, :B], old_first[:], 0)
+        add(banks[1][:, :B], old_second[:], B)
+        scatter(scalar_copy, 0, 2 * B)
 
-        quantise(early_in[0], first_codes[:], 0)
-        quantise(early_in[1], second_codes[:], second)
-        quantise(middle_in, middle_codes[:], middle)
-        late_in = sb.tile([P, BLOCK, PACK], BF16, name="late_in", tag="woven_in_turn", align_bytes=64)
-        nc.gpsimd.tensor_copy(late_in[:], late_picked[:].rearrange("p j n -> p n j"))
-        nc.vector.tensor_copy(old[:, :second], doubled[:].indirect(entries(slot_sb, 0, second)))
-        nc.vector.tensor_copy(old[:, second:VECTOR_OLD], doubled[:].indirect(entries(slot_sb, second, VECTOR_OLD)))
-        scalar_copy(old[:, VECTOR_OLD:], doubled[:].indirect(entries(slot_sb, VECTOR_OLD, S)))
+        middle_codes = sb.tile([P, 3 * B], U32, name="middle_codes", tag="turn_a", align_bytes=64)
+        late_woven = sb.tile([P, 2 * B, PACK], BF16, name="late_woven", tag="turn_b", align_bytes=64)
+        quantise(middle_codes[:], scales[:, 2 * B : 5 * B], woven[:, B:, :])
+        weave(nc.vector.tensor_copy, late_woven[:], rest)
+        weave(nc.gpsimd.tensor_copy, woven[:, B : 2 * B, :], sixth)
+        project(banks[2][:, : 2 * B], middle_codes[:, B:], scales[:, 3 * B : 5 * B])
+        project(banks[5][:, :B], middle_codes[:, :B], scales[:, 2 * B : 3 * B])
+        add(banks[2][:, :B], old_third[:], 2 * B)
+        add(banks[2][:, B : 2 * B], old_middle[:, :B], 3 * B)
+        add(banks[5][:, : CUT - 4 * B], old_middle[:, B:], 4 * B)
+        scatter(scalar_copy, 2 * B, CUT)
 
-        banks = [ps.tile([N, GROUP], F32, name=f"bank{g}") for g in range(4)]
-        minus = sb.tile([P, S - cut], F32, name="minus")
-        project(banks[0], 0, first_codes, 0, 0, second)
-        project(banks[2], middle, middle_codes, middle, middle, third)
-        project(banks[1], second, second_codes, second, second, middle)
-        nc.scalar.activation(minus[:, : third - cut], banks[2][:, cut - middle :], COPY, scale=-1.0)
-        add(banks[0], 0, 0.5, 0, second)
-        scalar_copy(doubled[:].indirect(entries(slot_sb, 0, second)), put[:, :second])
-        late_codes = sb.tile([P, GROUP], U32, name="late_codes", tag="codes_in_turn", align_bytes=64)
-        quantise(laid_in, late_codes[:, :BLOCK], third)
-        quantise(late_in, late_codes[:, BLOCK:], late)
-        project(banks[3], third, late_codes, third, third, S)
-        nc.scalar.activation(minus[:, third - cut :], banks[3][:], COPY, scale=-1.0)
-        add(banks[1], second, 0.5, second, middle)
-        add(banks[2], middle, 0.5, middle, cut)
-        scalar_copy(doubled[:].indirect(entries(slot_sb, second, cut)), put[:, second:cut])
-        for a, b in ((cut, third), (third, S)):
-            nc.vector.tensor_tensor(taken[:].indirect(entries(slot_sb, a, b)), old[:, a:b], minus[:, a - cut : b - cut], ADD)
-        a = 0
-        for n in CHUNKS:
-            nc.vector.scalar_tensor_tensor(merged[:, a : a + n], doubled[:, a : a + n], 2.0, taken[:, a : a + n], MULT, SUBTRACT)
-            nc.sync.dma_start(out[:, a : a + n], merged[:, a : a + n])
-            a = a + n
+        late_codes = sb.tile([P, 3 * B], U32, name="late_codes", tag="turn_c", align_bytes=64)
+        old_rest = sb.tile([P, S - CUT], F32, name="old_rest", tag="turn_d")
+        quantise(late_codes[:, B:], scales[:, 6 * B :], late_woven[:])
+        quantise(late_codes[:, :B], scales[:, 5 * B : 6 * B], woven[:, B : 2 * B, :])
+        project(banks[4][:, : 2 * B], late_codes[:, B:], scales[:, 6 * B :])
+        project(banks[3][:, :B], late_codes[:, :B], scales[:, 5 * B : 6 * B])
+        look_up(nc.vector.tensor_copy, old_rest[:, : 6 * B - CUT], source, CUT)
+        look_up(nc.vector.tensor_copy, old_rest[:, 6 * B - CUT :], source, 6 * B)
+        add(banks[5][:, CUT - 4 * B : B], old_rest[:, : 5 * B - CUT], CUT)
+        add(banks[3][:, :B], old_rest[:, 5 * B - CUT : 6 * B - CUT], 5 * B)
+        add(banks[4][:, : 2 * B], old_rest[:, 6 * B - CUT :], 6 * B)
+        scatter(nc.vector.tensor_copy, CUT, S)
+        nc.sync.dma_start(out, window[:])

@@ -20,7 +20,7 @@ P = 128
 PACK = 4
 LANES = 16
 B = 128
-CUT = 608
+CUT = 576
 
 
 def tile_picked_idxput_add_e_kernel(tc, xT, mem, w1_words, w1_scales, offs, slot, out):
@@ -38,7 +38,6 @@ def tile_picked_idxput_add_e_kernel(tc, xT, mem, w1_words, w1_scales, offs, slot
         w_scales = sb.tile([P, N], U8, name="w_scales", align_bytes=64)
         scale_rows = sb.tile([P, 4, N // 4], I32, name="scale_rows")
         woven = sb.tile([P, 4 * B, PACK], BF16, name="woven", align_bytes=64)
-        third = sb.tile([P, PACK, B], BF16, name="third")
         fourth = sb.tile([P, PACK, B], BF16, name="fourth")
         fifth = sb.tile([P, PACK, B], BF16, name="fifth")
         sixth = sb.tile([P, PACK, B], BF16, name="sixth")
@@ -48,7 +47,7 @@ def tile_picked_idxput_add_e_kernel(tc, xT, mem, w1_words, w1_scales, offs, slot
         old_first = sb.tile([P, B], F32, name="old_first", tag="turn_a", align_bytes=64)
         old_second = sb.tile([P, B], F32, name="old_second", tag="turn_b", align_bytes=64)
         old_third = sb.tile([P, B], F32, name="old_third", tag="turn_c", align_bytes=64)
-        old_middle = sb.tile([P, CUT - 3 * B], F32, name="old_middle", tag="turn_d")
+        old_middle = sb.tile([P, CUT - 3 * B], F32, name="old_middle", tag="turn_d", align_bytes=64)
         put = sb.tile([P, S], F32, name="put")
         banks = [ps.tile([N, 3 * B], F32, name=f"bank{g}") for g in range(6)]
         x_rows = xT.rearrange("(p j) t -> p j t", j=PACK)
@@ -92,18 +91,17 @@ def tile_picked_idxput_add_e_kernel(tc, xT, mem, w1_words, w1_scales, offs, slot
         nc.sync.dma_start(planes[0][:], x_rows[:, 0, :])
         nc.sync.dma_start(offs_sb[:], offs)
         nc.sync.dma_start(scale_rows[0:4, :, :], w1_scales[0].bitcast(I32).rearrange("(q r) c -> r q c", r=4))
-        nc.sync.dma_start(w_codes[:].bitcast(I32), w1_words[0].bitcast(I32))
         for j in range(1, PACK):
             nc.sync.dma_start(planes[j][:], x_rows[:, j, :])
         nc.sync.dma_start(slot_sb[:], slot)
         nc.sync.dma_start(window[:], mem)
+        nc.sync.dma_start(w_codes[:].bitcast(I32), w1_words[0].bitcast(I32))
         nc.sync.dma_start(source[:], mem)
         for q in range(4):
             nc.vector.tensor_copy(w_scales[32 * q : 32 * q + 4, :].bitcast(I32), scale_rows[0:4, q, :])
 
         for j in range(PACK):
-            pick(nc.vector.tensor_copy, woven[:, : 2 * B, j], j, 0)
-            pick(nc.vector.tensor_copy, third[:, j, :], j, 2 * B)
+            pick(nc.vector.tensor_copy, woven[:, : 3 * B, j], j, 0)
             pick(scalar_copy, fourth[:, j, :], j, 3 * B)
             pick(scalar_copy, fifth[:, j, :], j, 4 * B)
             pick(scalar_copy, sixth[:, j, :], j, 5 * B)
@@ -114,7 +112,6 @@ def tile_picked_idxput_add_e_kernel(tc, xT, mem, w1_words, w1_scales, offs, slot
                 pick(scalar_copy, rest[:, j, :], j, 6 * B)
         weave(nc.gpsimd.tensor_copy, woven[:, 3 * B :, :], fourth)
         quantise(first_codes[:], scales[:, : 2 * B], woven[:, : 2 * B, :])
-        weave(nc.vector.tensor_copy, woven[:, 2 * B : 3 * B, :], third)
         weave(nc.gpsimd.tensor_copy, woven[:, B : 2 * B, :], fifth)
         project(banks[0][:, :B], first_codes[:, :B], scales[:, :B])
         project(banks[1][:, :B], first_codes[:, B:], scales[:, B : 2 * B])
@@ -128,7 +125,8 @@ def tile_picked_idxput_add_e_kernel(tc, xT, mem, w1_words, w1_scales, offs, slot
 
         middle_codes = sb.tile([P, 3 * B], U32, name="middle_codes", tag="turn_a", align_bytes=64)
         late_woven = sb.tile([P, 2 * B, PACK], BF16, name="late_woven", tag="turn_b", align_bytes=64)
-        quantise(middle_codes[:], scales[:, 2 * B : 5 * B], woven[:, B:, :])
+        quantise(middle_codes[:, B:], scales[:, 3 * B : 5 * B], woven[:, 2 * B :, :])
+        quantise(middle_codes[:, :B], scales[:, 2 * B : 3 * B], woven[:, B : 2 * B, :])
         weave(nc.vector.tensor_copy, late_woven[:], rest)
         weave(nc.gpsimd.tensor_copy, woven[:, B : 2 * B, :], sixth)
         project(banks[2][:, : 2 * B], middle_codes[:, B:], scales[:, 3 * B : 5 * B])
@@ -138,13 +136,13 @@ def tile_picked_idxput_add_e_kernel(tc, xT, mem, w1_words, w1_scales, offs, slot
         add(banks[5][:, : CUT - 4 * B], old_middle[:, B:], 4 * B)
         scatter(scalar_copy, 2 * B, CUT)
 
-        late_codes = sb.tile([P, 3 * B], U32, name="late_codes", tag="turn_c", align_bytes=64)
-        old_rest = sb.tile([P, S - CUT], F32, name="old_rest", tag="turn_d")
+        late_codes = sb.tile([P, 3 * B], U32, name="late_codes", tag="turn_d", align_bytes=64)
+        old_rest = sb.tile([P, S - CUT], F32, name="old_rest", tag="turn_c", align_bytes=64)
+        look_up(nc.vector.tensor_copy, old_rest[:, : 6 * B - CUT], source, CUT)
         quantise(late_codes[:, B:], scales[:, 6 * B :], late_woven[:])
         quantise(late_codes[:, :B], scales[:, 5 * B : 6 * B], woven[:, B : 2 * B, :])
         project(banks[4][:, : 2 * B], late_codes[:, B:], scales[:, 6 * B :])
         project(banks[3][:, :B], late_codes[:, :B], scales[:, 5 * B : 6 * B])
-        look_up(nc.vector.tensor_copy, old_rest[:, : 6 * B - CUT], source, CUT)
         look_up(nc.vector.tensor_copy, old_rest[:, 6 * B - CUT :], source, 6 * B)
         add(banks[5][:, CUT - 4 * B : B], old_rest[:, : 5 * B - CUT], CUT)
         add(banks[3][:, :B], old_rest[:, 5 * B - CUT : 6 * B - CUT], 5 * B)

@@ -49,7 +49,7 @@ def tile_picked_idxput_add_e_kernel(tc, xT, mem, w1_words, w1_scales, offs, slot
         old_third = sb.tile([P, B], F32, name="old_third", tag="turn_c", align_bytes=64)
         old_middle = sb.tile([P, CUT - 3 * B], F32, name="old_middle", tag="turn_d", align_bytes=64)
         put = sb.tile([P, S], F32, name="put")
-        banks = [ps.tile([N, 3 * B], F32, name=f"bank{g}") for g in range(6)]
+        banks = [ps.tile([N, 3 * B], F32, name=f"bank{g}") for g in range(5)]
         x_rows = xT.rearrange("(p j) t -> p j t", j=PACK)
 
         def entries(lst, a, b):
@@ -88,14 +88,14 @@ def tile_picked_idxput_add_e_kernel(tc, xT, mem, w1_words, w1_scales, offs, slot
             copy(window[:].indirect(entries(slot_sb, a, b)), put[:, a:b])
 
         nc.vector.memset(w_scales[:].bitcast(I32), 0)
+        nc.scalar.dma_start(scale_rows[0:4, :, :], w1_scales[0].bitcast(I32).rearrange("(q r) c -> r q c", r=4))
+        nc.scalar.dma_start(w_codes[:].bitcast(I32), w1_words[0].bitcast(I32))
         nc.sync.dma_start(planes[0][:], x_rows[:, 0, :])
         nc.sync.dma_start(offs_sb[:], offs)
-        nc.sync.dma_start(scale_rows[0:4, :, :], w1_scales[0].bitcast(I32).rearrange("(q r) c -> r q c", r=4))
         for j in range(1, PACK):
             nc.sync.dma_start(planes[j][:], x_rows[:, j, :])
         nc.sync.dma_start(slot_sb[:], slot)
         nc.sync.dma_start(window[:], mem)
-        nc.sync.dma_start(w_codes[:].bitcast(I32), w1_words[0].bitcast(I32))
         nc.sync.dma_start(source[:], mem)
         for q in range(4):
             nc.vector.tensor_copy(w_scales[32 * q : 32 * q + 4, :].bitcast(I32), scale_rows[0:4, q, :])
@@ -111,7 +111,8 @@ def tile_picked_idxput_add_e_kernel(tc, xT, mem, w1_words, w1_scales, offs, slot
             else:
                 pick(scalar_copy, rest[:, j, :], j, 6 * B)
         weave(nc.gpsimd.tensor_copy, woven[:, 3 * B :, :], fourth)
-        quantise(first_codes[:], scales[:, : 2 * B], woven[:, : 2 * B, :])
+        quantise(first_codes[:, :B], scales[:, :B], woven[:, :B, :])
+        quantise(first_codes[:, B:], scales[:, B : 2 * B], woven[:, B : 2 * B, :])
         weave(nc.gpsimd.tensor_copy, woven[:, B : 2 * B, :], fifth)
         project(banks[0][:, :B], first_codes[:, :B], scales[:, :B])
         project(banks[1][:, :B], first_codes[:, B:], scales[:, B : 2 * B])
@@ -130,10 +131,10 @@ def tile_picked_idxput_add_e_kernel(tc, xT, mem, w1_words, w1_scales, offs, slot
         weave(nc.vector.tensor_copy, late_woven[:], rest)
         weave(nc.gpsimd.tensor_copy, woven[:, B : 2 * B, :], sixth)
         project(banks[2][:, : 2 * B], middle_codes[:, B:], scales[:, 3 * B : 5 * B])
-        project(banks[5][:, :B], middle_codes[:, :B], scales[:, 2 * B : 3 * B])
+        project(banks[3][:, :B], middle_codes[:, :B], scales[:, 2 * B : 3 * B])
         add(banks[2][:, :B], old_third[:], 2 * B)
         add(banks[2][:, B : 2 * B], old_middle[:, :B], 3 * B)
-        add(banks[5][:, : CUT - 4 * B], old_middle[:, B:], 4 * B)
+        add(banks[3][:, : CUT - 4 * B], old_middle[:, B:], 4 * B)
         scatter(scalar_copy, 2 * B, CUT)
 
         late_codes = sb.tile([P, 3 * B], U32, name="late_codes", tag="turn_d", align_bytes=64)
@@ -142,10 +143,9 @@ def tile_picked_idxput_add_e_kernel(tc, xT, mem, w1_words, w1_scales, offs, slot
         quantise(late_codes[:, B:], scales[:, 6 * B :], late_woven[:])
         quantise(late_codes[:, :B], scales[:, 5 * B : 6 * B], woven[:, B : 2 * B, :])
         project(banks[4][:, : 2 * B], late_codes[:, B:], scales[:, 6 * B :])
-        project(banks[3][:, :B], late_codes[:, :B], scales[:, 5 * B : 6 * B])
+        project(banks[3][:, B : 2 * B], late_codes[:, :B], scales[:, 5 * B : 6 * B])
         look_up(nc.vector.tensor_copy, old_rest[:, 6 * B - CUT :], source, 6 * B)
-        add(banks[5][:, CUT - 4 * B : B], old_rest[:, : 5 * B - CUT], CUT)
-        add(banks[3][:, :B], old_rest[:, 5 * B - CUT : 6 * B - CUT], 5 * B)
+        add(banks[3][:, CUT - 4 * B : 2 * B], old_rest[:, : 6 * B - CUT], CUT)
         add(banks[4][:, : 2 * B], old_rest[:, 6 * B - CUT :], 6 * B)
         scatter(nc.vector.tensor_copy, CUT, S)
         nc.sync.dma_start(out, window[:])

@@ -20,7 +20,7 @@ P = 128
 PACK = 4
 LANES = 16
 B = 128
-CUT = 576
+CUT = 608
 
 
 def tile_picked_idxput_add_e_kernel(tc, xT, mem, w1_words, w1_scales, offs, slot, out):
@@ -88,14 +88,14 @@ def tile_picked_idxput_add_e_kernel(tc, xT, mem, w1_words, w1_scales, offs, slot
             copy(window[:].indirect(entries(slot_sb, a, b)), put[:, a:b])
 
         nc.vector.memset(w_scales[:].bitcast(I32), 0)
-        nc.scalar.dma_start(scale_rows[0:4, :, :], w1_scales[0].bitcast(I32).rearrange("(q r) c -> r q c", r=4))
-        nc.scalar.dma_start(w_codes[:].bitcast(I32), w1_words[0].bitcast(I32))
         nc.sync.dma_start(planes[0][:], x_rows[:, 0, :])
         nc.sync.dma_start(offs_sb[:], offs)
+        nc.sync.dma_start(scale_rows[0:4, :, :], w1_scales[0].bitcast(I32).rearrange("(q r) c -> r q c", r=4))
         for j in range(1, PACK):
             nc.sync.dma_start(planes[j][:], x_rows[:, j, :])
         nc.sync.dma_start(slot_sb[:], slot)
         nc.sync.dma_start(window[:], mem)
+        nc.sync.dma_start(w_codes[:].bitcast(I32), w1_words[0].bitcast(I32))
         nc.sync.dma_start(source[:], mem)
         for q in range(4):
             nc.vector.tensor_copy(w_scales[32 * q : 32 * q + 4, :].bitcast(I32), scale_rows[0:4, q, :])
@@ -138,14 +138,15 @@ def tile_picked_idxput_add_e_kernel(tc, xT, mem, w1_words, w1_scales, offs, slot
         scatter(scalar_copy, 2 * B, CUT)
 
         late_codes = sb.tile([P, 3 * B], U32, name="late_codes", tag="turn_d", align_bytes=64)
-        old_rest = sb.tile([P, S - CUT], F32, name="old_rest", tag="turn_c", align_bytes=64)
-        look_up(nc.vector.tensor_copy, old_rest[:, : 6 * B - CUT], source, CUT)
+        old_rest = sb.tile([P, 6 * B - CUT], F32, name="old_rest", tag="turn_c", align_bytes=64)
+        look_up(nc.vector.tensor_copy, old_rest[:], source, CUT)
         quantise(late_codes[:, B:], scales[:, 6 * B :], late_woven[:])
         quantise(late_codes[:, :B], scales[:, 5 * B : 6 * B], woven[:, B : 2 * B, :])
         project(banks[4][:, : 2 * B], late_codes[:, B:], scales[:, 6 * B :])
         project(banks[3][:, B : 2 * B], late_codes[:, :B], scales[:, 5 * B : 6 * B])
-        look_up(nc.vector.tensor_copy, old_rest[:, 6 * B - CUT :], source, 6 * B)
-        add(banks[3][:, CUT - 4 * B : 2 * B], old_rest[:, : 6 * B - CUT], CUT)
-        add(banks[4][:, : 2 * B], old_rest[:, 6 * B - CUT :], 6 * B)
+        old_last = sb.tile([P, 2 * B], F32, name="old_last", tag="turn_b", align_bytes=64)
+        look_up(nc.vector.tensor_copy, old_last[:], source, 6 * B)
+        add(banks[3][:, CUT - 4 * B : 2 * B], old_rest[:], CUT)
+        add(banks[4][:, : 2 * B], old_last[:], 6 * B)
         scatter(nc.vector.tensor_copy, CUT, S)
         nc.sync.dma_start(out, window[:])

@@ -31,9 +31,9 @@ def tile_picked_idxput_add_e_kernel(tc, xT, mem, w1_words, w1_scales, offs, slot
 
         offs_sb = sb.tile([P, S // LANES], U16, name="offs_sb")
         slot_sb = sb.tile([P, S // LANES], U16, name="slot_sb")
-        planes = [sb.tile([P, T], F32, name=f"plane{j}") for j in range(PACK)]
-        window = sb.tile([P, U], F32, name="window")
-        source = sb.tile([P, U], F32, name="source")
+        planes = [sb.tile([P, T], F32, name=f"plane{j}", align_bytes=256) for j in range(PACK)]
+        window = sb.tile([P, U], F32, name="window", align_bytes=256)
+        source = sb.tile([P, U], F32, name="source", align_bytes=256)
         w_codes = sb.tile([P, 2 * N], U8, name="w_codes", align_bytes=64)
         w_scales = sb.tile([P, N], U8, name="w_scales", align_bytes=64)
         scale_rows = sb.tile([P, 4, N // 4], I32, name="scale_rows")

from contextlib import ExitStack

import concourse.mybir as mybir

K, T, S, N, U = 512, 2048, 1024, 128, 2048
FLOPS = 2 * K * N * S

F32 = mybir.dt.float32
BF16 = mybir.dt.bfloat16
I32 = mybir.dt.int32
U32 = mybir.dt.uint32
U16 = mybir.dt.uint16
U8 = mybir.dt.uint8
FP8X4 = mybir.dt.float8_e4m3fn_x4
FP4X4 = mybir.dt.float4_e2m1fn_x4
ADD = mybir.AluOpType.add
COPY = mybir.ActivationFunctionType.Copy

P = 128
PACK = 4
LANES = 16
B = 128
CUT = 608


def tile_picked_idxput_add_e_kernel(tc, xT, mem, w1_words, w1_scales, offs, slot, out):
    nc = tc.nc
    with ExitStack() as ctx:
        sb = ctx.enter_context(tc.tile_pool(name="sb", bufs=1))
        ps = ctx.enter_context(tc.psum_pool(name="ps", bufs=1))

        offs_sb = sb.tile([P, S // LANES], U16, name="offs_sb")
        slot_sb = sb.tile([P, S // LANES], U16, name="slot_sb")
        planes = [sb.tile([P, T], F32, name=f"plane{j}", align_bytes=256) for j in range(PACK)]
        window = sb.tile([P, U], F32, name="window", align_bytes=256)
        source = sb.tile([P, U], F32, name="source", align_bytes=256)
        w_codes = sb.tile([P, 2 * N], U8, name="w_codes", align_bytes=64)
        w_scales = sb.tile([P, N], U8, name="w_scales", align_bytes=64)
        scale_rows = sb.tile([P, 4, N // 4], I32, name="scale_rows")
        woven = sb.tile([P, 4 * B, PACK], BF16, name="woven", align_bytes=64)
        fourth = sb.tile([P, PACK, B], BF16, name="fourth")
        fifth = sb.tile([P, PACK, B], BF16, name="fifth")
        sixth = sb.tile([P, PACK, B], BF16, name="sixth")
        rest = sb.tile([P, PACK, 2 * B], BF16, name="rest")
        first_codes = sb.tile([P, 2 * B], U32, name="first_codes", align_bytes=64)
        scales = sb.tile([P, S], U8, name="scales", align_bytes=64)
        old_first = sb.tile([P, B], F32, name="old_first", tag="turn_a", align_bytes=64)
        old_second = sb.tile([P, B], F32, name="old_second", tag="turn_b", align_bytes=64)
        old_third = sb.tile([P, B], F32, name="old_third", tag="turn_c", align_bytes=64)
        old_middle = sb.tile([P, CUT - 3 * B], F32, name="old_middle", tag="turn_d", align_bytes=64)
        put = sb.tile([P, S], F32, name="put")
        banks = [ps.tile([N, 3 * B], F32, name=f"bank{g}") for g in range(5)]
        x_rows = xT.rearrange("(p j) t -> p j t", j=PACK)

        def entries(lst, a, b):
            return lst[:, a // LANES : b // LANES]

        def scalar_copy(to, src):
            nc.scalar.activation(to, src, COPY)

        def quantise(codes, plane, values):
            nc.vector.quantize_mx(out=codes.bitcast(FP8X4), scales=plane, in_=values.rearrange("p n j -> p (n j)"))

        def project(to, codes, plane):
            nc.tensor.matmul_mx(
                out=to,
                lhsT=w_codes[:].bitcast(FP4X4),
                lhsT_scale=w_scales[:],
                rhs=codes.bitcast(FP8X4),
                rhs_scale=plane,
                start=True,
                stop=True,
            )

        def weave(copy, to, picked):
            copy(to, picked[:].rearrange("p j n -> p n j"))

        def pick(copy, to, j, a):
            copy(to, planes[j][:].indirect(entries(offs_sb, a, a + to.shape[1])))

        def look_up(copy, old, tile, a):
            copy(old, tile[:].indirect(entries(slot_sb, a, a + old.shape[1])))

        def add(y, old, a):
            nc.vector.tensor_tensor(put[:, a : a + old.shape[1]], y, old, ADD)

        def scatter(copy, a, b):
            copy(window[:].indirect(entries(slot_sb, a, b)), put[:, a:b])

        nc.vector.memset(w_scales[:].bitcast(I32), 0)
        nc.sync.dma_start(planes[0][:], x_rows[:, 0, :])
        nc.sync.dma_start(offs_sb[:], offs)
        nc.sync.dma_start(scale_rows[0:4, :, :], w1_scales[0].bitcast(I32).rearrange("(q r) c -> r q c", r=4))
        for j in range(1, PACK):
            nc.sync.dma_start(planes[j][:], x_rows[:, j, :])
        nc.sync.dma_start(slot_sb[:], slot)
        nc.sync.dma_start(window[:], mem)
        nc.sync.dma_start(w_codes[:].bitcast(I32), w1_words[0].bitcast(I32))
        nc.sync.dma_start(source[:], mem)
        for q in range(4):
            nc.vector.tensor_copy(w_scales[32 * q : 32 * q + 4, :].bitcast(I32), scale_rows[0:4, q, :])

        for j in range(PACK):
            pick(nc.vector.tensor_copy, woven[:, : 3 * B, j], j, 0)
            pick(scalar_copy, fourth[:, j, :], j, 3 * B)
            pick(scalar_copy, fifth[:, j, :], j, 4 * B)
            pick(scalar_copy, sixth[:, j, :], j, 5 * B)
            if j < PACK - 1:
                pick(scalar_copy, rest[:, j, :B], j, 6 * B)
                pick(nc.vector.tensor_copy, rest[:, j, B:], j, 7 * B)
            else:
                pick(scalar_copy, rest[:, j, :], j, 6 * B)
        weave(nc.gpsimd.tensor_copy, woven[:, 3 * B :, :], fourth)
        quantise(first_codes[:, :B], scales[:, :B], woven[:, :B, :])
        quantise(first_codes[:, B:], scales[:, B : 2 * B], woven[:, B : 2 * B, :])
        weave(nc.gpsimd.tensor_copy, woven[:, B : 2 * B, :], fifth)
        project(banks[0][:, :B], first_codes[:, :B], scales[:, :B])
        project(banks[1][:, :B], first_codes[:, B:], scales[:, B : 2 * B])
        look_up(nc.vector.tensor_copy, old_first[:], window, 0)
        look_up(scalar_copy, old_second[:], window, B)
        look_up(nc.vector.tensor_copy, old_third[:], window, 2 * B)
        look_up(scalar_copy, old_middle[:], window, 3 * B)
        add(banks[0][:, :B], old_first[:], 0)
        add(banks[1][:, :B], old_second[:], B)
        scatter(scalar_copy, 0, 2 * B)

        middle_codes = sb.tile([P, 3 * B], U32, name="middle_codes", tag="turn_a", align_bytes=64)
        late_woven = sb.tile([P, 2 * B, PACK], BF16, name="late_woven", tag="turn_b", align_bytes=64)
        quantise(middle_codes[:, B:], scales[:, 3 * B : 5 * B], woven[:, 2 * B :, :])
        quantise(middle_codes[:, :B], scales[:, 2 * B : 3 * B], woven[:, B : 2 * B, :])
        weave(nc.vector.tensor_copy, late_woven[:], rest)
        weave(nc.gpsimd.tensor_copy, woven[:, B : 2 * B, :], sixth)
        project(banks[2][:, : 2 * B], middle_codes[:, B:], scales[:, 3 * B : 5 * B])
        project(banks[3][:, :B], middle_codes[:, :B], scales[:, 2 * B : 3 * B])
        add(banks[2][:, :B], old_third[:], 2 * B)
        add(banks[2][:, B : 2 * B], old_middle[:, :B], 3 * B)
        add(banks[3][:, : CUT - 4 * B], old_middle[:, B:], 4 * B)
        scatter(scalar_copy, 2 * B, CUT)

        late_codes = sb.tile([P, 3 * B], U32, name="late_codes", tag="turn_d", align_bytes=64)
        old_rest = sb.tile([P, 6 * B - CUT], F32, name="old_rest", tag="turn_c", align_bytes=64)
        look_up(nc.vector.tensor_copy, old_rest[:], source, CUT)
        quantise(late_codes[:, B:], scales[:, 6 * B :], late_woven[:])
        quantise(late_codes[:, :B], scales[:, 5 * B : 6 * B], woven[:, B : 2 * B, :])
        project(banks[4][:, : 2 * B], late_codes[:, B:], scales[:, 6 * B :])
        project(banks[3][:, B : 2 * B], late_codes[:, :B], scales[:, 5 * B : 6 * B])
        old_last = sb.tile([P, 2 * B], F32, name="old_last", tag="turn_b", align_bytes=64)
        look_up(nc.vector.tensor_copy, old_last[:], source, 6 * B)
        add(banks[3][:, CUT - 4 * B : 2 * B], old_rest[:], CUT)
        add(banks[4][:, : 2 * B], old_last[:], 6 * B)
        scatter(nc.vector.tensor_copy, CUT, S)
        nc.sync.dma_start(out, window[:])
